import numpy as np, ml_dtypes
CORES = [13,21,141,149]
N = 4
BF = ml_dtypes.bfloat16
def gentries(a):
    return np.ascontiguousarray(a.reshape(8, 16, -1).transpose(0, 2, 1)).reshape(8, -1)
def gtable(e):
    e = np.asarray(e); return np.ascontiguousarray(e.reshape(8, -1, 16).transpose(0, 2, 1)).reshape(128, -1).astype(np.int32)
W, P, R, S, E, LM = 1408, 256, 5, 1, 1, 14
def pack(nb, x, v, z, th):
    return {"nb": np.ascontiguousarray(nb.reshape(N, 128, W)).astype(np.int32), "xd": np.ascontiguousarray(x.reshape(N, 128, W)).astype(np.float32).astype(BF),
            "pv": np.stack([gtable(a) for a in v]), "pz": np.ascontiguousarray(z.reshape(N, 128, P)).astype(np.float32).astype(BF), "th": np.repeat(th, 16, axis=1).astype(np.int32)}
def blur(rng, pat, sel, m):
    b = np.stack([pat[g][sel[:, g]] for g in range(8)], axis=1).transpose(0, 1, 3, 2)
    b = np.clip(b + rng.integers(-1, 2, b.shape) * (rng.random(b.shape) < 0.25), 0, 15)
    return np.where(np.arange(16)[:, None] < m[:, :, None, :], b, rng.integers(0, 16, b.shape))
def alike(rng, s, want):
    o = np.argsort(s, kind="stable"); n = np.bincount(s, minlength=8); b = np.add.accumulate(n) - n
    return o[np.minimum(b[want] + (rng.random(want.shape) * n[want]).astype(np.int64), len(s) - 1)]
def parts(rng):
    pat = rng.integers(0, 16, (8, 8, 16))
    s = np.where(rng.random((N, 8, W)) < 0.7, rng.integers(0, 8, (1, 8, W)), rng.integers(0, 8, (N, 8, W)))
    x = blur(rng, pat, s, rng.integers(0, 17, (N, 8, W)))
    sp = rng.integers(0, 8, (N, 8, P)); z = blur(rng, pat, sp, rng.integers(0, 17, (N, 8, P)))
    nb = rng.integers(0, W, (N, 8, 16, W)); v = rng.integers(0, W, (N, 8, P))
    for q in range(N):
        for g in range(8):
            w = alike(rng, s[q, g], np.broadcast_to(s[q, g], (16, W)))
            nb[q, g] = np.where(rng.random((16, W)) < 0.5, w, nb[q, g])
            v[q, g] = np.where(rng.random(P) < 0.6, alike(rng, s[q, g], sp[q, g]), v[q, g])
    th = np.stack([rng.integers(40, 91, (N, 8)), rng.integers(25, 76, (N, 8))], axis=-1)
    return nb, x, v, z, th
def setup_inputs(rng):
    return pack(*parts(rng))
def uneven(rng, shape, n):
    a = np.minimum((n * rng.random(shape) ** 3).astype(np.int64), n - 1)
    return np.where(rng.random(shape[:-1] + (1,)) < 0.5, a, n - 1 - a)
def setup_inputs_spread(rng):
    def digits(n):
        top = 1 << rng.integers(0, 5, (N, 8, 1, n)); a = np.minimum((rng.random((N, 8, 16, n)) * top).astype(np.int64), 15)
        return np.where(rng.random((N, 8, 1, n)) < 0.5, a, 15 - a)
    return pack(uneven(rng, (N, 8, 16, W), W), digits(W), uneven(rng, (N, 8, P), W), digits(P), rng.integers(0, 242, (N, 8, 2)))
def setup_inputs_ends(rng):
    def digits(n):
        return np.where(rng.random((N, 8, 1, n)) < 0.5, 15 * rng.integers(0, 2, (N, 8, 1, n)), 15 * rng.integers(0, 2, (N, 8, 16, n)))
    x = digits(W); x[..., 0] = 0; x[..., W - 1] = 15; x[:, 1:6:2, :, 0] = 15; x[:, 1:6:2, :, W - 1] = 0
    z = digits(P); z[..., 0] = 0; z[..., 1] = 15; z[..., P - 2] = 15; z[..., P - 1] = 0
    nb = np.where(rng.random((N, 8, 16, W)) < 0.25, rng.integers(0, W, (N, 8, 16, W)), (W - 1) * rng.integers(0, 2, (N, 8, 16, W)))
    nb[:, 7, :, W - 1] = W - 1
    v = np.where(rng.random((N, 8, P)) < 0.25, rng.integers(0, W, (N, 8, P)), (W - 1) * rng.integers(0, 2, (N, 8, P)))
    v[..., 0] = 0; v[..., 1] = W - 1; v[..., P - 2] = W - 1; v[..., P - 1] = W - 1
    pairs = np.array([[0, 0], [0, 241], [241, 0], [241, 241]])
    th = pairs[np.argsort(rng.random((N, 8)), axis=1) & 3]; th[N - 1] = pairs[np.array([0, 3, 2, 1, 0, 2, 3, 1])]; th[:, 2] = np.array([120, 121])
    return pack(nb, x, v, z, th)
def setup_inputs_corners(rng):
    M = P // 4; nb = np.zeros((N, 8, 16, W), np.int64); x = np.zeros((N, 8, 16, W), np.int64); v = np.zeros((N, 8, P), np.int64); z = np.zeros((N, 8, 16, P), np.int64)
    th = np.zeros((N, 8, 2), np.int64); th[..., 0] = 40; th[..., 1] = 24
    rows = np.arange(16)[:, None]
    for q in range(N):
        for g in range(8):
            zz = rng.integers(4, 12, 16)[:, None]; o = rng.permutation(W); place = o[:P]; cont = o[P:P + 16 * M].reshape(M, 16); good = o[P + 16 * M::2]; miss = o[P + 16 * M + 1::2]
            lw = rng.choice(np.array([0, 1, 2, 7, LM - 1, LM, LM + 1, 15, 16]), P); lv = np.minimum(lw, LM)[:M]; case = rng.permutation(np.arange(M) & 7)
            d = np.zeros(W, np.int64); d[good] = rng.choice(np.array([0, 1, 23]), len(good)); d[miss] = rng.choice(np.array([24, 24, 25, 39, 40]), len(miss))
            d[cont] = rng.choice(np.array([40, 40, 41, 54, 55, 56]), (M, 16)); j = np.flatnonzero(case == 0); d[cont[j, lv[j]]] = 39
            sign = 1 - 2 * rng.integers(0, 2, (16, W)); diff = (d >> 4) + (np.argsort(rng.random((16, W)), axis=0) < (d & 15))
            diff[:, place] = np.where(rows < lw, rng.integers(0, 2, (16, P)), np.where(rows == lw, 2, rng.integers(0, 5, (16, P))))
            x[q, g] = zz + sign * diff
            w = rng.random((16, W)); b = np.where(w < 0.15, np.arange(W), np.where(w < 0.25, 0, np.where(w < 0.35, W - 1, rng.integers(0, W, (16, W)))))
            b[:, place[:M]] = cont.T
            for e in range(E + 1): b[(lv + e)[:, None], cont] = rng.choice(miss, (M, 16))
            last = (lv + 15) & 15
            for c, e, k in ((1, 0, last), (2, 0, lv), (3, 1, last), (4, E, lv), (6, 0, last), (7, 0, 0 * lv + 15), (7, 0, 0 * lv)):
                j = np.flatnonzero(case == c); b[lv[j] + e, cont[j, k[j]]] = rng.choice(good, len(j))
            j = np.flatnonzero(case == 6); b[(lv[j] + 1)[:, None], cont[j]] = rng.choice(good, (len(j), 16))
            nb[q, g] = b
            pl = place.copy(); n = P - M; pl[M:] = np.where(rng.random(n) < 0.25, rng.choice(place[:M], n), pl[M:]); pl[P - 1] = W - 1; pl[P - 2] = 0
            t = np.repeat(zz, P, axis=1); t[:, M:] = np.where(rng.random(n) < 0.5, np.clip(zz + rng.integers(-3, 4, (16, n)), 0, 15), rng.integers(0, 16, (16, n)))
            r = rng.permutation(P); v[q, g] = pl[r]; z[q, g] = t[:, r]
    th[1, :, 0] = 0; th[N - 1, :4] = np.array([[0, 0], [0, 241], [241, 0], [241, 241]])
    return pack(nb, x, v, z, th)
def setup_inputs_crowd(rng):
    nb, x, v, z, th = parts(rng)
    v[:, 0] = rng.integers(0, W, (N, 1)); v[:, 1] = rng.integers(0, W - 1, (N, 1))
    for q in range(N): v[q, 1, rng.integers(0, P)] = W - 1
    v[:, 2] = rng.choice(np.array([0, 3, W // 2, W - 1]), (N, P)); v[:, 3] = np.repeat(v[:, 3, :P // 2], 2, axis=1)
    nb[:, 4, :15] = rng.integers(0, W, (N, 1, 1)); nb[:, 5] = nb[:, 5, :1]
    v[:, 6] = rng.integers(0, W, (N, 1)); z[:, 6] = z[:, 6, :, :1]; v[:, 7] = W - 1
    th[0, :, 0] = 0; th[1, :, 0] = 0; th[1, 7, 0] = 1
    x[1, 7, 15] = np.minimum(x[1, 7, 15], 14); z[1, 7, 15] = 15; j = rng.integers(0, P); u = rng.integers(0, W - 1)
    nb[1, 7, :, v[1, 7, j]] = u; z[1, 7, :, j] = x[1, 7, :, u]
    th[2, :7, 0] = 241; th[2, 7, 0] = 0
    return pack(nb, x, v, z, th)
def setup_inputs_calm(rng):
    M = P - P // 8; rows = np.arange(16)[:, None]
    nb = rng.integers(0, W, (N, 8, 16, W)); x = rng.integers(0, 16, (N, 8, 16, W))
    n = np.argsort(rng.random((8, W)), axis=1)[:, :(R + 1) * M].reshape(8, R + 1, M)
    th = np.zeros((N, 8, 2), np.int64); th[..., 0] = rng.integers(16, 33, (N, 8))
    z0 = np.clip(rng.integers(0, 16, (8, 16, M)) + rng.integers(-1, 2, (N, 8, 16, M)), 0, 15); z = z0
    at = np.where(rows < rng.integers(0, 17, (N, 8, 1, M)), np.clip(z + rng.integers(-1, 2, z.shape), 0, 15), rng.integers(0, 16, z.shape))
    o = rng.permutation(N); want = np.zeros((R - 1, N), np.int64)
    for t in range(R - 1): want[t, o] = (np.arange(N) + t) & 3
    want[0, o[0]] = 8 * P; want[0, o[1]] = 8 * P - 1
    weight = 1 + (np.arange(M) < P - M).astype(np.int64); a = np.zeros(N, np.int64)
    for t in range(R):
        if t > 0: z = np.roll(z, S, axis=0)
        near = (np.abs(at - z) <= 1).astype(np.int64)
        l = np.minimum(np.add.reduce(np.multiply.accumulate(near, axis=2), axis=2), LM)
        for q in range(N):
            for g in range(8):
                x[q, g][:, n[g, t]] = at[q, g]; nb[q, g][l[q, g], n[g, t]] = n[g, t + 1]
                if t < R - 1: nb[q, g][15, n[g, t]] = n[g, t + 1]
        fail = rng.random((N, 8, M)) < 0.4; over = np.where(rng.random((N, 8, M)) < 0.5, 0, rng.integers(0, 8, (N, 8, M)))
        if t < R - 1:
            over = 0 * over
            for q in range(N):
                k = int(want[t, q]); j = rng.permutation(8 * (2 * M - P))[:min(k, 8 * P - k)]
                fail[q] = k > 3; fail[q, j & 7, P - M + (j >> 3)] = k < 4
        h = th[..., 0][:, :, None] + (a & 15)[:, None, None]
        under = np.where(rng.random((N, 8, M)) < 0.5, 0, rng.integers(0, 16, (N, 8, M)))
        need = np.where(fail, h + over, h - 1 - under)[:, :, None, :]
        m = rng.integers(0, 10, (N, 8, 1, M)); base = need // (16 - m)
        place = np.argsort(np.argsort(rng.random(z.shape) + 2 * (rows < m), axis=2), axis=2)
        diff = np.where(rows >= m, base + (place < need - base * (16 - m)), 0)
        come = z + np.where(z < 8, diff, -diff)
        a = np.add.reduce((fail * weight).reshape(N, -1), axis=1)
        z = np.where(fail[:, :, None, :], np.abs(z - at), z); at = come
    v = np.zeros((N, 8, P), np.int64); zp = np.zeros((N, 8, 16, P), np.int64); who = np.concatenate([np.arange(M), np.arange(P - M)])
    for q in range(N):
        for g in range(8):
            x[q, g][:, n[g, R]] = at[q, g]
            r = who[rng.permutation(P)]; v[q, g] = n[g, 0][r]; zp[q, g] = z0[q, g][:, r]
    return pack(nb, x, v, zp, th)
def check_inputs(d):
    bad = []
    for k, hi in (("nb", W - 1), ("xd", 15), ("pv", W - 1), ("pz", 15), ("th", 241)):
        a = np.asarray(d[k]).astype(np.float64)
        if not (np.min(a) >= 0 and np.max(a) <= hi): bad.append("range of " + k)
        if np.any(a != np.floor(a)): bad.append("whole numbers of " + k)
    t = np.asarray(d["th"]).reshape(N, 8, 16, 2)
    if np.any(t != t[:, :, :1]): bad.append("rows of a group alike in th")
    return bad
def dist(x, z, u):
    s = np.zeros(u.shape, np.int64)
    for p in range(16):
        s = s + np.abs(np.take_along_axis(x[:, :, p], u.reshape(N, 8, -1), 2).reshape(u.shape) - z[:, :, p][:, :, None, :])
    return s
def reference(nb, xd, pv, pz, th):
    c = nb.astype(np.int64).reshape(N, 8, 16, W); x = xd.astype(np.float32).astype(np.int64).reshape(N, 8, 16, W)
    v = np.stack([gentries(a) for a in pv]).astype(np.int64); z = pz.astype(np.float32).astype(np.int64).reshape(N, 8, 16, P)
    h = th.astype(np.int64).reshape(N, 8, 16, 2)[:, :, 0]; a = np.zeros(N, np.int64)
    for t in range(R):
        if t > 0: v = np.roll(v, S, axis=0); z = np.roll(z, S, axis=0)
        xv = np.take_along_axis(x, v[:, :, None, :], 3); con = np.take_along_axis(c, v[:, :, None, :], 3)
        near = (np.abs(xv - z) <= 1).astype(np.int64)
        l = np.minimum(np.add.reduce(np.multiply.accumulate(near, axis=2), axis=2), LM)
        tl = np.take_along_axis(con, l[:, :, None, :], 2)
        ok = dist(x, z, tl)[:, :, 0] < h[:, :, 0, None] + (a & 15)[:, None, None]
        new = np.where(ok, tl[:, :, 0], con[:, :, 15]); todo = ~ok; fixed = np.zeros(ok.shape, bool)
        order = (l[:, :, None, :] + np.arange(16)[:, None]) & 15
        for e in range(E + 1):
            cand = np.take_along_axis(c.reshape(N, 8, 16 * W), ((l + e)[:, :, None, :] * W + con).reshape(N, 8, -1), 2).reshape(N, 8, 16, P)
            hit = np.take_along_axis(dist(x, z, cand) < h[:, :, 1, None, None], order, 2); cand = np.take_along_axis(cand, order, 2)
            got = todo & np.any(hit, axis=2)
            new = np.where(got, np.take_along_axis(cand, np.argmax(hit, axis=2)[:, :, None, :], 2)[:, :, 0], new)
            fixed = fixed | got; todo = todo & ~got
        a = np.add.reduce((~ok).astype(np.int64).reshape(N, -1), axis=1)
        for q in range(N):
            for g in range(8):
                i = np.flatnonzero(fixed[q, g]); u, k = np.unique(v[q, g, i], return_index=True); i = i[k]
                c[q, g][l[q, g][i], u] = new[q, g][i]
                if t < R - 1:
                    u, i = np.unique(v[q, g], return_index=True)
                    x[q, g][:, u] = (xv[q, g][:, i] + z[q, g][:, i]) >> 1
        z = np.where(todo[:, :, None, :], np.abs(z - xv), z); v = new
    return {"ynb": c.reshape(N, 128, W).astype(np.float32), "yv": np.stack([gtable(b) for b in v]).astype(np.float32), "yz": z.reshape(N, 128, P).astype(np.float32).astype(BF)}

@@ -1,0 +1,617 @@
+import math
+import numpy as np
+from concourse.mybir import AluOpType as Op, ActivationFunctionType as Fn
+
+W, R = 1408, 5
+PK, SLOT = 264, 392
+ND = (11, 8)
+REP = 4
+GCH = 1024
+LN2 = math.log(2.0)
+
+MATS = (("mI", 128), ("mN", 128), ("mH", 128), ("mS", 128), ("mB", 128), ("mHB", 128), ("mL", 128), ("mNL", 128), ("mV", 128),
+        ("mC", 128), ("c132", 128), ("z1", 144), ("z2", 144), ("zn", 144), ("z16", 144), ("zs", 144), ("z34", 144), ("zp", 144),
+        ("te", 144), ("to", 144), ("x1", 256), ("xh", 256), ("xk", 256), ("xn", 256), ("xb", 256), ("pw", 256), ("cz0", 128),
+        ("cz1", 128), ("tmpa", 128), ("tmpb", 128), ("tmpc", 128), ("tmpd", 128), ("tmpe", 128), ("p4", 256), ("nn", 160), ("gn", 128),
+        ("n2", 256), ("g2", 256), ("junk", 128), ("keep", 64), ("k8", 64))
+MOFF = {}
+_o = 0
+for _n, _c in MATS:
+    MOFF[_n] = (_o, _c)
+    _o += _c
+
+SCRATCH = {
+    "km": ("sbuf", [128, _o], "bfloat16"),
+    "pko": ("sbuf", [128, 10 * SLOT], "float16"), "pki": ("sbuf", [128, 8 * PK], "float16"),
+    "iw": ("sbuf", [128, W], "int32"),
+    "ip": ("sbuf", [128, 2], "int32"), "ci": ("sbuf", [128, 8], "int32"), "cf": ("sbuf", [128, 8], "float32"),
+    "cs": ("sbuf", [128, 16], "float32"),
+    "i8": ("sbuf", [128, 8], "float32"), "dum": ("sbuf", [128, 8], "float32"), "powl": ("sbuf", [128, 8], "float32"),
+    "px": ("sbuf", [128, 256], "int32"), "p1": ("sbuf", [128, 256], "int32"), "p2": ("sbuf", [128, 256], "int32"),
+    "p3": ("sbuf", [128, 256], "float32"), "hc": ("sbuf", [128, 2], "float32"), "ai": ("sbuf", [128, 2], "int32"),
+}
+for _h in (0, 1):
+    for _n, _c, _d in (("nbi", W, "int32"), ("nbf", W + 128, "float32"), ("xt", W + 128, "bfloat16"), ("pvb", 8, "int32"),
+                       ("pzb", 128, "bfloat16"), ("thb", 4, "int32"), ("yvb", 8, "float32"), ("yzb", 128, "bfloat16"),
+                       ("vb0", 128, "float16"), ("v16", 8, "float16"), ("thf", 4, "float32"), ("dmv", 8, "float32"),
+                       ("v32", 8, "float32"), ("vu", 8, "uint16"), ("dv", 128, "bfloat16"), ("adv", 128, "bfloat16"),
+                       ("fs", 128, "bfloat16"), ("oh", 128, "bfloat16"), ("mk", 128 * REP, "bfloat16"), ("c16", 128, "float16"),
+                       ("tr", 128, "float16"), ("tl", 128, "uint16"), ("q", 128, "float16"), ("pa", 256, "float32"),
+                       ("pb", 256, "float32"), ("cl", 264, "uint16"), ("gm", 2048, "float16"), ("xg", 4224, "bfloat16"),
+                       ("ab", 4224, "bfloat16"), ("rr", 384, "bfloat16"), ("hw", 384, "bfloat16"), ("win", 384, "bfloat16"),
+                       ("sel", 384, "float16"), ("sb", 64, "float32"), ("cm", 8, "float32"),
+                       ("cn", 8, "float16"), ("wl", 8, "float32"), ("ox", 16, "uint16"), ("on", 16, "uint16"),
+                       ("nx", 256, "bfloat16"), ("qq", 128, "bfloat16")):
+        SCRATCH["%s%d" % (_n, _h)] = ("sbuf", [128, _c], _d)
+    SCRATCH["ew%d" % _h] = ("sbuf", [128, 8, 8, 16], "bfloat16")
+BANKS = ("H0", "H1", "M0", "M1", "D0", "D1", "E0", "E1")
+for _n in BANKS:
+    SCRATCH[_n] = ("psum", [128, 512], "float32")
+
+SEMAPHORES = (["sv", "sa", "st", "sp", "sent", "outd"] + ["ar%d" % i for i in range(8)]
+              + ["l%s%d" % (x, s) for x in ("nb", "xd", "pv", "pz", "th") for s in (0, 1)])
+
+COST = {"f": 1.04, "g": 1.56, "s": 3.8, "pe": 0.52, "fv": 25.0, "fa": 70.0, "fp": 10.0, "sem": 150.0, "hop": 6500.0}
+TUNE = {"rounds": 600, "shake": 2500.0, "lag": 10000.0, "heat": 1000.0, "seed": 1, "reach": 1e9, "back": 1}
+CASES = ({"g": 1.1, "s": 2.5, "hop": 7500.0}, {"g": 2.0, "s": 5.0, "sem": 60.0, "hop": 4000.0}, {"pe": 0.75, "sem": 200.0}, {"fv": 65.0, "pe": 0.4, "g": 1.2, "s": 5.5})
+ORDER = {}
+
+
+def helper_of(T, topo, r):
+    src, dst = T.cores[r], T.cores[(r + 1) % len(T.cores)]
+    if topo.may_write(src, dst):
+        return None
+    c = [x for x in topo.cores_of(src) if x != src and T.rank_of(x) is None and topo.may_write(x, dst)]
+    near = [x for x in c if topo.die(x) == topo.die(src)]
+    return (near or c)[0]
+
+
+def count(mask):
+    return bin(mask).count("1")
+
+
+def build(g, core, T, topo, rank):
+    n = len(T.cores)
+    hp = helper_of(T, topo, rank)
+    first = hp if hp is not None else T.cores[(rank + 1) % n]
+    smask = topo.mask(core, first)
+    prev = (rank - 1) % n
+    php = helper_of(T, topo, prev)
+    acount = count(topo.mask(php if php is not None else T.cores[prev], core))
+    V, A, PE = g.vector, g.scalar, g.tensor
+    ops, state, cur, tile = [], {}, [0], [0]
+    F, G, S = COST["f"], COST["g"], COST["s"]
+
+    def add(e, fn, rd, wr, cost, ext=None, lat=0.0):
+        i = len(ops)
+        deps = {}
+        for k in rd:
+            s = state.setdefault(k, [None, []])
+            if s[0] is not None:
+                deps[s[0]] = True
+            if k in BANKS:
+                for j in s[1]:
+                    if ops[j]["e"] != e:
+                        deps[j] = True
+        for k in wr:
+            s = state.setdefault(k, [None, []])
+            for j in ([s[0]] if s[0] is not None else []) + s[1]:
+                deps[j] = deps.get(j, False) or ops[j]["e"] != e or e != "t"
+        for k in rd:
+            state[k][1].append(i)
+        for k in wr:
+            state[k] = [i, []]
+        ops.append({"e": e, "fn": fn, "deps": deps, "cost": cost, "ext": ext, "lat": lat, "n": (wr + rd)[0][:4], "u": cur[0]})
+        return i
+
+    def vec(fn, rd, wr, cyc, fix=0.0):
+        return add("v", lambda: [fn()], rd, wr, COST["fv"] + fix + max(cyc, 64) * F)
+
+    def act(fn, rd, wr, cyc):
+        return add("a", lambda: [fn()], rd, wr, COST["fa"] + cyc * F)
+
+    def mm(lst, rd, wr):
+        cost = sum(COST["fp"] + max(64, m[5]) * COST["pe"] for m in lst)
+        return add("t", lambda: [PE.matmul(m[0], m[1], m[2], m[3], m[4]) for m in lst], rd, wr, cost)
+
+    def grp(out, pairs, nn_, start=True, stop=True):
+        return [(out, a, b, start and i == 0, stop and i == len(pairs) - 1, nn_) for i, (a, b) in enumerate(pairs)]
+
+    def pool(fn, rd, wr, cyc):
+        return add("p", lambda: [fn()], rd, wr, 160 + 2 * cyc * F)
+
+    def ts(out, in0, s1, s2, o0, o1=None):
+        if o1 is None:
+            return lambda: V.tensor_scalar(out, in0, s1, None, o0)
+        return lambda: V.tensor_scalar(out, in0, s1, s2, o0, o1)
+
+    def tt(out, a, b, o):
+        return lambda: V.tensor_tensor(out, a, b, o)
+
+    def cp(out, a):
+        return lambda: V.tensor_copy(out, a)
+
+    def dma(q, out, in_, sem, val, rd, wr, lat):
+        eng = g.sync if q == "s" else A
+        return add(q, lambda: [eng.dma_start(out, in_).then_inc(T.sem[sem], 16)], rd + ["q" + q], wr + ["q" + q], 60.0, ext=(sem, val), lat=lat)
+
+    def K(name, a=0, b=None):
+        o, c = MOFF[name]
+        return T.km[:, o + a:o + (c if b is None else b)]
+
+    def wr_(z, r):
+        return K(z, 15 - r, 143 - r)
+
+    def B(name, s):
+        return T["%s%d" % (name, s)]
+
+    def blk(b, j):
+        return b[:, 128 * j:128 * j + 128]
+
+    for s in (0, 1):
+        rows = slice(64 * s, 64 * s + 64)
+        for name, buf, wd, lat in (("pv", "pvb", 8, 2500.0), ("xd", "xt", W, 3200.0), ("pz", "pzb", 128, 3000.0), ("nb", "nbi", W, 4500.0), ("th", "thb", 2, 4000.0)):
+            for h in (0, 1):
+                own = name in ("pv", "pz")
+                i = dma("sa"[h], B(buf, s)[64 * h:64 * h + 64, 0:wd], T[name][rows, wd * h * own:wd * h * own + wd],
+                        "l%s%d" % (name, s), 32, [], ["%s%d%d" % (buf, s, h)], lat + 3000.0 * s)
+                for j in ops[i]["deps"]:
+                    ops[i]["deps"][j] = None
+            add("x", None, ["%s%d0" % (buf, s), "%s%d1" % (buf, s)], ["%s%d" % (buf, s)], 0.0, ext=("l%s%d" % (name, s), 32))
+
+    def iota(out, pat, base, cm, key, cyc, small=True):
+        if small:
+            pool(lambda: g.iota(out, pat, base, cm, allow_small_or_imprecise_dtypes=True), [], [key], cyc)
+        else:
+            pool(lambda: g.iota(out, pat, base, cm), [], [key], cyc)
+
+    iota(T.ip[:], [[16, 2]], 0, 1, "ip", 2, False)
+    iota(K("nn"), [[1, 160]], -16, 0, "nn", 160)
+    iota(K("gn"), [[16, 8], [0, 16]], 0, 0, "gn", 128)
+    iota(T.i8[:], [[16, 8]], W, 1, "i8", 8)
+    iota(K("n2"), [[-64, 2], [0, 2], [1, 64]], 64, 0, "n2", 256)
+    for h in (0, 1):
+        iota(K("g2", 128 * h, 128 * h + 128), [[0, 2], [16, 4], [0, 16]], 64 - 64 * h, 0, "g2%d" % h, 128)
+        iota(T.px[:, 128 * h:128 * h + 128], [[16, 8], [1, 8], [256, 2]], 8 * h + 128 + 32768, -257, "px%d" % h, 128, False)
+    iota(K("k8"), [[0, 8], [1, 8]], 0, 0, "k8", 64)
+    vec(ts(K("keep"), K("k8"), 1.0, None, Op.min), ["k8"], ["keep"], 32)
+    iota(T.iw[:], [[1, W]], 0, 0, "iw", W, False)
+    for j, m in enumerate((127, 112, 113, 15)):
+        vec(ts(T.ci[:, j:j + 1], T.ip[:, 0:1], m, None, Op.bitwise_and), ["ip"], ["ci%d" % j], 1)
+    vec(ts(T.ci[:, 4:6], T.ip[:], 4, 1, Op.logical_shift_right, Op.bitwise_and), ["ip"], ["ci4"], 1)
+    vec(cp(T.cf[:, 0:6], T.ci[:, 0:6]), ["ci%d" % j for j in range(5)], ["cf"], 1)
+    pf, g16, gpar, kf, odd, even = [T.cf[:, j:j + 1] for j in range(6)]
+    sbias, obias, k16, nk16, kl15 = [T.cs[:, j:j + 1] for j in range(5)]
+    vec(ts(sbias, kf, 14.0, -0.6, Op.is_ge, Op.add), ["cf"], ["sbias"], 1)
+    vec(ts(obias, kf, -1.0, 0.5, Op.mult, Op.add), ["cf"], ["obias"], 1)
+    vec(ts(k16, kf, 15.0, 16.0, Op.is_equal, Op.mult), ["cf"], ["k16"], 1)
+    vec(ts(nk16, kf, 15.0, -16.0, Op.is_equal, Op.mult), ["cf"], ["nk16"], 1)
+    vec(ts(kl15, kf, 15.0, None, Op.is_lt), ["cf"], ["kl15"], 1)
+    for s in (0, 1):
+        vec(cp(B("thf", s)[:, 0:2], B("thb", s)[:, 0:2]), ["thb%d" % s], ["thf%d" % s], 1)
+        vec(ts(B("thf", s)[:, 2:3], k16, 64.0, B("thf", s)[:, 0:1], Op.mult, Op.add), ["k16", "thf%d" % s], ["hm%d" % s], 1)
+    n0 = K("nn", 16, 144)
+    for name, wgt in (("mI", 1.0), ("mN", -1.0), ("mH", 0.5)):
+        vec(ts(K(name), n0, pf, wgt, Op.is_equal, Op.mult), ["nn", "cf"], [name], 64)
+    vec(ts(K("tmpa"), K("nn", 15, 143), pf, None, Op.is_equal), ["nn", "cf"], ["tmpa"], 64)
+    vec(tt(K("mS"), K("tmpa"), K("mI"), Op.add), ["tmpa", "mI"], ["mS"], 256)
+    for name, wgt, dep in (("mB", 1.0, "cf"), ("mHB", 0.5, "cf"), ("mL", k16, "k16"), ("mNL", nk16, "nk16")):
+        vec(ts(K(name), K("gn"), g16, wgt, Op.is_equal, Op.mult), ["gn", "cf", dep], [name], 64)
+    vec(ts(K("tmpb"), n0, pf, -1.0, Op.is_gt, Op.mult), ["nn", "cf"], ["tmpb"], 64)
+    vec(tt(K("tmpc"), K("tmpb"), K("mB"), Op.mult), ["tmpb", "mB"], ["tmpc"], 256)
+    vec(tt(K("mV"), K("tmpc"), K("mH"), Op.add), ["tmpc", "mH"], ["mV"], 256)
+    vec(ts(K("te"), K("nn", 0, 144), pf, even, Op.is_equal, Op.mult), ["nn", "cf"], ["te"], 72)
+    vec(ts(K("to"), K("nn", 16, 160), pf, odd, Op.is_equal, Op.mult), ["nn", "cf"], ["to"], 72)
+    vec(ts(K("zp", 0, 142), K("nn", 2, 144), gpar, None, Op.is_equal), ["nn", "cf"], ["zp"], 72)
+    for name, wgt in (("z1", 1.0), ("z2", 2.0), ("zn", -1.0), ("z16", 1.0 / 16), ("zs", 0.4), ("z34", 2.0 ** -34)):
+        vec(ts(K(name, 0, 143), K("nn", 1, 144), g16, wgt, Op.is_equal, Op.mult), ["nn", "cf"], [name], 72)
+    for name, wgt in (("x1", 1.0), ("xh", 0.5), ("xk", 2048.0), ("xn", -2048.0)):
+        vec(ts(K(name), K("n2"), pf, wgt, Op.is_equal, Op.mult), ["n2", "cf"], [name], 128)
+    vec(ts(K("xb"), K("g2"), g16, None, Op.is_equal), ["g20", "g21", "cf"], ["xb"], 128)
+    czn = {}
+    for kh, nd in enumerate(ND):
+        if nd not in czn and nd > 0:
+            czn[nd] = "cz%d" % kh
+            tmp = "tmp" + "de"[kh]
+            vec(ts(K(tmp), K("nn", 16 - nd, 144 - nd), g16, -1.0, Op.is_lt, Op.mult), ["nn", "cf"], [tmp], 64)
+            vec(tt(K(czn[nd]), K(tmp), K("mB"), Op.mult), [tmp, "mB"], [czn[nd]], 256)
+    vec(ts(K("mC"), n0, 0.0, kl15, Op.mult, Op.add), ["nn", "kl15"], ["mC"], 64)
+    vec(lambda: V.memset(K("c132"), -132.0), [], ["c132"], 64)
+    vec(ts(T.dum[:], T.i8[:], g16, None, Op.subtract), ["i8", "cf"], ["dum"], 8)
+    act(lambda: A.activation(T.powl[:], T.dum[:], Fn.Exp, bias=LN2 * (63 + W), scale=-LN2), ["dum"], ["powl"], 1400)
+    vec(ts(T.p1[:], T.px[:], 15, None, Op.bitwise_and), ["px0", "px1"], ["p1"], 256)
+    vec(ts(T.p2[:], T.px[:], 4, 16, Op.logical_shift_right, Op.bitwise_and), ["px0", "px1"], ["p2"], 256)
+    vec(tt(T.p3[:], T.p1[:], T.p2[:], Op.add), ["p1", "p2"], ["p3"], 512)
+    act(lambda: A.activation(K("p4"), T.p3[:], Fn.Exp, bias=-LN2, scale=-LN2), ["p3", "powl"], ["p4"], 256)
+    for kh in (0, 1):
+        vec(tt(K("pw", 128 * kh, 128 * kh + 128), K("p4", 128 * kh, 128 * kh + 128), K("mB"), Op.mult), ["p4", "mB"], ["pw%d" % kh], 256)
+
+    sends = {}
+
+    def both(name):
+        return [K(name, 0, 128), K(name, 128, 256)]
+
+    def src(t, h):
+        if t == 0:
+            return B("v16", h)[:], B("pzb", h)[:], B("vb0", h)[:], "v16%d" % h, "pzb%d" % h, "vb0%d" % h
+        o = PK * (2 * (t - 1) + h)
+        k = "pki%d%d" % (t, h)
+        return T.pki[:, o:o + 8], T.pki[:, o + 8:o + 136], T.pki[:, o + 136:o + 264], k, k, k
+
+    def dedupe(t, h, wt, wk, off, bank):
+        s = str(h)
+        vl, z, vb, lk, zk, vk = src(t, h)
+        P = T[bank]
+        ew = B("ew", h)
+        for c in range(8):
+            vec(ts(ew[:, :, c, :], vb, B("v32", h)[:, c:c + 1], wt[:, c:c + 1], Op.is_equal, Op.mult),
+                [vk, "v32" + s, wk], ["ew%d%d" % (h, c)], 64)
+        mm(grp(P[:, 0:64], [(wr_("zs", r), ew[:, :, :, r]) for r in range(16)], 64), ["zs"] + ["ew%d%d" % (h, c) for c in range(8)], [bank])
+        vec(lambda: V.tensor_tensor_scan(B("sb", h)[:], K("keep", 0, 64), P[:, 0:64], 0.0, Op.mult, Op.add), [bank, "keep"], ["sb" + s], 64)
+        vec(tt(B("cm", h)[:], B("sb", h)[:, 7:64:8], wt[:], Op.is_ge), ["sb" + s, wk], ["cm" + s], 16)
+        vec(tt(B("cn", h)[:], B("cm", h)[:], B("dmv", h)[:], Op.mult), ["cm" + s, "dmv" + s], ["cn" + s], 16)
+        mm(sum([grp(P[:, 136 + 8 * j:144 + 8 * j], [(x, vl), (x, B("cn", h)[:])], 8) for j, x in enumerate(both("x1"))], []),
+           ["x1", lk, "cn" + s], [bank])
+        vec(cp(B(off, h)[:], P[:, 136:152]), [bank], [off + s], 16)
+
+    def level(t, h):
+        s = str(h)
+        vl, z, vb, lk, zk, vk = src(t, h)
+        E, ek = T["E" + s], "E" + s
+        if t > 0:
+            add("x", None, [], [lk], 0.0, ext=("ar%d" % (2 * (t - 1) + h), acount), lat=COST["hop"])
+            ops[-1]["deps"][sends[(t - 1, h)]] = False
+            vec(cp(B("v32", h)[:], vl), [lk], ["v32" + s], 8)
+            vec(cp(B("vu", h)[:], B("v32", h)[:]), ["v32" + s], ["vu" + s], 8)
+        else:
+            vec(cp(B("vu", h)[:], B("pvb", h)[:]), ["pvb" + s], ["vu" + s], 8)
+            vec(cp(B("v32", h)[:], B("pvb", h)[:]), ["pvb" + s], ["v32" + s], 8)
+            vec(cp(vl, B("v32", h)[:]), ["v32" + s], [lk], 8)
+            vec(cp(vb, T.iw[:].indirect(B("vu", h)[:])), ["iw", "vu" + s], [vk], 128 * G, 30)
+        vec(tt(B("dmv", h)[:], T.dum[:], B("v32", h)[:], Op.subtract), ["dum", "v32" + s], ["dmv" + s], 16)
+        vec(tt(B("dv", h)[:], B("xt", h)[:, 0:W].indirect(B("vu", h)[:]), z, Op.subtract), ["xt" + s, "vu" + s, zk], ["dv" + s], 128 * G, 30)
+        act(lambda: A.activation(B("adv", h)[:], B("dv", h)[:], Fn.Abs), ["dv" + s], ["adv" + s], 128)
+        act(lambda: A.activation(B("fs", h)[:], B("adv", h)[:], Fn.Sign, bias=sbias, scale=0.4), ["adv" + s, "sbias"], ["fs" + s], 128)
+        mm(grp(E[:, 0:128], [(K("mV"), B("fs", h)[:])], 128), ["mV", "fs" + s], [ek])
+        act(lambda: A.activation(B("oh", h)[:], E[:, 0:128], Fn.Relu, bias=obias), [ek, "obias"], ["oh" + s], 128)
+        mm(sum([grp(blk(E, j), [(K("mS"), B("oh", h)[:])], 128) for j in range(REP)], []), ["mS", "oh" + s], [ek])
+        act(lambda: A.activation(B("mk", h)[:], E[:, 0:128 * REP], Fn.Copy), [ek], ["mk" + s], 128 * REP)
+
+    def early(t, h):
+        s = str(h)
+        vl, z, vb, lk, zk, vk = src(t, h)
+        D, dk = T["D" + s], "D" + s
+        lst, oh = [], B("oh", h)[:]
+        for j in (0, 1):
+            lst += grp(blk(D, j), [(both("x1")[j], B("c16", h)[:]), (both("xn")[j], oh)], 128)
+        if t < R - 1:
+            for j in (0, 1):
+                lst += grp(blk(D, 2 + j), [(both("xh")[j], B("dv", h)[:]), (both("x1")[j], z)], 128)
+        mm(lst, ["x1", "xn", "xh", "c16" + s, "oh" + s, "dv" + s, zk], [dk])
+        act(lambda: A.activation(B("pa", h)[:], D[:, 0:256], Fn.Copy), [dk], ["pa" + s], 256)
+        if t < R - 1:
+            act(lambda: A.activation(B("nx", h)[:], D[:, 256:512], Fn.Identity, bias=131.75), [dk], ["nx" + s], 256)
+            dedupe(t, h, T.powl, "powl", "ox", "M" + s)
+
+    def absfold(cols, dst, h, z, zk, rk, key):
+        d = "EM"[tile[0] & 1] + str(h)
+        tile[0] += 1
+        lst = []
+        for j, c in enumerate(cols):
+            lst += grp(blk(T[d], j), [(K("mI"), c), (K("mN"), z)], 128)
+        mm(lst, ["mI", "mN", zk] + rk, [d])
+        act(lambda: A.activation(B("ab", h)[:, dst:dst + 128 * len(cols)], T[d][:, 0:128 * len(cols)], Fn.Abs), [d], [key], 128 * len(cols))
+
+    def contacts(t, h):
+        s = str(h)
+        H, M = T["H" + s], T["M" + s]
+        vl, z, vb, lk, zk, vk = src(t, h)
+        xwin = B("xt", h)[:, 0:W]
+        win, wk = (B("nbi", h)[:], "nbi" + s) if t == 0 else (B("nbf", h)[:, 0:W], "nbf" + s)
+        vec(cp(B("c16", h)[:], win.indirect(B("vu", h)[:])), [wk, "vu" + s], ["c16" + s], 128 * G, 30)
+        vec(lambda: V.transpose(B("tr", h)[:], B("c16", h)[:]), ["c16" + s], ["tr" + s], 64)
+        lst = []
+        for c2 in range(4):
+            for hh in (0, 1):
+                mats = (K("te", 16, 144), K("te", 0, 128)) if hh == 0 else (K("to", 16, 144), K("to", 0, 128))
+                lst += grp(M[:, 2 * c2 + hh:128:8], [(mats[gl], B("tr", h)[:, 32 * c2 + 16 * gl:32 * c2 + 16 * gl + 16]) for gl in (0, 1)], 16)
+        mm(lst, ["te", "to", "tr" + s], ["M" + s])
+        vec(cp(B("tl", h)[:], M[:, 0:128]), ["M" + s], ["tl" + s], 128)
+        mm(grp(H[:, 256:384], [(K("mI"), B("c16", h)[:])], 128) + grp(H[:, 384:512], [(K("mI"), z)], 128), ["mI", "c16" + s, zk], ["H" + s])
+        vec(tt(B("q", h)[:], H[:, 256:384], B("oh", h)[:], Op.mult), ["H" + s, "oh" + s], ["q" + s], 128)
+        mm(grp(M[:, 128:136], [(wr_("z1", r), B("q", h)[:, r:128:16]) for r in range(16)], 8), ["z1", "q" + s], ["M" + s])
+        vec(cp(B("cl", h)[:, 256:264], M[:, 128:136]), ["M" + s], ["cll" + s], 8)
+        act(lambda: A.activation(B("xg", h)[:, 4096:4224], xwin.indirect(B("cl", h)[:, 256:264]), Fn.Copy), ["xt" + s, "cll" + s], ["xgl" + s], 128 * G)
+        wdt = 128 * REP
+        for kh in (0, 1):
+            for j in range(1024 // wdt):
+                o = 1024 * kh + wdt * j
+                key = "gm%d%d%d" % (h, kh, j)
+                vec(tt(B("gm", h)[:, o:o + wdt], win.indirect(B("tl", h)[:, o // 16:(o + wdt) // 16]), B("mk", h)[:], Op.mult),
+                    [wk, "tl" + s, "mk" + s], [key], wdt * G, 30)
+                a0 = j * REP
+                mm(grp(blk(H, kh), [(K("zp", 14 - 2 * a, 142 - 2 * a), blk(B("gm", h), 8 * kh + a)) for a in range(a0, a0 + REP)],
+                       128, a0 == 0, a0 + REP == 8), ["zp", key], ["H" + s])
+            vec(cp(blk(B("cl", h), kh), blk(H, kh)), ["H" + s], ["cl%d%d" % (h, kh)], 128)
+            for o in range(2048 * kh, 2048 * kh + 2048, GCH):
+                act(lambda o=o: A.activation(B("xg", h)[:, o:o + GCH], xwin.indirect(B("cl", h)[:, o // 16:(o + GCH) // 16]), Fn.Copy),
+                    ["xt" + s, "cl%d%d" % (h, kh)], ["xg%d_%d" % (h, o)], GCH * G)
+
+    def health(t, h):
+        s = str(h)
+        vl, z, vb, lk, zk, vk = src(t, h)
+        absfold([B("xg", h)[:, 4096:4224]], 4096, h, z, zk, ["xgl" + s], "abl" + s)
+        mm(grp(T["D" + s][:, 256:384], [(K("mB"), B("ab", h)[:, 4096:4224])], 128), ["mB", "abl" + s], ["D" + s])
+
+    def fold(t, h, kh):
+        s = str(h)
+        vl, z, vb, lk, zk, vk = src(t, h)
+        nd = ND[kh]
+        o = 2048 * kh
+        rk = ["xg%d_%d" % (h, x) for x in range(o, o + 2048, GCH)]
+        out, dk = blk(T["D" + s], kh), "D" + s
+        col = lambda q: B("xg", h)[:, o + q:o + 2048:16]
+        res = lambda q: blk(B("ab", h), 16 * kh + q)
+        parts, dv, seq = [], [], []
+        rest = list(range(nd, 16))
+        while rest:
+            qs, rest = rest[:4], rest[4:]
+            key = "ab%d%d%d" % (h, kh, qs[0])
+            absfold([col(q) for q in qs], o + 128 * qs[0], h, z, zk, rk, key)
+            parts.append(([(wr_("z1", q), res(q)) for q in qs], ["z1", key]))
+        if nd:
+            seq.append(([(K(czn[nd]), z)] + [(wr_("zn", q), col(q)) for q in range(nd)], [czn[nd], "zn", zk] + rk))
+        for q0 in range(0, nd, 3):
+            qs = list(range(q0, min(nd, q0 + 3)))
+            for q in qs:
+                vec(tt(res(q), col(q), T["H" + s][:, 384:512], Op.max), rk + ["H" + s], ["ab%d%d%d" % (h, kh, q)], 128)
+            dv.append(([(wr_("z2", q), res(q)) for q in qs], ["z2"] + ["ab%d%d%d" % (h, kh, q) for q in qs]))
+        while dv or parts:
+            if dv:
+                seq.append(dv.pop(0))
+            if len(dv) > len(parts):
+                seq.append(dv.pop(0))
+            if parts:
+                seq.append(parts.pop(0))
+        for i, (pairs, rd) in enumerate(seq):
+            mm(grp(out, pairs, 128, i == 0, i == len(seq) - 1), rd, [dk])
+
+    def choose(t, h):
+        s = str(h)
+        H, M, D = T["H" + s], T["M" + s], T["D" + s]
+        vl, z, vb, lk, zk, vk = src(t, h)
+        oh, rr, hw, win, sel, thf = B("oh", h)[:], B("rr", h), B("hw", h), B("win", h), B("sel", h), B("thf", h)
+        mm(grp(blk(M, 0), [(both("pw")[0], oh)], 128) + grp(blk(M, 1), [(both("pw")[1], oh)], 128)
+           + grp(blk(M, 2), [(K("mI"), oh), (wr_("z34", 15), oh)], 128), ["pw0", "pw1", "mI", "z34", "oh" + s], ["M" + s])
+        th_, tk = (thf[:, 2:3], "hm" + s) if t == 0 else (thf[:, 3:4], "thr" + s)
+        act(lambda: A.activation(rr[:, 0:256], D[:, 0:256], Fn.Relu, bias=thf[:, 1:2], scale=-1.0), ["D" + s, "thf" + s], ["rra" + s], 256)
+        act(lambda: A.activation(rr[:, 256:384], D[:, 256:384], Fn.Relu, bias=th_, scale=-1.0), ["D" + s, tk], ["rrb" + s], 128)
+        vec(tt(hw[:], M[:, 0:384], rr[:], Op.min), ["M" + s, "rra" + s, "rrb" + s], ["hw" + s], 384)
+        mm(grp(blk(M, 3), [(K("mHB"), blk(hw, j)) for j in range(3)], 128), ["mHB", "hw" + s], ["M" + s])
+        for j in range(3):
+            vec(tt(blk(win, j), blk(M, 3), blk(hw, j), Op.is_le), ["M" + s, "hw" + s], ["win%d%d" % (h, j)], 128)
+        wins = ["win%d%d" % (h, j) for j in range(3)]
+        vec(tt(sel[:], H[:, 0:384], win[:], Op.mult), ["H" + s] + wins, ["sel" + s], 384)
+        mm(grp(blk(D, 0), [(K("mI"), z), (K("mNL"), blk(win, 2))], 128)
+           + grp(blk(D, 1), [(K("mI"), B("adv", h)[:]), (K("mL"), blk(win, 2))], 128), ["mI", "mL", "mNL", zk, "adv" + s, wins[2]], ["D" + s])
+        act(lambda: A.activation(B("qq", h)[:], blk(D, 1), Fn.Relu, bias=-16.0), ["D" + s], ["qq" + s], 128)
+        mm(grp(blk(M, 1), [(K("mB"), blk(win, j)) for j in range(2)], 128)
+           + grp(blk(M, 0), [(K("mB"), blk(sel, j)) for j in range(3)], 128), ["mB", "sel" + s] + wins, ["M" + s])
+        o = SLOT * (2 * t + h)
+        k = "po%d%d" % (t, h)
+        vec(cp(T.pko[:, o + 136:o + 392], M[:, 0:256]), ["M" + s], [k + "b"], 256)
+        zout = T.pko[:, o + 8:o + 136] if t < R - 1 else B("yzb", h)[:]
+        vec(tt(zout, blk(D, 0), B("qq", h)[:], Op.max), ["D" + s, "qq" + s], [k + "z"], 128)
+        mm(grp(H[:, 0:16], [(wr_("z16", r), T.pko[:, o + 136 + r:o + 392:16]) for r in range(16)], 16), ["z16", k + "b"], ["H" + s])
+        lout = T.pko[:, o:o + 8] if t < R - 1 else B("yvb", h)[:]
+        vec(cp(lout, H[:, 0:8]), ["H" + s], [k + "l"], 8)
+        vec(tt(B("wl", h)[:], H[:, 8:16], T.powl[:], Op.mult), ["H" + s, "powl"], ["wl" + s], 8)
+        if t < R - 1:
+            rid, pid = topo.addr(first, core)
+            i = 2 * t + h
+            sends[(t, h)] = add("p", lambda: [g.remote_dma(T.pki[:, PK * i:PK * i + PK], T.pko[:, o:o + PK], T.sem["ar%d" % i], T.sem.sent,
+                                                           pid, rid, smask)], [k + "b", k + "z", k + "l"], [], 300.0, ext=("", 0))
+        E = T["E" + s]
+        mm(sum([grp(blk(E, j), [(both("x1")[j], T.pko[:, o + 136:o + 264]), (both("xk")[j], oh)], 128) for j in (0, 1)], []),
+           ["x1", "xk", k + "b", "oh" + s], ["E" + s])
+        act(lambda: A.activation(B("pb", h)[:], E[:, 0:256], Fn.Identity, bias=-2048.0), ["E" + s], ["pb" + s], 256)
+        dedupe(t, h, B("wl", h), "wl" + s, "on", "M" + s)
+
+    def put_x(h):
+        for j in (0, 1):
+            vec(tt(B("xt", h)[:].indirect(B("ox", h)[:, 8 * j:8 * j + 8]), blk(B("nx", h), j), K("c132"), Op.add),
+                ["ox%d" % h, "nx%d" % h, "c132"], ["xt%d" % h], 128 * S, 30)
+
+    def put_nb(h):
+        for j in (0, 1):
+            vec(tt(B("nbf", h)[:].indirect(B("on", h)[:, 8 * j:8 * j + 8]), blk(B("pa", h), j), blk(B("pb", h), j), Op.max),
+                ["on%d" % h, "pa%d" % h, "pb%d" % h], ["nbf%d" % h], 128 * S, 30)
+
+    def tally():
+        mm(grp(T.D1[:, 256:384], [(K("mC"), B("win", h)[:, 256:384]) for h in (0, 1)], 128), ["mC", "win12", "win02"], ["D1"])
+        act(lambda: A.activation(K("junk"), T.D1[:, 256:384], Fn.Copy, accum_out=T.hc[:, 0:1]), ["D1"], ["hc", "junk"], 150)
+        vec(ts(T.ai[:, 0:1], T.hc[:, 0:1], -1.0, 2048.0, Op.mult, Op.add), ["hc"], ["ai0"], 1)
+        vec(ts(T.ai[:, 1:2], T.ai[:, 0:1], 15, None, Op.bitwise_and), ["ai0"], ["ai1"], 1)
+        for s in (0, 1):
+            vec(ts(B("thf", s)[:, 3:4], T.ai[:, 1:2], B("thf", s)[:, 2:3], None, Op.add), ["ai1", "hm%d" % s], ["thr%d" % s], 1)
+
+    outs = []
+    for t in range(R):
+        last = t == R - 1
+        for h in (0, 1):
+            cur[0] = 2 * t + h
+            level(t, h)
+            contacts(t, h)
+            early(t, h)
+            if t == 0:
+                for a in range(0, W, 352):
+                    vec(cp(B("nbf", h)[:, a:a + 352], B("nbi", h)[:, a:a + 352]), ["nbi%d" % h], ["nbf%d_%d" % (h, a)], 352)
+                add("x", None, ["nbf%d_%d" % (h, a) for a in range(0, W, 352)], ["nbf%d" % h], 0.0)
+            health(t, h)
+            fold(t, h, 0)
+            fold(t, h, 1)
+            if not last:
+                put_x(h)
+            choose(t, h)
+            put_nb(h)
+            if last:
+                rows, k = slice(64 * h, 64 * h + 64), "po%d%d" % (t, h)
+                for j in (0, 1):
+                    part = slice(64 * j, 64 * j + 64)
+                    outs.append(dma("s", T.yz[rows, 128 * j:128 * j + 128], B("yzb", h)[part, :], "outd", 0, [k + "z"], [], 2500.0))
+                    outs.append(dma("s", T.yv[rows, 8 * j:8 * j + 8], B("yvb", h)[part, :], "outd", 0, [k + "l"], [], 2500.0))
+                for j in (0, 1):
+                    part = slice(64 * j, 64 * j + 64)
+                    outs.append(dma("s", T.ynb[rows, 704 * j:704 * j + 704], B("nbf", h)[part, 704 * j:704 * j + 704], "outd", 0, ["nbf%d" % h], [], 3500.0))
+        if not last:
+            tally()
+    for i in outs:
+        for j in ops[i]["deps"]:
+            if ops[j]["e"] == "s":
+                ops[i]["deps"][j] = None
+    return ops, len(outs), count(smask)
+
+
+def place(ops, seq, pred):
+    start, busy = [0.0] * len(ops), {}
+    for i in seq:
+        o = ops[i]
+        t = 0.0
+        for j, gap in pred[i]:
+            if start[j] + gap > t:
+                t = start[j] + gap
+        if o["e"] != "x":
+            a, b = busy.setdefault(o["e"], ([], []))
+            k, hi = 0, len(b)
+            while k < hi:
+                m = (k + hi) // 2
+                if b[m] <= t:
+                    k = m + 1
+                else:
+                    hi = m
+            while k < len(a) and a[k] < t + o["cost"]:
+                t = max(t, b[k])
+                k += 1
+            a.insert(k, t)
+            b.insert(k, t + o["cost"])
+        start[i] = t
+    return start
+
+
+def plan(g, core, T, topo, rank):
+    base, others = dict(COST), []
+    for case in CASES:
+        COST.update(case)
+        others.append((dict(COST), build(g, core, T, topo, rank)[0]))
+        COST.update(base)
+    return schedule(build(g, core, T, topo, rank)[0], others)
+
+
+def schedule(ops, others=()):
+    n = len(ops)
+    fw, bw = [[] for _ in ops], [[] for _ in ops]
+    for i, o in enumerate(ops):
+        for j, hard in o["deps"].items():
+            extra = 0.0 if hard is None else ops[j]["lat"] + (COST["sem"] if hard and ops[j]["e"] != "x" else 0.0)
+            fw[i].append((j, ops[j]["cost"] + extra + 1e-3))
+            bw[j].append((i, o["cost"] + extra + 1e-3))
+    rng = np.random.default_rng(TUNE["seed"])
+
+    def span(st):
+        return max(st[i] + ops[i]["cost"] + ops[i]["lat"] for i in range(n))
+
+    def pack(key, pred):
+        k = list(key)
+        for i in (range(n) if pred is fw else range(n - 1, -1, -1)):
+            for j, gap in pred[i]:
+                k[i] = max(k[i], k[j] + 1e-3)
+        return place(ops, sorted(range(n), key=lambda i: k[i]), pred)
+
+    head = [0.0] * n
+    for i in range(n - 1, -1, -1):
+        head[i] = max([head[j] + gap for j, gap in bw[i]] + [ops[i]["lat"]])
+    best = now = pack([TUNE["lag"] * (ops[i]["u"] % 2) - head[i] - ops[i]["cost"] for i in range(n)], fw)
+    cases = []
+    for cost, alt in others:
+        cases.append(([[(j, alt[j]["cost"] + (0.0 if hard is None else alt[j]["lat"] + (cost["sem"] if hard and alt[j]["e"] != "x" else 0.0)))
+                        for j, hard in o["deps"].items()] for o in alt], [o["cost"] for o in alt], [o["lat"] for o in alt]))
+    eng = [o["e"] for o in ops]
+
+    def judge(st):
+        order, tot = sorted(range(n), key=lambda i: (st[i], i)), span(st)
+        for pred, cost, lat in cases:
+            at, free, end = [0.0] * n, {}, 0.0
+            for i in order:
+                t = free.get(eng[i], 0.0)
+                for j, gap in pred[i]:
+                    if at[j] + gap > t:
+                        t = at[j] + gap
+                at[i] = t
+                if eng[i] != "x":
+                    free[eng[i]] = t + cost[i]
+                end = max(end, t + cost[i] + lat[i])
+            tot += end
+        return tot / (1 + len(cases))
+
+    sbest = snow = judge(best)
+    for r in range(TUNE["rounds"]):
+        amp = TUNE["shake"] * float(rng.random())
+        lo = float(rng.random()) * now[-1]
+        st = pack([x + amp * float(y) * (lo < x < lo + TUNE["reach"]) for x, y in zip(now, rng.random(n))], fw)
+        if r % TUNE["back"] == 0:
+            back = pack([-(st[i] + ops[i]["cost"] + ops[i]["lat"]) for i in range(n)], bw)
+            st = pack([-(back[i] + ops[i]["cost"]) for i in range(n)], fw)
+        s = judge(st)
+        if s < snow + TUNE["heat"] * (1 - r / TUNE["rounds"]) * float(rng.random()):
+            now, snow = st, s
+        if s < sbest:
+            best, sbest = st, s
+    return sorted(range(n), key=lambda i: (best[i], i)), best, [best[i] + ops[i]["cost"] + ops[i]["lat"] for i in range(n)]
+
+
+def rank_program(g, core, T, topo):
+    rank = T.rank_of(core)
+    if rank is None:
+        for r in range(len(T.cores)):
+            if helper_of(T, topo, r) == core:
+                dst = T.cores[(r + 1) % len(T.cores)]
+                rid, pid = topo.addr(dst, core)
+                m, got = topo.mask(core, dst), count(topo.mask(T.cores[r], core))
+                for i in range(2 * (R - 1)):
+                    g.wait_ge(T.sem["ar%d" % i], got)
+                    g.remote_dma(T.pki[:, PK * i:PK * i + PK], T.pki[:, PK * i:PK * i + PK], T.sem["ar%d" % i], T.sem.sent, pid, rid, m)
+                g.wait_ge(T.sem.sent, 2 * (R - 1) * count(m))
+        return
+    ops, nout, nsend = build(g, core, T, topo, rank)
+    if "o" not in ORDER:
+        ORDER["o"] = plan(g, core, T, topo, rank)[0]
+    queue = {"v": g.vector, "a": g.scalar, "t": g.tensor, "p": g, "s": g.sync}
+    sem = {"v": "sv", "a": "sa", "t": "st", "p": "sp"}
+    total, mark, seen = {}, {}, {}
+    for i in ORDER["o"]:
+        o = ops[i]
+        need = {}
+        for j, hard in o["deps"].items():
+            if hard:
+                for s, val in mark[j].items():
+                    need[s] = max(need.get(s, 0), val)
+        if o["e"] == "x":
+            mark[i] = dict([o["ext"]]) if o["ext"] else need
+            continue
+        for s, val in need.items():
+            if seen.get((o["e"], s), 0) < val:
+                queue[o["e"]].wait_ge(T.sem[s], val)
+                seen[(o["e"], s)] = val
+        ins = o["fn"]()
+        if o["ext"] is not None:
+            mark[i] = dict([o["ext"]])
+        else:
+            s = sem[o["e"]]
+            for x in ins:
+                x.then_inc(T.sem[s], 1)
+            total[s] = total.get(s, 0) + len(ins)
+            mark[i] = {s: total[s]}
+    for s, val in total.items():
+        g.wait_ge(T.sem[s], val)
+    g.wait_ge(T.sem.sent, 2 * (R - 1) * nsend)
+    g.sync.wait_ge(T.sem.outd, 16 * nout)

@@ -1,19 +1,18 @@
-import math
 import numpy as np
 from concourse.mybir import AluOpType as Op, ActivationFunctionType as Fn
 
 W, R = 1408, 5
 PK, SLOT = 264, 392
-ND = (11, 8)
-REP = 4
-GCH = 1024
-LN2 = math.log(2.0)
+NQ = 34
+BIG, EPS, KK = 2.0 ** 19, 2.0 ** -17, 2.0 ** 28
+AQ = (7,)
+ENG = {"vu": "v", "v32": "p", "c16": "a", "tl": "a", "cll": "a", "cl": "a", "vb": "a", "lst": "a", "off": "a", "y": "a",
+       "pt": "a", "nv": "a", "nbf": "p", "bc": "v"}
 
-MATS = (("mI", 128), ("mN", 128), ("mH", 128), ("mS", 128), ("mB", 128), ("mHB", 128), ("mL", 128), ("mNL", 128), ("mV", 128),
-        ("mC", 128), ("c132", 128), ("z1", 144), ("z2", 144), ("zn", 144), ("z16", 144), ("zs", 144), ("z34", 144), ("zp", 144),
-        ("te", 144), ("to", 144), ("x1", 256), ("xh", 256), ("xk", 256), ("xn", 256), ("xb", 256), ("pw", 256), ("cz0", 128),
-        ("cz1", 128), ("tmpa", 128), ("tmpb", 128), ("tmpc", 128), ("tmpd", 128), ("tmpe", 128), ("p4", 256), ("nn", 160), ("gn", 128),
-        ("n2", 256), ("g2", 256), ("junk", 128), ("keep", 64), ("k8", 64))
+MATS = (("mI", 128), ("mN", 128), ("n16", 128), ("n2k", 128), ("mV", 128), ("alt", 128), ("alT", 128), ("a2k", 128), ("c132", 128),
+        ("z1", 144), ("zp", 144), ("te", 144), ("to", 144), ("x1", 256), ("xh", 256), ("xn", 256), ("o16", 128), ("oB", 128),
+        ("tmpa", 128), ("tmpb", 128), ("sgn", 128), ("tri", 128), ("nn", 160), ("gn", 128), ("n2", 256), ("s1", 8), ("s15", 8),
+        ("sm", 8), ("sa", 8), ("sp", 16), ("ip2", 16), ("rq", 8), ("prs", 40), ("c96", 40), ("am", 8))
 MOFF = {}
 _o = 0
 for _n, _c in MATS:
@@ -23,37 +22,41 @@ for _n, _c in MATS:
 SCRATCH = {
     "km": ("sbuf", [128, _o], "bfloat16"),
     "pko": ("sbuf", [128, 10 * SLOT], "float16"), "pki": ("sbuf", [128, 8 * PK], "float16"),
-    "iw": ("sbuf", [128, W], "int32"),
+    "iw": ("sbuf", [128, W], "int32"), "i32": ("sbuf", [128, 128], "float32"),
     "ip": ("sbuf", [128, 2], "int32"), "ci": ("sbuf", [128, 8], "int32"), "cf": ("sbuf", [128, 8], "float32"),
-    "cs": ("sbuf", [128, 16], "float32"),
-    "i8": ("sbuf", [128, 8], "float32"), "dum": ("sbuf", [128, 8], "float32"), "powl": ("sbuf", [128, 8], "float32"),
-    "px": ("sbuf", [128, 256], "int32"), "p1": ("sbuf", [128, 256], "int32"), "p2": ("sbuf", [128, 256], "int32"),
-    "p3": ("sbuf", [128, 256], "float32"), "hc": ("sbuf", [128, 2], "float32"), "ai": ("sbuf", [128, 2], "int32"),
+    "cs": ("sbuf", [128, 8], "float32"), "i8": ("sbuf", [128, 8], "float32"),
+    "px": ("sbuf", [128, 32], "int32"), "p1": ("sbuf", [128, 32], "int32"), "p2": ("sbuf", [128, 32], "int32"),
+    "p3": ("sbuf", [128, 32], "float32"), "hc": ("sbuf", [128, 1], "float32"), "hs": ("sbuf", [128, 8], "float32"),
+    "zt": ("sbuf", [128, 16, 144], "bfloat16"), "gq": ("sbuf", [128, 8, NQ], "bfloat16"), "db": ("sbuf", [128, 8, NQ], "bfloat16"),
+    "pr": ("sbuf", [128, 8, NQ], "bfloat16"), "keep": ("sbuf", [128, 8 * NQ], "bfloat16"),
+    "dn": ("sbuf", [128, 8, 4], "bfloat16"), "bo": ("sbuf", [128, 8], "uint16"), "bf": ("sbuf", [128, 8], "float32"),
+    "m88": ("sbuf", [128, 88], "float32"), "m89": ("sbuf", [128, 88], "float32"), "d0": ("sbuf", [128, 88], "bfloat16"),
+    "c88": ("sbuf", [128, 88], "float16"),
 }
 for _h in (0, 1):
-    for _n, _c, _d in (("nbi", W, "int32"), ("nbf", W + 128, "float32"), ("xt", W + 128, "bfloat16"), ("pvb", 8, "int32"),
-                       ("pzb", 128, "bfloat16"), ("thb", 4, "int32"), ("yvb", 8, "float32"), ("yzb", 128, "bfloat16"),
-                       ("vb0", 128, "float16"), ("v16", 8, "float16"), ("thf", 4, "float32"), ("dmv", 8, "float32"),
-                       ("v32", 8, "float32"), ("vu", 8, "uint16"), ("dv", 128, "bfloat16"), ("adv", 128, "bfloat16"),
-                       ("fs", 128, "bfloat16"), ("oh", 128, "bfloat16"), ("mk", 128 * REP, "bfloat16"), ("c16", 128, "float16"),
-                       ("tr", 128, "float16"), ("tl", 128, "uint16"), ("q", 128, "float16"), ("pa", 256, "float32"),
-                       ("pb", 256, "float32"), ("cl", 264, "uint16"), ("gm", 2048, "float16"), ("xg", 4224, "bfloat16"),
-                       ("ab", 4224, "bfloat16"), ("rr", 384, "bfloat16"), ("hw", 384, "bfloat16"), ("win", 384, "bfloat16"),
-                       ("sel", 384, "float16"), ("sb", 64, "float32"), ("cm", 8, "float32"),
-                       ("cn", 8, "float16"), ("wl", 8, "float32"), ("ox", 16, "uint16"), ("on", 16, "uint16"),
-                       ("nx", 256, "bfloat16"), ("qq", 128, "bfloat16")):
-        SCRATCH["%s%d" % (_n, _h)] = ("sbuf", [128, _c], _d)
-    SCRATCH["ew%d" % _h] = ("sbuf", [128, 8, 8, 16], "bfloat16")
-BANKS = ("H0", "H1", "M0", "M1", "D0", "D1", "E0", "E1")
+    for _n, _c, _d in (("nbi", [W], "int32"), ("nbf", [W + 128], "float32"), ("xt", [W + 128], "bfloat16"), ("pvb", [8], "int32"),
+                       ("pzb", [128], "bfloat16"), ("thb", [4], "int32"), ("yvb", [8], "float32"), ("yzb", [128], "bfloat16"),
+                       ("vb0", [128], "float16"), ("v16", [8], "float16"), ("thf", [4], "float32"), ("v32", [8], "float32"),
+                       ("vu", [8], "uint16"), ("dv", [128], "bfloat16"), ("adv", [128], "bfloat16"), ("fs", [128], "bfloat16"),
+                       ("mk", [512], "bfloat16"), ("c16", [128], "float16"), ("tr", [128], "float16"), ("tl", [128], "uint16"),
+                       ("q", [128], "float16"), ("cl", [264], "uint16"), ("gm", [2048], "float16"), ("xg", [4224], "bfloat16"),
+                       ("ab", [4224], "bfloat16"), ("ys", [8 * NQ], "float32"), ("sc", [8 * NQ], "float32"),
+                       ("bst", [8 * NQ], "float32"), ("pt", [128], "bfloat16"), ("bc", [128], "float32"), ("rr", [128], "bfloat16"), ("sl", [8], "float32"),
+                       ("hl", [8], "bfloat16"), ("uu", [128], "float16"), ("nv", [256], "float32"), ("nx", [256], "bfloat16"),
+                       ("ew", [8, 11, 16], "bfloat16"), ("ds", [88], "float16"), ("ox", [16], "uint16"), ("on", [16], "uint16"),
+                       ("thr", [8, NQ], "bfloat16")):
+        SCRATCH["%s%d" % (_n, _h)] = ("sbuf", [128] + _c, _d)
+BANKS = ("Z0", "Z1", "R0", "R1", "M0", "M1", "E0", "E1")
 for _n in BANKS:
-    SCRATCH[_n] = ("psum", [128, 512], "float32")
+    SCRATCH[_n] = ("psum", [128, 512] if _n[0] == "M" else [128, 8, 64], "float32")
 
 SEMAPHORES = (["sv", "sa", "st", "sp", "sent", "outd"] + ["ar%d" % i for i in range(8)]
               + ["l%s%d" % (x, s) for x in ("nb", "xd", "pv", "pz", "th") for s in (0, 1)])
 
-COST = {"f": 1.04, "g": 1.56, "s": 3.8, "pe": 0.52, "fv": 25.0, "fa": 70.0, "fp": 10.0, "sem": 150.0, "hop": 6500.0}
-TUNE = {"rounds": 600, "shake": 2500.0, "lag": 10000.0, "heat": 1000.0, "seed": 1, "reach": 1e9, "back": 1}
-CASES = ({"g": 1.1, "s": 2.5, "hop": 7500.0}, {"g": 2.0, "s": 5.0, "sem": 60.0, "hop": 4000.0}, {"pe": 0.75, "sem": 200.0}, {"fv": 65.0, "pe": 0.4, "g": 1.2, "s": 5.5})
+COST = {"f": 0.9, "g": 1.56, "s": 3.8, "pe": 0.45, "fv": 30.0, "fa": 65.0, "fp": 6.0, "sem": 80.0, "hop": 5500.0}
+TUNE = {"rounds": 1200, "shake": 2500.0, "lag": 10000.0, "heat": 800.0, "seed": 1, "reach": 1e9, "back": 1}
+CASES = ({"f": 0.83, "g": 1.2, "s": 2.5, "hop": 7000.0, "sem": 60.0}, {"f": 1.15, "g": 2.0, "s": 5.0, "sem": 60.0, "hop": 4500.0, "pe": 0.55},
+         {"pe": 0.6, "sem": 150.0, "fp": 12.0}, {"fv": 60.0, "pe": 0.42, "g": 1.2, "s": 5.5})
 ORDER = {}
 
 
@@ -79,7 +82,7 @@ def build(g, core, T, topo, rank):
     php = helper_of(T, topo, prev)
     acount = count(topo.mask(php if php is not None else T.cores[prev], core))
     V, A, PE = g.vector, g.scalar, g.tensor
-    ops, state, cur, tile = [], {}, [0], [0]
+    ops, state, cur = [], {}, [0]
     F, G, S = COST["f"], COST["g"], COST["s"]
 
     def add(e, fn, rd, wr, cost, ext=None, lat=0.0):
@@ -101,14 +104,14 @@ def build(g, core, T, topo, rank):
             state[k][1].append(i)
         for k in wr:
             state[k] = [i, []]
-        ops.append({"e": e, "fn": fn, "deps": deps, "cost": cost, "ext": ext, "lat": lat, "n": (wr + rd)[0][:4], "u": cur[0]})
+        ops.append({"e": e, "fn": fn, "deps": deps, "cost": cost, "ext": ext, "lat": lat, "n": (wr + rd)[0][:5], "u": cur[0]})
         return i
 
     def vec(fn, rd, wr, cyc, fix=0.0):
         return add("v", lambda: [fn()], rd, wr, COST["fv"] + fix + max(cyc, 64) * F)
 
-    def act(fn, rd, wr, cyc):
-        return add("a", lambda: [fn()], rd, wr, COST["fa"] + cyc * F)
+    def act(out, in_, func, rd, wr, cyc, fix=0.0, **kw):
+        return add("a", lambda: [A.activation(out, in_, func, **kw)], rd, wr, COST["fa"] + fix + cyc * F)
 
     def mm(lst, rd, wr):
         cost = sum(COST["fp"] + max(64, m[5]) * COST["pe"] for m in lst)
@@ -118,7 +121,7 @@ def build(g, core, T, topo, rank):
         return [(out, a, b, start and i == 0, stop and i == len(pairs) - 1, nn_) for i, (a, b) in enumerate(pairs)]
 
     def pool(fn, rd, wr, cyc):
-        return add("p", lambda: [fn()], rd, wr, 160 + 2 * cyc * F)
+        return add("p", lambda: [fn()], rd, wr, 170 + 2 * cyc * F)
 
     def ts(out, in0, s1, s2, o0, o1=None):
         if o1 is None:
@@ -131,13 +134,30 @@ def build(g, core, T, topo, rank):
     def cp(out, a):
         return lambda: V.tensor_copy(out, a)
 
+    def fill(out, val, key, cyc, rd=()):
+        return vec(lambda: V.memset(out, val), list(rd), [key], cyc)
+
+    def sel(out, in_, pat, op, other, base, cm, rd, wr, cyc):
+        return pool(lambda: g.affine_select(out, in_, pat, op, other, base, cm), rd, wr, cyc)
+
+    def copy(e, out, in_, rd, wr, cols, scale=1.0, bias=0.0, fix=0.0):
+        if e == "p":
+            return sel(out, in_, [[0, cols]], Op.is_ge, 0.0, 0, 0, rd, wr, cols)
+        if e == "a":
+            if bias:
+                return act(out, in_, Fn.Identity, rd, wr, cols, bias=bias, scale=scale)
+            return act(out, in_, Fn.Copy, rd, wr, cols, scale=scale)
+        if scale == 1.0 and not bias:
+            return vec(cp(out, in_), rd, wr, cols, fix)
+        return vec(ts(out, in_, scale, bias, Op.mult, Op.add), rd, wr, cols, fix)
+
     def dma(q, out, in_, sem, val, rd, wr, lat):
         eng = g.sync if q == "s" else A
         return add(q, lambda: [eng.dma_start(out, in_).then_inc(T.sem[sem], 16)], rd + ["q" + q], wr + ["q" + q], 60.0, ext=(sem, val), lat=lat)
 
-    def K(name, a=0, b=None):
+    def K(name, a=0, b=None, step=1):
         o, c = MOFF[name]
-        return T.km[:, o + a:o + (c if b is None else b)]
+        return T.km[:, o + a:o + (c if b is None else b):step]
 
     def wr_(z, r):
         return K(z, 15 - r, 143 - r)
@@ -147,6 +167,12 @@ def build(g, core, T, topo, rank):
 
     def blk(b, j):
         return b[:, 128 * j:128 * j + 128]
+
+    def pb(bank, j, m=1):
+        return bank[:, 2 * j:2 * (j + m), :]
+
+    def both(name):
+        return [K(name, 0, 128), K(name, 128, 256)]
 
     for s in (0, 1):
         rows = slice(64 * s, 64 * s + 64)
@@ -170,66 +196,86 @@ def build(g, core, T, topo, rank):
     iota(K("gn"), [[16, 8], [0, 16]], 0, 0, "gn", 128)
     iota(T.i8[:], [[16, 8]], W, 1, "i8", 8)
     iota(K("n2"), [[-64, 2], [0, 2], [1, 64]], 64, 0, "n2", 256)
-    for h in (0, 1):
-        iota(K("g2", 128 * h, 128 * h + 128), [[0, 2], [16, 4], [0, 16]], 64 - 64 * h, 0, "g2%d" % h, 128)
-        iota(T.px[:, 128 * h:128 * h + 128], [[16, 8], [1, 8], [256, 2]], 8 * h + 128 + 32768, -257, "px%d" % h, 128, False)
-    iota(K("k8"), [[0, 8], [1, 8]], 0, 0, "k8", 64)
-    vec(ts(K("keep"), K("k8"), 1.0, None, Op.min), ["k8"], ["keep"], 32)
+    iota(K("sgn"), [[0, 64], [-2, 2]], 1, 0, "sgn", 128)
+    iota(K("ip2"), [[16, 8], [1, 2]], 0, 0, "ip2", 16)
+    iota(T.gq[:], [[16, 8], [0, NQ]], 0, 0, "gq", 8 * NQ)
+    iota(T.px[:], [[1, 16], [256, 2]], 128 + 32768, -257, "px", 32, False)
+    iota(T.m88[:], [[1, 8], [1, 11]], -7, 0, "m88", 88)
     iota(T.iw[:], [[1, W]], 0, 0, "iw", W, False)
     for j, m in enumerate((127, 112, 113, 15)):
         vec(ts(T.ci[:, j:j + 1], T.ip[:, 0:1], m, None, Op.bitwise_and), ["ip"], ["ci%d" % j], 1)
     vec(ts(T.ci[:, 4:6], T.ip[:], 4, 1, Op.logical_shift_right, Op.bitwise_and), ["ip"], ["ci4"], 1)
     vec(cp(T.cf[:, 0:6], T.ci[:, 0:6]), ["ci%d" % j for j in range(5)], ["cf"], 1)
     pf, g16, gpar, kf, odd, even = [T.cf[:, j:j + 1] for j in range(6)]
-    sbias, obias, k16, nk16, kl15 = [T.cs[:, j:j + 1] for j in range(5)]
-    vec(ts(sbias, kf, 14.0, -0.6, Op.is_ge, Op.add), ["cf"], ["sbias"], 1)
-    vec(ts(obias, kf, -1.0, 0.5, Op.mult, Op.add), ["cf"], ["obias"], 1)
-    vec(ts(k16, kf, 15.0, 16.0, Op.is_equal, Op.mult), ["cf"], ["k16"], 1)
-    vec(ts(nk16, kf, 15.0, -16.0, Op.is_equal, Op.mult), ["cf"], ["nk16"], 1)
-    vec(ts(kl15, kf, 15.0, None, Op.is_lt), ["cf"], ["kl15"], 1)
-    for s in (0, 1):
-        vec(cp(B("thf", s)[:, 0:2], B("thb", s)[:, 0:2]), ["thb%d" % s], ["thf%d" % s], 1)
-        vec(ts(B("thf", s)[:, 2:3], k16, 64.0, B("thf", s)[:, 0:1], Op.mult, Op.add), ["k16", "thf%d" % s], ["hm%d" % s], 1)
+    k14, fb0, fbias, par, psign = [T.cs[:, j:j + 1] for j in range(5)]
+    act(k14, kf, Fn.Sigmoid, ["cf"], ["k14"], 1, 1300.0, bias=256.0 * 14.5, scale=-256.0)
+    vec(ts(fb0, kf, 14.0, 2.0, Op.is_equal, Op.mult), ["cf"], ["fb0"], 1)
+    vec(ts(par, fb0, k14, 8192.0, Op.add, Op.mult), ["fb0", "k14"], ["fb1"], 1)
+    vec(ts(fbias, par, -8192.0 - 384.0, None, Op.add), ["fb1"], ["fbias"], 1)
     n0 = K("nn", 16, 144)
-    for name, wgt in (("mI", 1.0), ("mN", -1.0), ("mH", 0.5)):
+    for name, wgt in (("mI", 1.0), ("mN", -1.0), ("n16", -16.0), ("n2k", -2048.0)):
         vec(ts(K(name), n0, pf, wgt, Op.is_equal, Op.mult), ["nn", "cf"], [name], 64)
-    vec(ts(K("tmpa"), K("nn", 15, 143), pf, None, Op.is_equal), ["nn", "cf"], ["tmpa"], 64)
-    vec(tt(K("mS"), K("tmpa"), K("mI"), Op.add), ["tmpa", "mI"], ["mS"], 256)
-    for name, wgt, dep in (("mB", 1.0, "cf"), ("mHB", 0.5, "cf"), ("mL", k16, "k16"), ("mNL", nk16, "nk16")):
-        vec(ts(K(name), K("gn"), g16, wgt, Op.is_equal, Op.mult), ["gn", "cf", dep], [name], 64)
-    vec(ts(K("tmpb"), n0, pf, -1.0, Op.is_gt, Op.mult), ["nn", "cf"], ["tmpb"], 64)
-    vec(tt(K("tmpc"), K("tmpb"), K("mB"), Op.mult), ["tmpb", "mB"], ["tmpc"], 256)
-    vec(tt(K("mV"), K("tmpc"), K("mH"), Op.add), ["tmpc", "mH"], ["mV"], 256)
+    vec(ts(T.i32[:], n0, pf, None, Op.is_equal), ["nn", "cf"], ["i32"], 128)
+    vec(ts(K("tmpa"), K("gn"), g16, -4.0, Op.is_equal, Op.mult), ["gn", "cf"], ["tmpa"], 64)
+    sel(K("mV"), K("tmpa"), [[1, 128]], Op.is_ge, 1.0, -2, -1, ["tmpa"], ["mV"], 128)
+    sel(K("mV"), K("mV"), [[1, 128]], Op.is_ge, 0.0, 0, -1, ["mV"], ["mV"], 128)
+    vec(ts(psign, gpar, g16, -2.0, Op.subtract, Op.mult), ["cf"], ["ps0"], 1)
+    vec(ts(psign, psign, 1.0, None, Op.add), ["ps0"], ["psign"], 1)
+    vec(ts(K("tmpb"), K("gn"), g16, psign, Op.is_equal, Op.mult), ["gn", "cf", "psign"], ["tmpb"], 64)
+    vec(tt(K("tmpb"), K("tmpb"), K("sgn"), Op.mult), ["tmpb", "sgn"], ["tmpb"], 256)
+    sel(K("alt"), K("tmpb"), [[1, 128]], Op.is_ge, 0.0, 0, -1, ["tmpb"], ["alt"], 128)
+    vec(lambda: V.transpose(K("alT"), K("alt")), ["alt"], ["alT"], 64)
+    vec(ts(K("a2k"), K("alt"), 2048.0, None, Op.mult), ["alt"], ["a2k"], 64)
     vec(ts(K("te"), K("nn", 0, 144), pf, even, Op.is_equal, Op.mult), ["nn", "cf"], ["te"], 72)
     vec(ts(K("to"), K("nn", 16, 160), pf, odd, Op.is_equal, Op.mult), ["nn", "cf"], ["to"], 72)
     vec(ts(K("zp", 0, 142), K("nn", 2, 144), gpar, None, Op.is_equal), ["nn", "cf"], ["zp"], 72)
-    for name, wgt in (("z1", 1.0), ("z2", 2.0), ("zn", -1.0), ("z16", 1.0 / 16), ("zs", 0.4), ("z34", 2.0 ** -34)):
-        vec(ts(K(name, 0, 143), K("nn", 1, 144), g16, wgt, Op.is_equal, Op.mult), ["nn", "cf"], [name], 72)
-    for name, wgt in (("x1", 1.0), ("xh", 0.5), ("xk", 2048.0), ("xn", -2048.0)):
+    vec(ts(K("z1", 0, 143), K("nn", 1, 144), g16, None, Op.is_equal), ["nn", "cf"], ["z1"], 72)
+    for name, wgt in (("x1", 1.0), ("xh", 0.5), ("xn", -1.0)):
         vec(ts(K(name), K("n2"), pf, wgt, Op.is_equal, Op.mult), ["n2", "cf"], [name], 128)
-    vec(ts(K("xb"), K("g2"), g16, None, Op.is_equal), ["g20", "g21", "cf"], ["xb"], 128)
-    czn = {}
-    for kh, nd in enumerate(ND):
-        if nd not in czn and nd > 0:
-            czn[nd] = "cz%d" % kh
-            tmp = "tmp" + "de"[kh]
-            vec(ts(K(tmp), K("nn", 16 - nd, 144 - nd), g16, -1.0, Op.is_lt, Op.mult), ["nn", "cf"], [tmp], 64)
-            vec(tt(K(czn[nd]), K(tmp), K("mB"), Op.mult), [tmp, "mB"], [czn[nd]], 256)
-    vec(ts(K("mC"), n0, 0.0, kl15, Op.mult, Op.add), ["nn", "kl15"], ["mC"], 64)
-    vec(lambda: V.memset(K("c132"), -132.0), [], ["c132"], 64)
-    vec(ts(T.dum[:], T.i8[:], g16, None, Op.subtract), ["i8", "cf"], ["dum"], 8)
-    act(lambda: A.activation(T.powl[:], T.dum[:], Fn.Exp, bias=LN2 * (63 + W), scale=-LN2), ["dum"], ["powl"], 1400)
-    vec(ts(T.p1[:], T.px[:], 15, None, Op.bitwise_and), ["px0", "px1"], ["p1"], 256)
-    vec(ts(T.p2[:], T.px[:], 4, 16, Op.logical_shift_right, Op.bitwise_and), ["px0", "px1"], ["p2"], 256)
-    vec(tt(T.p3[:], T.p1[:], T.p2[:], Op.add), ["p1", "p2"], ["p3"], 512)
-    act(lambda: A.activation(K("p4"), T.p3[:], Fn.Exp, bias=-LN2, scale=-LN2), ["p3", "powl"], ["p4"], 256)
-    for kh in (0, 1):
-        vec(tt(K("pw", 128 * kh, 128 * kh + 128), K("p4", 128 * kh, 128 * kh + 128), K("mB"), Op.mult), ["p4", "mB"], ["pw%d" % kh], 256)
+    for name, wgt in (("s1", 1.0), ("sm", -2 * BIG), ("sa", -BIG)):
+        vec(ts(K(name), K("nn", 16, 144, 16), g16, wgt, Op.is_equal, Op.mult), ["nn", "cf"], [name], 8)
+    vec(ts(K("s15"), K("nn", 31, 159, 16), pf, None, Op.is_equal), ["nn", "cf"], ["s15"], 8)
+    vec(ts(K("sp"), K("ip2"), gpar, None, Op.is_equal), ["ip2", "cf"], ["sp"], 16)
+    vec(ts(T.db[:], T.gq[:], g16, BIG, Op.is_equal, Op.mult), ["gq", "cf"], ["db"], 4 * NQ)
+    vec(ts(T.dn[:], T.gq[:, :, 0:4], g16, -BIG, Op.is_equal, Op.mult), ["gq", "cf"], ["dn"], 16)
+    fill(K("c132"), -132.0, "c132", 64)
+    fill(K("o16"), 1.0 / 16, "o16", 64)
+    fill(K("oB"), BIG / 128, "oB", 64)
+    fill(K("c96"), 96.0 / 256, "c96", 8)
+    fill(T.keep[:], 1.0, "keep", 4 * NQ)
+    fill(T.keep[:, 0:8 * NQ:NQ], 0.0, "keep", 8)
+    iota(T.bf[:], [[NQ, 8]], NQ - 1, 0, "bf", 8)
+    vec(cp(T.bo[:], T.bf[:]), ["bf"], ["bo"], 8)
+    vec(ts(T.p1[:], T.px[:], 15, None, Op.bitwise_and), ["px"], ["p1"], 32)
+    vec(ts(T.p2[:], T.px[:], 4, 16, Op.logical_shift_right, Op.bitwise_and), ["px"], ["p2"], 32)
+    vec(tt(T.p3[:], T.p1[:], T.p2[:], Op.add), ["p1", "p2"], ["p3"], 64)
+    vec(ts(K("prs", 0, 32), T.p3[:], -1.0 / 256, None, Op.mult), ["p3"], ["prs0"], 32)
+    fill(K("prs", 32, 33), 1.0 / 256, "prs1", 1)
+    fill(K("prs", 33, 34), -32.0 / 256, "prs2", 1)
+    mm(sum([grp(T.R0[:, j, 0:NQ], [(K("alT"), K("prs", 0, NQ)), (K("mI"), K("c96", 0, NQ))], NQ) for j in range(8)], []),
+       ["alT", "prs0", "prs1", "prs2", "mI", "c96"], ["R0"])
+    vec(tt(T.pr[:], T.R0[:, :, 0:NQ], T.db[:], Op.mult), ["R0", "db"], ["pr"], 8 * NQ)
+    fill(T.zt[:], 0.0, "zt", 8 * 144)
+    sel(K("tri"), K("o16"), [[1, 16], [16, 8]], Op.is_gt, EPS / 16, 0, -1, ["o16"], ["tri"], 128)
+    sel(K("tri"), K("tri"), [[0, 16], [-16, 8]], Op.is_ge, 0.0, 0, 1, ["tri"], ["tri"], 128)
+    sel(K("tri"), K("tri"), [[0, 16], [16, 8]], Op.is_ge, 0.0, 15, -1, ["tri"], ["tri"], 128)
+    vec(ts(T.zt[:, :, 15:143:16], K("tri"), 16.0, None, Op.mult), ["tri", "zt"], ["zt"], 64)
+    vec(ts(T.m89[:], T.m88[:], EPS - 1.0, 0.0, Op.add, Op.max), ["m88"], ["m89"], 88)
+    vec(ts(T.d0[:], T.m89[:], 1.0, None, Op.min), ["m89"], ["d0"], 88)
+    fill(T.d0[:, 9:88:11], -KK, "d0", 8)
+    fill(T.d0[:, 10:88:11], -1.0, "d0", 8)
+    vec(ts(T.c88[:], T.m88[:], 0.0, None, Op.mult), ["m88"], ["c88"], 88)
+    vec(ts(T.c88[:, 8:88:11], T.i8[:], 0.0, -1.0, Op.mult, Op.add), ["i8", "c88"], ["c88"], 8)
+    vec(ts(T.c88[:, 9:88:11], T.i8[:], g16, -1.0, Op.subtract, Op.mult), ["i8", "cf", "c88"], ["c88"], 8)
+    for s in (0, 1):
+        thf, thr = B("thf", s), B("thr", s)
+        vec(cp(thf[:, 0:2], B("thb", s)[:, 0:2]), ["thb%d" % s], ["thf%d" % s], 1)
+        vec(ts(thr[:, :, 0:32], T.db[:, :, 0:32], thf[:, 1:2], None, Op.mult), ["db", "thf%d" % s], ["thra%d" % s], 128)
+        vec(ts(thr[:, :, 32], T.db[:, :, 32], thf[:, 0:1], None, Op.mult), ["db", "thf%d" % s], ["thrb%d" % s], 8)
+        vec(cp(thr[:, :, 33], T.db[:, :, 33]), ["db"], ["thrc%d" % s], 8)
+        fill(B("ew", s)[:, :, 8:11, :], 0.0, "ewz%d" % s, 192)
 
     sends = {}
-
-    def both(name):
-        return [K(name, 0, 128), K(name, 128, 256)]
 
     def src(t, h):
         if t == 0:
@@ -238,21 +284,22 @@ def build(g, core, T, topo, rank):
         k = "pki%d%d" % (t, h)
         return T.pki[:, o:o + 8], T.pki[:, o + 8:o + 136], T.pki[:, o + 136:o + 264], k, k, k
 
-    def dedupe(t, h, wt, wk, off, bank):
+    def dedupe(t, h, off, rep):
         s = str(h)
         vl, z, vb, lk, zk, vk = src(t, h)
-        P = T[bank]
-        ew = B("ew", h)
+        P, bank, ew, ds = T["M" + s], "M" + s, B("ew", h), B("ds", h)
         for c in range(8):
-            vec(ts(ew[:, :, c, :], vb, B("v32", h)[:, c:c + 1], wt[:, c:c + 1], Op.is_equal, Op.mult),
-                [vk, "v32" + s, wk], ["ew%d%d" % (h, c)], 64)
-        mm(grp(P[:, 0:64], [(wr_("zs", r), ew[:, :, :, r]) for r in range(16)], 64), ["zs"] + ["ew%d%d" % (h, c) for c in range(8)], [bank])
-        vec(lambda: V.tensor_tensor_scan(B("sb", h)[:], K("keep", 0, 64), P[:, 0:64], 0.0, Op.mult, Op.add), [bank, "keep"], ["sb" + s], 64)
-        vec(tt(B("cm", h)[:], B("sb", h)[:, 7:64:8], wt[:], Op.is_ge), ["sb" + s, wk], ["cm" + s], 16)
-        vec(tt(B("cn", h)[:], B("cm", h)[:], B("dmv", h)[:], Op.mult), ["cm" + s, "dmv" + s], ["cn" + s], 16)
-        mm(sum([grp(P[:, 136 + 8 * j:144 + 8 * j], [(x, vl), (x, B("cn", h)[:])], 8) for j, x in enumerate(both("x1"))], []),
-           ["x1", lk, "cn" + s], [bank])
-        vec(cp(B(off, h)[:], P[:, 136:152]), [bank], [off + s], 16)
+            vc = B("v32", h)[:, c:c + 1]
+            fn = ts(ew[:, :, 7 - c, :], vb, vc, B("sl", h)[:, c:c + 1], Op.is_equal, Op.is_gt) if rep else ts(ew[:, :, 7 - c, :], vb, vc, None, Op.is_equal)
+            vec(fn, [vk, "v32" + s] + ["sl" + s] * rep, ["ew%d%d" % (h, c)], 64)
+        lst = [(P[:, 0:88], K("mI"), T.c88[:], True, False, 88), (P[:, 10:88:11], K("mI"), vl, False, False, 8)]
+        if rep:
+            lst.append((P[:, 8:88:11], T.i32[:], B("sl", h)[:], False, False, 256))
+        lst += grp(P[:, 0:88], [(T.zt[:, r, 15 - r:143 - r], ew[:, :, :, r]) for r in range(16)], 88, False, True)
+        mm(lst, ["mI", "c88", lk, "zt", "ewz" + s] + ["sl" + s, "i32"] * rep + ["ew%d%d" % (h, c) for c in range(8)], [bank])
+        vec(lambda: V.tensor_tensor_scan(ds[:], T.d0[:], P[:, 0:88], 0.0, Op.mult, Op.max), [bank, "d0"], ["ds" + s], 88)
+        mm(sum([grp(P[:, 96 + 8 * j:104 + 8 * j], [(x, ds[:, 10:88:11])], 8) for j, x in enumerate(both("x1"))], []), ["x1", "ds" + s], [bank])
+        copy(ENG["off"], B(off, h)[:], P[:, 96:112], [bank], [off + s], 16)
 
     def level(t, h):
         s = str(h)
@@ -261,179 +308,139 @@ def build(g, core, T, topo, rank):
         if t > 0:
             add("x", None, [], [lk], 0.0, ext=("ar%d" % (2 * (t - 1) + h), acount), lat=COST["hop"])
             ops[-1]["deps"][sends[(t - 1, h)]] = False
-            vec(cp(B("v32", h)[:], vl), [lk], ["v32" + s], 8)
-            vec(cp(B("vu", h)[:], B("v32", h)[:]), ["v32" + s], ["vu" + s], 8)
+            copy(ENG["vu"], B("vu", h)[:], vl, [lk], ["vu" + s], 8)
+            copy(ENG["v32"], B("v32", h)[:], vl, [lk], ["v32" + s], 8)
         else:
             vec(cp(B("vu", h)[:], B("pvb", h)[:]), ["pvb" + s], ["vu" + s], 8)
             vec(cp(B("v32", h)[:], B("pvb", h)[:]), ["pvb" + s], ["v32" + s], 8)
             vec(cp(vl, B("v32", h)[:]), ["v32" + s], [lk], 8)
-            vec(cp(vb, T.iw[:].indirect(B("vu", h)[:])), ["iw", "vu" + s], [vk], 128 * G, 30)
-        vec(tt(B("dmv", h)[:], T.dum[:], B("v32", h)[:], Op.subtract), ["dum", "v32" + s], ["dmv" + s], 16)
-        vec(tt(B("dv", h)[:], B("xt", h)[:, 0:W].indirect(B("vu", h)[:]), z, Op.subtract), ["xt" + s, "vu" + s, zk], ["dv" + s], 128 * G, 30)
-        act(lambda: A.activation(B("adv", h)[:], B("dv", h)[:], Fn.Abs), ["dv" + s], ["adv" + s], 128)
-        act(lambda: A.activation(B("fs", h)[:], B("adv", h)[:], Fn.Sign, bias=sbias, scale=0.4), ["adv" + s, "sbias"], ["fs" + s], 128)
-        mm(grp(E[:, 0:128], [(K("mV"), B("fs", h)[:])], 128), ["mV", "fs" + s], [ek])
-        act(lambda: A.activation(B("oh", h)[:], E[:, 0:128], Fn.Relu, bias=obias), [ek, "obias"], ["oh" + s], 128)
-        mm(sum([grp(blk(E, j), [(K("mS"), B("oh", h)[:])], 128) for j in range(REP)], []), ["mS", "oh" + s], [ek])
-        act(lambda: A.activation(B("mk", h)[:], E[:, 0:128 * REP], Fn.Copy), [ek], ["mk" + s], 128 * REP)
-
-    def early(t, h):
-        s = str(h)
-        vl, z, vb, lk, zk, vk = src(t, h)
-        D, dk = T["D" + s], "D" + s
-        lst, oh = [], B("oh", h)[:]
-        for j in (0, 1):
-            lst += grp(blk(D, j), [(both("x1")[j], B("c16", h)[:]), (both("xn")[j], oh)], 128)
-        if t < R - 1:
-            for j in (0, 1):
-                lst += grp(blk(D, 2 + j), [(both("xh")[j], B("dv", h)[:]), (both("x1")[j], z)], 128)
-        mm(lst, ["x1", "xn", "xh", "c16" + s, "oh" + s, "dv" + s, zk], [dk])
-        act(lambda: A.activation(B("pa", h)[:], D[:, 0:256], Fn.Copy), [dk], ["pa" + s], 256)
-        if t < R - 1:
-            act(lambda: A.activation(B("nx", h)[:], D[:, 256:512], Fn.Identity, bias=131.75), [dk], ["nx" + s], 256)
-            dedupe(t, h, T.powl, "powl", "ox", "M" + s)
-
-    def absfold(cols, dst, h, z, zk, rk, key):
-        d = "EM"[tile[0] & 1] + str(h)
-        tile[0] += 1
-        lst = []
-        for j, c in enumerate(cols):
-            lst += grp(blk(T[d], j), [(K("mI"), c), (K("mN"), z)], 128)
-        mm(lst, ["mI", "mN", zk] + rk, [d])
-        act(lambda: A.activation(B("ab", h)[:, dst:dst + 128 * len(cols)], T[d][:, 0:128 * len(cols)], Fn.Abs), [d], [key], 128 * len(cols))
+            copy("v", vb, T.iw[:].indirect(B("vu", h)[:]), ["iw", "vu" + s], [vk], 128 * G, fix=20.0)
+        vec(tt(B("dv", h)[:], B("xt", h)[:, 0:W].indirect(B("vu", h)[:]), z, Op.subtract), ["xt" + s, "vu" + s, zk], ["dv" + s], 128 * G, 20)
+        act(B("adv", h)[:], B("dv", h)[:], Fn.Abs, ["dv" + s], ["adv" + s], 128)
+        act(B("fs", h)[:], B("adv", h)[:], Fn.Sigmoid, ["adv" + s, "fbias"], ["fs" + s], 128, bias=fbias, scale=256.0)
+        mm(sum([grp(pb(E, j), [(K("mV"), B("fs", h)[:])], 128) for j in range(4)], []), ["mV", "fs" + s], [ek])
+        act(B("mk", h)[:], E[:], Fn.Sigmoid, [ek], ["mk" + s], 512, bias=-128.0, scale=256.0)
+        mm([(T["Z" + s][:, :, r:64:4], K("mI"), z, True, True, 128) for r in range(4)], ["mI", zk], ["Z" + s])
 
     def contacts(t, h):
         s = str(h)
-        H, M = T["H" + s], T["M" + s]
+        E, M, ek, mk_ = T["E" + s], T["M" + s], "E" + s, "M" + s
         vl, z, vb, lk, zk, vk = src(t, h)
-        xwin = B("xt", h)[:, 0:W]
+        xwin, mk, c16, cl, gm, xg = B("xt", h)[:, 0:W], B("mk", h), B("c16", h)[:], B("cl", h), B("gm", h), B("xg", h)
         win, wk = (B("nbi", h)[:], "nbi" + s) if t == 0 else (B("nbf", h)[:, 0:W], "nbf" + s)
-        vec(cp(B("c16", h)[:], win.indirect(B("vu", h)[:])), [wk, "vu" + s], ["c16" + s], 128 * G, 30)
-        vec(lambda: V.transpose(B("tr", h)[:], B("c16", h)[:]), ["c16" + s], ["tr" + s], 64)
+        copy(ENG["c16"], c16, win.indirect(B("vu", h)[:]), [wk, "vu" + s], ["c16" + s], 128 * G, fix=20.0)
+        vec(lambda: V.transpose(B("tr", h)[:], c16), ["c16" + s], ["tr" + s], 64)
         lst = []
         for c2 in range(4):
             for hh in (0, 1):
                 mats = (K("te", 16, 144), K("te", 0, 128)) if hh == 0 else (K("to", 16, 144), K("to", 0, 128))
                 lst += grp(M[:, 2 * c2 + hh:128:8], [(mats[gl], B("tr", h)[:, 32 * c2 + 16 * gl:32 * c2 + 16 * gl + 16]) for gl in (0, 1)], 16)
-        mm(lst, ["te", "to", "tr" + s], ["M" + s])
-        vec(cp(B("tl", h)[:], M[:, 0:128]), ["M" + s], ["tl" + s], 128)
-        mm(grp(H[:, 256:384], [(K("mI"), B("c16", h)[:])], 128) + grp(H[:, 384:512], [(K("mI"), z)], 128), ["mI", "c16" + s, zk], ["H" + s])
-        vec(tt(B("q", h)[:], H[:, 256:384], B("oh", h)[:], Op.mult), ["H" + s, "oh" + s], ["q" + s], 128)
-        mm(grp(M[:, 128:136], [(wr_("z1", r), B("q", h)[:, r:128:16]) for r in range(16)], 8), ["z1", "q" + s], ["M" + s])
-        vec(cp(B("cl", h)[:, 256:264], M[:, 128:136]), ["M" + s], ["cll" + s], 8)
-        act(lambda: A.activation(B("xg", h)[:, 4096:4224], xwin.indirect(B("cl", h)[:, 256:264]), Fn.Copy), ["xt" + s, "cll" + s], ["xgl" + s], 128 * G)
-        wdt = 128 * REP
-        for kh in (0, 1):
-            for j in range(1024 // wdt):
-                o = 1024 * kh + wdt * j
-                key = "gm%d%d%d" % (h, kh, j)
-                vec(tt(B("gm", h)[:, o:o + wdt], win.indirect(B("tl", h)[:, o // 16:(o + wdt) // 16]), B("mk", h)[:], Op.mult),
-                    [wk, "tl" + s, "mk" + s], [key], wdt * G, 30)
-                a0 = j * REP
-                mm(grp(blk(H, kh), [(K("zp", 14 - 2 * a, 142 - 2 * a), blk(B("gm", h), 8 * kh + a)) for a in range(a0, a0 + REP)],
-                       128, a0 == 0, a0 + REP == 8), ["zp", key], ["H" + s])
-            vec(cp(blk(B("cl", h), kh), blk(H, kh)), ["H" + s], ["cl%d%d" % (h, kh)], 128)
-            for o in range(2048 * kh, 2048 * kh + 2048, GCH):
-                act(lambda o=o: A.activation(B("xg", h)[:, o:o + GCH], xwin.indirect(B("cl", h)[:, o // 16:(o + GCH) // 16]), Fn.Copy),
-                    ["xt" + s, "cl%d%d" % (h, kh)], ["xg%d_%d" % (h, o)], GCH * G)
+        mm(lst, ["te", "to", "tr" + s], [mk_])
+        copy(ENG["tl"], B("tl", h)[:], blk(M, 0), [mk_], ["tl" + s], 128)
+        mm(grp(pb(E, 0), [(K("alt"), mk[:, 0:128])], 128), ["alt", "mk" + s], [ek])
+        vec(tt(B("q", h)[:], pb(E, 0), c16, Op.mult), [ek, "c16" + s], ["q" + s], 128)
+        mm(grp(E[:, 2, 0:8], [(wr_("z1", r), B("q", h)[:, r:128:16]) for r in range(16)], 8), ["z1", "q" + s], [ek])
+        copy(ENG["cll"], cl[:, 256:264], E[:, 2, 0:8], [ek], ["cll" + s], 8)
+        for j in range(4):
+            vec(tt(gm[:, 512 * j:512 * j + 512], win.indirect(B("tl", h)[:, 32 * j:32 * j + 32]), mk[:], Op.mult),
+                [wk, "tl" + s, "mk" + s], ["gm%d%d" % (h, j)], 512 * G, 20)
+            mm(grp(M[:, 256 + 64 * j:320 + 64 * j], [(K("zp", 14 - 8 * ip - 2 * a, 142 - 8 * ip - 2 * a), gm[:, 512 * j + 128 * a + ip:512 * j + 128 * a + 128:2])
+                                    for a in range(4) for ip in (0, 1)], 64), ["zp", "gm%d%d" % (h, j)], [mk_])
+            copy(ENG["cl"], cl[:, 64 * j:64 * j + 64], M[:, 256 + 64 * j:320 + 64 * j], [mk_], ["cl%d%d" % (h, j)], 64)
+            e = 8 * (j == 3)
+            act(xg[:, 1024 * j:1024 * j + 1024 + 16 * e], xwin.indirect(cl[:, 64 * j:64 * j + 64 + e]), Fn.Copy,
+                ["xt" + s, "cl%d%d" % (h, j)] + ["cll" + s] * (j == 3), ["xg%d%d" % (h, j)], (1024 + 16 * e) * G)
+        if t < R - 1:
+            mm(sum([grp(pb(E, j), [(both("xh")[j], B("dv", h)[:]), (both("x1")[j], z)], 128) for j in (0, 1)], []), ["x1", "xh", "dv" + s, zk], [ek])
+            act(B("nx", h)[:], pb(E, 0, 2), Fn.Identity, [ek], ["nx" + s], 256, bias=131.75)
+        lst = [(E[:, :, 0:NQ], mk[:, 0:128], T.pr[:], True, False, 8 * NQ)]
+        lst += [(E[:, :, 2 * k:2 * k + 2], blk(gm, k), K("sp"), False, False, 16) for k in range(16)]
+        lst += [(E[:, :, 32], B("q", h)[:], K("s1"), False, False, 8), (E[:, :, 33], c16, K("s15"), False, True, 8)]
+        mm(lst, ["mk" + s, "pr", "sp", "s1", "s15", "q" + s, "c16" + s] + ["gm%d%d" % (h, j) for j in range(4)], [ek])
+        copy(ENG["y"], B("ys", h)[:], E[:, :, 0:NQ], [ek], ["ys" + s], 8 * NQ)
 
-    def health(t, h):
+    def fold(t, h):
         s = str(h)
         vl, z, vb, lk, zk, vk = src(t, h)
-        absfold([B("xg", h)[:, 4096:4224]], 4096, h, z, zk, ["xgl" + s], "abl" + s)
-        mm(grp(T["D" + s][:, 256:384], [(K("mB"), B("ab", h)[:, 4096:4224])], 128), ["mB", "abl" + s], ["D" + s])
-
-    def fold(t, h, kh):
-        s = str(h)
-        vl, z, vb, lk, zk, vk = src(t, h)
-        nd = ND[kh]
-        o = 2048 * kh
-        rk = ["xg%d_%d" % (h, x) for x in range(o, o + 2048, GCH)]
-        out, dk = blk(T["D" + s], kh), "D" + s
-        col = lambda q: B("xg", h)[:, o + q:o + 2048:16]
-        res = lambda q: blk(B("ab", h), 16 * kh + q)
-        parts, dv, seq = [], [], []
-        rest = list(range(nd, 16))
-        while rest:
-            qs, rest = rest[:4], rest[4:]
-            key = "ab%d%d%d" % (h, kh, qs[0])
-            absfold([col(q) for q in qs], o + 128 * qs[0], h, z, zk, rk, key)
-            parts.append(([(wr_("z1", q), res(q)) for q in qs], ["z1", key]))
-        if nd:
-            seq.append(([(K(czn[nd]), z)] + [(wr_("zn", q), col(q)) for q in range(nd)], [czn[nd], "zn", zk] + rk))
-        for q0 in range(0, nd, 3):
-            qs = list(range(q0, min(nd, q0 + 3)))
-            for q in qs:
-                vec(tt(res(q), col(q), T["H" + s][:, 384:512], Op.max), rk + ["H" + s], ["ab%d%d%d" % (h, kh, q)], 128)
-            dv.append(([(wr_("z2", q), res(q)) for q in qs], ["z2"] + ["ab%d%d%d" % (h, kh, q) for q in qs]))
-        while dv or parts:
-            if dv:
-                seq.append(dv.pop(0))
-            if len(dv) > len(parts):
-                seq.append(dv.pop(0))
-            if parts:
-                seq.append(parts.pop(0))
-        for i, (pairs, rd) in enumerate(seq):
-            mm(grp(out, pairs, 128, i == 0, i == len(seq) - 1), rd, [dk])
+        Rb, rk, Z, E, xg, ab = T["R" + s], "R" + s, T["Z" + s], T["E" + s], B("xg", h), B("ab", h)
+        lst = [(Rb[:, :, 0:NQ], K("o16"), B("thr", h)[:], True, False, 8 * NQ)]
+        lst.append((Rb[:, :, 0:33], z, T.db[:, :, 0:33], False, False, 8 * 33))
+        for u in AQ:
+            lst.append((Rb[:, :, 8 * (u // 2) + u % 2:8 * (u // 2) + 8:2], z, T.dn[:], False, False, 32))
+        mm(lst, ["o16", "thra" + s, "thrb" + s, "thrc" + s, "db", "dn", zk], [rk])
+        xs = T.db[:, :, 0]
+        for u in range(8):
+            j, par_ = u // 2, u % 2
+            xk, key, quad, res = "xg%d%d" % (h, j), "ab%d%d" % (h, u), xg[:, 1024 * j + par_:1024 * j + 1024:2], ab[:, 512 * u:512 * u + 512]
+            sets = [(Rb[:, :, 8 * j + 2 * a + par_], xg[:, 1024 * j + 2 * a + par_:1024 * j + 1024:8], ab[:, 512 * u + a:512 * u + 512:4]) for a in range(4)]
+            if u in AQ:
+                mm([(E[:], K("mI"), quad, True, False, 512)]
+                   + [(E[:, :, r:64:4], K("mN"), z, False, r == 3, 128) for r in range(4)], ["mI", "mN", xk, zk], ["E" + s])
+                act(res, E[:], Fn.Abs, ["E" + s], [key], 512)
+                mm([(o, m, K("sa"), False, False, 8) for o, x, m in sets], ["sa", key], [rk])
+            else:
+                vec(tt(res, quad, Z[:], Op.max), [xk, "Z" + s], [key], 512)
+                mm([(o, x, xs, False, False, 8) for o, x, m in sets], ["db", xk], [rk])
+                mm([(o, m, K("sm"), False, False, 8) for o, x, m in sets], ["sm", key], [rk])
+        vec(tt(ab[:, 4096:4224], xg[:, 4096:4224], Z[:, :, 0:64:4], Op.max), ["xg%d3" % h, "Z" + s], ["abl" + s], 128)
+        lst = [(Rb[:, :, 32], xg[:, 4096:4224], xs, False, False, 8)]
+        if t > 0:
+            lst.append((Rb[:, :, 32], K("oB"), K("am"), False, False, 8))
+        lst.append((Rb[:, :, 32], ab[:, 4096:4224], K("sm"), False, True, 8))
+        mm(lst, ["db", "sm", "oB", "xg%d3" % h, "abl" + s] + ["am"] * (t > 0), [rk])
 
     def choose(t, h):
         s = str(h)
-        H, M, D = T["H" + s], T["M" + s], T["D" + s]
         vl, z, vb, lk, zk, vk = src(t, h)
-        oh, rr, hw, win, sel, thf = B("oh", h)[:], B("rr", h), B("hw", h), B("win", h), B("sel", h), B("thf", h)
-        mm(grp(blk(M, 0), [(both("pw")[0], oh)], 128) + grp(blk(M, 1), [(both("pw")[1], oh)], 128)
-           + grp(blk(M, 2), [(K("mI"), oh), (wr_("z34", 15), oh)], 128), ["pw0", "pw1", "mI", "z34", "oh" + s], ["M" + s])
-        th_, tk = (thf[:, 2:3], "hm" + s) if t == 0 else (thf[:, 3:4], "thr" + s)
-        act(lambda: A.activation(rr[:, 0:256], D[:, 0:256], Fn.Relu, bias=thf[:, 1:2], scale=-1.0), ["D" + s, "thf" + s], ["rra" + s], 256)
-        act(lambda: A.activation(rr[:, 256:384], D[:, 256:384], Fn.Relu, bias=th_, scale=-1.0), ["D" + s, tk], ["rrb" + s], 128)
-        vec(tt(hw[:], M[:, 0:384], rr[:], Op.min), ["M" + s, "rra" + s, "rrb" + s], ["hw" + s], 384)
-        mm(grp(blk(M, 3), [(K("mHB"), blk(hw, j)) for j in range(3)], 128), ["mHB", "hw" + s], ["M" + s])
-        for j in range(3):
-            vec(tt(blk(win, j), blk(M, 3), blk(hw, j), Op.is_le), ["M" + s, "hw" + s], ["win%d%d" % (h, j)], 128)
-        wins = ["win%d%d" % (h, j) for j in range(3)]
-        vec(tt(sel[:], H[:, 0:384], win[:], Op.mult), ["H" + s] + wins, ["sel" + s], 384)
-        mm(grp(blk(D, 0), [(K("mI"), z), (K("mNL"), blk(win, 2))], 128)
-           + grp(blk(D, 1), [(K("mI"), B("adv", h)[:]), (K("mL"), blk(win, 2))], 128), ["mI", "mL", "mNL", zk, "adv" + s, wins[2]], ["D" + s])
-        act(lambda: A.activation(B("qq", h)[:], blk(D, 1), Fn.Relu, bias=-16.0), ["D" + s], ["qq" + s], 128)
-        mm(grp(blk(M, 1), [(K("mB"), blk(win, j)) for j in range(2)], 128)
-           + grp(blk(M, 0), [(K("mB"), blk(sel, j)) for j in range(3)], 128), ["mB", "sel" + s] + wins, ["M" + s])
+        Rb, Z, E, rk, zb, ek = T["R" + s], T["Z" + s], T["E" + s], "R" + s, "Z" + s, "E" + s
+        sc, bst, pt, mk = B("sc", h), B("bst", h), B("pt", h)[:], B("mk", h)[:, 0:128]
+        last = t == R - 1
+        vec(tt(sc[:], Rb[:, :, 0:NQ], B("ys", h)[:], Op.min), [rk, "ys" + s], ["sc" + s], 8 * NQ)
+        vec(lambda: V.tensor_tensor_scan(bst[:], T.keep[:], sc[:], 0.0, Op.mult, Op.max), ["sc" + s, "keep"], ["bst" + s], 8 * NQ)
+        best = bst[:].indirect(T.bo[:])
+        copy(ENG["pt"], pt, best, ["bst" + s, "bo"], ["pt" + s], 128 * G, 1.0 / 2048, -0.35, 20.0)
+        copy(ENG["bc"], B("bc", h)[:], best, ["bst" + s, "bo"], ["bc" + s], 128 * G, fix=20.0)
+        mm([(pb(Z, 0), B("bc", h)[:], T.i32[:], True, False, 512)], ["bc" + s, "i32"], [zb])
+        mm([(pb(Z, 0), pt, K("n2k"), False, True, 128), (pb(Z, 1), pt, K("mI"), True, True, 128)], ["pt" + s, "n2k", "mI"], [zb])
         o = SLOT * (2 * t + h)
         k = "po%d%d" % (t, h)
-        vec(cp(T.pko[:, o + 136:o + 392], M[:, 0:256]), ["M" + s], [k + "b"], 256)
-        zout = T.pko[:, o + 8:o + 136] if t < R - 1 else B("yzb", h)[:]
-        vec(tt(zout, blk(D, 0), B("qq", h)[:], Op.max), ["D" + s, "qq" + s], [k + "z"], 128)
-        mm(grp(H[:, 0:16], [(wr_("z16", r), T.pko[:, o + 136 + r:o + 392:16]) for r in range(16)], 16), ["z16", k + "b"], ["H" + s])
-        lout = T.pko[:, o:o + 8] if t < R - 1 else B("yvb", h)[:]
-        vec(cp(lout, H[:, 0:8]), ["H" + s], [k + "l"], 8)
-        vec(tt(B("wl", h)[:], H[:, 8:16], T.powl[:], Op.mult), ["H" + s, "powl"], ["wl" + s], 8)
-        if t < R - 1:
+        copy(ENG["vb"], T.pko[:, o + 136:o + 392], pb(Z, 0, 2), [zb], [k + "b"], 256)
+        mm(grp(pb(Rb, 0), [(K("mI"), B("dv", h)[:]), (K("mI"), z), (pt, K("n16"))], 128), ["mI", "dv" + s, zk, "pt" + s, "n16"], [rk])
+        act(B("rr", h)[:], pb(Rb, 0), Fn.Relu, [rk], ["rr" + s], 128, bias=2560.0)
+        mm(grp(pb(Rb, 1), [(K("mI"), z), (K("mN"), B("rr", h)[:])], 128), ["mI", "mN", zk, "rr" + s], [rk])
+        act(B("yzb", h)[:] if last else T.pko[:, o + 8:o + 136], pb(Rb, 1), Fn.Abs, [rk], [k + "z"], 128)
+        mm(grp(E[:, 0, 0:16], [(wr_("z1", r), T.pko[:, o + 136 + r:o + 392:16]) for r in range(16)], 16), ["z1", k + "b"], [ek])
+        copy(ENG["lst"], B("yvb", h)[:] if last else T.pko[:, o:o + 8], E[:, 0, 0:8], [ek], [k + "l"], 8, 1.0 / 16)
+        act(B("sl", h)[:], E[:, 0, 8:16], Fn.Abs, [ek], ["sl" + s], 8, bias=-176.5 / 16, scale=1.0 / 256)
+        if not last:
             rid, pid = topo.addr(first, core)
             i = 2 * t + h
             sends[(t, h)] = add("p", lambda: [g.remote_dma(T.pki[:, PK * i:PK * i + PK], T.pko[:, o:o + PK], T.sem["ar%d" % i], T.sem.sent,
                                                            pid, rid, smask)], [k + "b", k + "z", k + "l"], [], 300.0, ext=("", 0))
-        E = T["E" + s]
-        mm(sum([grp(blk(E, j), [(both("x1")[j], T.pko[:, o + 136:o + 264]), (both("xk")[j], oh)], 128) for j in (0, 1)], []),
-           ["x1", "xk", k + "b", "oh" + s], ["E" + s])
-        act(lambda: A.activation(B("pb", h)[:], E[:, 0:256], Fn.Identity, bias=-2048.0), ["E" + s], ["pb" + s], 256)
-        dedupe(t, h, B("wl", h), "wl" + s, "on", "M" + s)
+            act(B("hl", h)[:], B("pt", h)[:, 0:128:16], Fn.Relu, ["pt" + s], ["hl" + s], 8, bias=-192.0)
+        mm(grp(pb(Z, 2), [(K("mI"), T.pko[:, o + 136:o + 264]), (K("a2k"), mk)], 128), ["mI", "a2k", k + "b", "mk" + s], [zb])
+        act(B("uu", h)[:], pb(Z, 2), Fn.Relu, [zb], ["uu" + s], 128, bias=-2048.0)
+        mm(sum([grp(pb(Z, j), [(both("x1")[j], B("c16", h)[:]), (both("xn")[j], B("q", h)[:]), (both("x1")[j], B("uu", h)[:])], 128)
+                for j in (0, 1)], []), ["x1", "xn", "c16" + s, "q" + s, "uu" + s], [zb])
+        copy(ENG["nv"], B("nv", h)[:], pb(Z, 0, 2), [zb], ["nv" + s], 256)
+        dedupe(t, h, "on", True)
 
     def put_x(h):
         for j in (0, 1):
             vec(tt(B("xt", h)[:].indirect(B("ox", h)[:, 8 * j:8 * j + 8]), blk(B("nx", h), j), K("c132"), Op.add),
-                ["ox%d" % h, "nx%d" % h, "c132"], ["xt%d" % h], 128 * S, 30)
+                ["ox%d" % h, "nx%d" % h, "c132"], ["xt%d" % h], 128 * S, 20)
 
     def put_nb(h):
         for j in (0, 1):
-            vec(tt(B("nbf", h)[:].indirect(B("on", h)[:, 8 * j:8 * j + 8]), blk(B("pa", h), j), blk(B("pb", h), j), Op.max),
-                ["on%d" % h, "pa%d" % h, "pb%d" % h], ["nbf%d" % h], 128 * S, 30)
+            vec(cp(B("nbf", h)[:].indirect(B("on", h)[:, 8 * j:8 * j + 8]), blk(B("nv", h), j)),
+                ["on%d" % h, "nv%d" % h], ["nbf%d" % h], 128 * S, 20)
 
     def tally():
-        mm(grp(T.D1[:, 256:384], [(K("mC"), B("win", h)[:, 256:384]) for h in (0, 1)], 128), ["mC", "win12", "win02"], ["D1"])
-        act(lambda: A.activation(K("junk"), T.D1[:, 256:384], Fn.Copy, accum_out=T.hc[:, 0:1]), ["D1"], ["hc", "junk"], 150)
-        vec(ts(T.ai[:, 0:1], T.hc[:, 0:1], -1.0, 2048.0, Op.mult, Op.add), ["hc"], ["ai0"], 1)
-        vec(ts(T.ai[:, 1:2], T.ai[:, 0:1], 15, None, Op.bitwise_and), ["ai0"], ["ai1"], 1)
-        for s in (0, 1):
-            vec(ts(B("thf", s)[:, 3:4], T.ai[:, 1:2], B("thf", s)[:, 2:3], None, Op.add), ["ai1", "hm%d" % s], ["thr%d" % s], 1)
+        P = T.E1[:, 1, 0:8]
+        mm(grp(P, [(K("o16"), B("hl", h)[:]) for h in (0, 1)], 8), ["o16", "hl0", "hl1"], ["E1"])
+        act(T.hs[:], P, Fn.Identity, ["E1"], ["hc", "junk"], 8, 20.0, bias=256.0, scale=16.0, accum_out=T.hc[:])
+        vec(ts(K("rq"), K("o16", 0, 8), T.hc[:], 0.47, Op.mult, Op.add), ["o16", "hc"], ["rq"], 8)
+        vec(ts(K("am"), K("rq"), 16.0, T.hc[:], Op.mult, Op.subtract), ["rq", "hc"], ["am"], 8)
 
     outs = []
     for t in range(R):
@@ -442,14 +449,13 @@ def build(g, core, T, topo, rank):
             cur[0] = 2 * t + h
             level(t, h)
             contacts(t, h)
-            early(t, h)
             if t == 0:
                 for a in range(0, W, 352):
-                    vec(cp(B("nbf", h)[:, a:a + 352], B("nbi", h)[:, a:a + 352]), ["nbi%d" % h], ["nbf%d_%d" % (h, a)], 352)
+                    copy(ENG["nbf"], B("nbf", h)[:, a:a + 352], B("nbi", h)[:, a:a + 352], ["nbi%d" % h], ["nbf%d_%d" % (h, a)], 352)
                 add("x", None, ["nbf%d_%d" % (h, a) for a in range(0, W, 352)], ["nbf%d" % h], 0.0)
-            health(t, h)
-            fold(t, h, 0)
-            fold(t, h, 1)
+            if not last:
+                dedupe(t, h, "ox", False)
+            fold(t, h)
             if not last:
                 put_x(h)
             choose(t, h)

@@ -1,15 +1,17 @@
+import math
 import numpy as np
 from concourse.mybir import AluOpType as Op, ActivationFunctionType as Fn
 
 W, R = 1408, 5
-PK, SLOT = 264, 392
+WS = W + 128
+PK, SLOT = 272, 400
 NQ = 34
-BIG, EPS, KK = 2.0 ** 19, 2.0 ** -17, 2.0 ** 28
-AQ = (7,)
-ENG = {"vu": "v", "v32": "p", "c16": "a", "tl": "a", "cll": "a", "cl": "a", "vb": "a", "lst": "a", "off": "a", "y": "a",
-       "pt": "a", "nv": "a", "nbf": "p", "bc": "v"}
+BIG, EPS, ETA = 2.0 ** 19, 2.0 ** -17, 24.26
+AQ = {}
+XV = {}
+ENG = {"vu": "v", "v32": "p", "c16": "a", "tl": "a", "cl": "v", "vb": "a", "off": "v", "pt": "a", "nv": "a", "nbf": "p", "bc": "v", "k": "a"}
 
-MATS = (("mI", 128), ("mN", 128), ("n16", 128), ("n2k", 128), ("mV", 128), ("alt", 128), ("alT", 128), ("a2k", 128), ("c132", 128),
+MATS = (("mI", 128), ("mN", 128), ("n16", 128), ("n2k", 128), ("hI", 128), ("sq", 128), ("cl16", 16), ("mV", 128), ("alt", 128), ("alT", 128), ("a2k", 128), ("c132", 128),
         ("z1", 144), ("zp", 144), ("te", 144), ("to", 144), ("x1", 256), ("xh", 256), ("xn", 256), ("o16", 128), ("oB", 128),
         ("tmpa", 128), ("tmpb", 128), ("sgn", 128), ("tri", 128), ("nn", 160), ("gn", 128), ("n2", 256), ("s1", 8), ("s15", 8),
         ("sm", 8), ("sa", 8), ("sp", 16), ("ip2", 16), ("rq", 8), ("prs", 40), ("c96", 40), ("am", 8))
@@ -24,39 +26,40 @@ SCRATCH = {
     "pko": ("sbuf", [128, 10 * SLOT], "float16"), "pki": ("sbuf", [128, 8 * PK], "float16"),
     "iw": ("sbuf", [128, W], "int32"), "i32": ("sbuf", [128, 128], "float32"),
     "ip": ("sbuf", [128, 2], "int32"), "ci": ("sbuf", [128, 8], "int32"), "cf": ("sbuf", [128, 8], "float32"),
-    "cs": ("sbuf", [128, 8], "float32"), "i8": ("sbuf", [128, 8], "float32"),
-    "px": ("sbuf", [128, 32], "int32"), "p1": ("sbuf", [128, 32], "int32"), "p2": ("sbuf", [128, 32], "int32"),
-    "p3": ("sbuf", [128, 32], "float32"), "hc": ("sbuf", [128, 1], "float32"), "hs": ("sbuf", [128, 8], "float32"),
-    "zt": ("sbuf", [128, 16, 144], "bfloat16"), "gq": ("sbuf", [128, 8, NQ], "bfloat16"), "db": ("sbuf", [128, 8, NQ], "bfloat16"),
-    "pr": ("sbuf", [128, 8, NQ], "bfloat16"), "keep": ("sbuf", [128, 8 * NQ], "bfloat16"),
-    "dn": ("sbuf", [128, 8, 4], "bfloat16"), "bo": ("sbuf", [128, 8], "uint16"), "bf": ("sbuf", [128, 8], "float32"),
-    "m88": ("sbuf", [128, 88], "float32"), "m89": ("sbuf", [128, 88], "float32"), "d0": ("sbuf", [128, 88], "bfloat16"),
-    "c88": ("sbuf", [128, 88], "float16"),
+    "cs": ("sbuf", [128, 8], "float32"), "i8": ("sbuf", [128, 16], "float32"),
+    "px": ("sbuf", [128, NQ], "int32"), "p1": ("sbuf", [128, NQ], "int32"), "p2": ("sbuf", [128, NQ], "int32"),
+    "p3": ("sbuf", [128, NQ], "float32"), "hc": ("sbuf", [128, 1], "float32"), "hs": ("sbuf", [128, 8], "float32"),
+    "zt": ("sbuf", [128, 16, 144], "bfloat16"), "zx": ("sbuf", [128, 16, 144], "bfloat16"),
+    "gq": ("sbuf", [128, 8 * NQ], "bfloat16"), "db": ("sbuf", [128, 8 * NQ], "bfloat16"),
+    "pr": ("sbuf", [128, 8 * NQ], "bfloat16"), "keep": ("sbuf", [128, 8 * NQ], "bfloat16"),
+    "bo": ("sbuf", [128, 8], "uint16"), "bf": ("sbuf", [128, 8], "float32"),
+    "m88": ("sbuf", [128, 88], "float32"), "m89": ("sbuf", [128, 88], "float32"), "d0": ("sbuf", [128, 176], "bfloat16"),
+    "c88": ("sbuf", [128, 176], "float16"),
 }
 for _h in (0, 1):
-    for _n, _c, _d in (("nbi", [W], "int32"), ("nbf", [W + 128], "float32"), ("xt", [W + 128], "bfloat16"), ("pvb", [8], "int32"),
+    for _n, _c, _d in (("nbi", [W], "int32"), ("nbf", [WS], "float32"), ("xt", [WS], "bfloat16"), ("pvb", [8], "int32"),
                        ("pzb", [128], "bfloat16"), ("thb", [4], "int32"), ("yvb", [8], "float32"), ("yzb", [128], "bfloat16"),
                        ("vb0", [128], "float16"), ("v16", [8], "float16"), ("thf", [4], "float32"), ("v32", [8], "float32"),
                        ("vu", [8], "uint16"), ("dv", [128], "bfloat16"), ("adv", [128], "bfloat16"), ("fs", [128], "bfloat16"),
                        ("mk", [512], "bfloat16"), ("c16", [128], "float16"), ("tr", [128], "float16"), ("tl", [128], "uint16"),
                        ("q", [128], "float16"), ("cl", [264], "uint16"), ("gm", [2048], "float16"), ("xg", [4224], "bfloat16"),
-                       ("ab", [4224], "bfloat16"), ("ys", [8 * NQ], "float32"), ("sc", [8 * NQ], "float32"),
-                       ("bst", [8 * NQ], "float32"), ("pt", [128], "bfloat16"), ("bc", [128], "float32"), ("rr", [128], "bfloat16"), ("sl", [8], "float32"),
+                       ("ab", [4224], "bfloat16"), ("hit", [8 * NQ], "bfloat16"), ("bst", [8 * NQ], "float32"),
+                       ("pt", [128], "bfloat16"), ("bc", [128], "float32"), ("rr", [128], "bfloat16"), ("wl", [8], "float32"),
                        ("hl", [8], "bfloat16"), ("uu", [128], "float16"), ("nv", [256], "float32"), ("nx", [256], "bfloat16"),
-                       ("ew", [8, 11, 16], "bfloat16"), ("ds", [88], "float16"), ("ox", [16], "uint16"), ("on", [16], "uint16"),
-                       ("thr", [8, NQ], "bfloat16")):
+                       ("ew", [8, 11, 16], "bfloat16"), ("ds", [176], "float16"), ("off", [32], "uint16"),
+                       ("thr", [8 * NQ], "bfloat16")):
         SCRATCH["%s%d" % (_n, _h)] = ("sbuf", [128] + _c, _d)
 BANKS = ("Z0", "Z1", "R0", "R1", "M0", "M1", "E0", "E1")
 for _n in BANKS:
-    SCRATCH[_n] = ("psum", [128, 512] if _n[0] == "M" else [128, 8, 64], "float32")
+    SCRATCH[_n] = ("psum", [128, 512], "float32")
 
-SEMAPHORES = (["sv", "sa", "st", "sp", "sent", "outd"] + ["ar%d" % i for i in range(8)]
+OWN = [_n[:-1] for _n in SCRATCH if _n[:-1] + "1" in SCRATCH and _n[-1] == "0"] + ["abl", "po", "pk"]
+SEMAPHORES = (["sv", "sa", "st", "sp", "sent", "outd", "zcp"] + ["ar%d" % i for i in range(8)]
               + ["l%s%d" % (x, s) for x in ("nb", "xd", "pv", "pz", "th") for s in (0, 1)])
 
-COST = {"f": 0.9, "g": 1.56, "s": 3.8, "pe": 0.45, "fv": 30.0, "fa": 65.0, "fp": 6.0, "sem": 80.0, "hop": 5500.0}
-TUNE = {"rounds": 1200, "shake": 2500.0, "lag": 10000.0, "heat": 800.0, "seed": 1, "reach": 1e9, "back": 1}
-CASES = ({"f": 0.83, "g": 1.2, "s": 2.5, "hop": 7000.0, "sem": 60.0}, {"f": 1.15, "g": 2.0, "s": 5.0, "sem": 60.0, "hop": 4500.0, "pe": 0.55},
-         {"pe": 0.6, "sem": 150.0, "fp": 12.0}, {"fv": 60.0, "pe": 0.42, "g": 1.2, "s": 5.5})
+COST = {"f": 0.97, "g": 1.56, "s": 3.8, "pe": 0.49, "fv": 15.0, "fa": 55.0, "fp": 4.0, "sem": 55.0, "hop": 4500.0, "dma": 0.8}
+TUNE = {"stages": ((3, 42000, 1200.0), (R, 4000, 300.0)), "last": 4000, "cool": 100.0, "seed": 2, "half": 8000.0, "split": 0}
+CASES = ({}, {"f": 0.9, "g": 1.3, "s": 4.5, "hop": 6000.0, "pe": 0.47, "sem": 80.0, "fv": 25.0})
 ORDER = {}
 
 
@@ -73,7 +76,7 @@ def count(mask):
     return bin(mask).count("1")
 
 
-def build(g, core, T, topo, rank):
+def build(g, core, T, topo, rank, R=R):
     n = len(T.cores)
     hp = helper_of(T, topo, rank)
     first = hp if hp is not None else T.cores[(rank + 1) % n]
@@ -82,7 +85,7 @@ def build(g, core, T, topo, rank):
     php = helper_of(T, topo, prev)
     acount = count(topo.mask(php if php is not None else T.cores[prev], core))
     V, A, PE = g.vector, g.scalar, g.tensor
-    ops, state, cur = [], {}, [0]
+    ops, state, cur, seen = [], {}, [-1], {}
     F, G, S = COST["f"], COST["g"], COST["s"]
 
     def add(e, fn, rd, wr, cost, ext=None, lat=0.0):
@@ -104,7 +107,12 @@ def build(g, core, T, topo, rank):
             state[k][1].append(i)
         for k in wr:
             state[k] = [i, []]
-        ops.append({"e": e, "fn": fn, "deps": deps, "cost": cost, "ext": ext, "lat": lat, "n": (wr + rd)[0][:5], "u": cur[0]})
+        name = (wr + rd)[0].replace("po%d" % (cur[0] // 2), "po").replace("pki%d" % (cur[0] // 2), "pk")
+        cut = max([len(b) for b in OWN if name.startswith(b + str(cur[0] % 2))] + [0]) if cur[0] >= 0 else 0
+        name = e + (name[:cut] + name[cut + 1:] if cut else name)
+        seen[(cur[0], name)] = seen.get((cur[0], name), 0) + 1
+        ops.append({"e": e, "fn": fn, "deps": deps, "cost": cost, "ext": ext, "lat": lat, "n": (wr + rd)[0][:5], "u": cur[0],
+                    "kind": (name, seen[(cur[0], name)])})
         return i
 
     def vec(fn, rd, wr, cyc, fix=0.0):
@@ -116,6 +124,18 @@ def build(g, core, T, topo, rank):
     def mm(lst, rd, wr):
         cost = sum(COST["fp"] + max(64, m[5]) * COST["pe"] for m in lst)
         return add("t", lambda: [PE.matmul(m[0], m[1], m[2], m[3], m[4]) for m in lst], rd, wr, cost)
+
+    def acc(lst, rd, bank, members):
+        left = members[0]
+
+        def fn():
+            left[0] -= 1
+            return [PE.matmul(m[0], m[1], m[2], False, left[0] == 0 and m is lst[-1]) for m in lst]
+        left[0] += 1
+        i = add("t", fn, rd, [], sum(COST["fp"] + max(64, m[3]) * COST["pe"] for m in lst))
+        ops[i]["deps"][state[bank][0]] = False
+        ops[i]["n"] = bank
+        members.append(i)
 
     def grp(out, pairs, nn_, start=True, stop=True):
         return [(out, a, b, start and i == 0, stop and i == len(pairs) - 1, nn_) for i, (a, b) in enumerate(pairs)]
@@ -153,7 +173,7 @@ def build(g, core, T, topo, rank):
 
     def dma(q, out, in_, sem, val, rd, wr, lat):
         eng = g.sync if q == "s" else A
-        return add(q, lambda: [eng.dma_start(out, in_).then_inc(T.sem[sem], 16)], rd + ["q" + q], wr + ["q" + q], 60.0, ext=(sem, val), lat=lat)
+        return add(q, lambda: [eng.dma_start(out, in_).then_inc(T.sem[sem], 16)], rd + ["q" + q], wr + ["q" + q], 60.0, ext=(sem, val), lat=lat * COST["dma"])
 
     def K(name, a=0, b=None, step=1):
         o, c = MOFF[name]
@@ -169,7 +189,7 @@ def build(g, core, T, topo, rank):
         return b[:, 128 * j:128 * j + 128]
 
     def pb(bank, j, m=1):
-        return bank[:, 2 * j:2 * (j + m), :]
+        return bank[:, 128 * j:128 * (j + m)]
 
     def both(name):
         return [K(name, 0, 128), K(name, 128, 256)]
@@ -194,12 +214,12 @@ def build(g, core, T, topo, rank):
     iota(T.ip[:], [[16, 2]], 0, 1, "ip", 2, False)
     iota(K("nn"), [[1, 160]], -16, 0, "nn", 160)
     iota(K("gn"), [[16, 8], [0, 16]], 0, 0, "gn", 128)
-    iota(T.i8[:], [[16, 8]], W, 1, "i8", 8)
+    iota(T.i8[:], [[0, 2], [16, 8]], W, 1, "i8", 16)
     iota(K("n2"), [[-64, 2], [0, 2], [1, 64]], 64, 0, "n2", 256)
     iota(K("sgn"), [[0, 64], [-2, 2]], 1, 0, "sgn", 128)
     iota(K("ip2"), [[16, 8], [1, 2]], 0, 0, "ip2", 16)
     iota(T.gq[:], [[16, 8], [0, NQ]], 0, 0, "gq", 8 * NQ)
-    iota(T.px[:], [[1, 16], [256, 2]], 128 + 32768, -257, "px", 32, False)
+    iota(T.px[:], [[256, 2], [1, 17]], 128 + 32768, -257, "px", NQ, False)
     iota(T.m88[:], [[1, 8], [1, 11]], -7, 0, "m88", 88)
     iota(T.iw[:], [[1, W]], 0, 0, "iw", W, False)
     for j, m in enumerate((127, 112, 113, 15)):
@@ -213,9 +233,10 @@ def build(g, core, T, topo, rank):
     vec(ts(par, fb0, k14, 8192.0, Op.add, Op.mult), ["fb0", "k14"], ["fb1"], 1)
     vec(ts(fbias, par, -8192.0 - 384.0, None, Op.add), ["fb1"], ["fbias"], 1)
     n0 = K("nn", 16, 144)
-    for name, wgt in (("mI", 1.0), ("mN", -1.0), ("n16", -16.0), ("n2k", -2048.0)):
-        vec(ts(K(name), n0, pf, wgt, Op.is_equal, Op.mult), ["nn", "cf"], [name], 64)
-    vec(ts(T.i32[:], n0, pf, None, Op.is_equal), ["nn", "cf"], ["i32"], 128)
+    vec(ts(K("mI"), n0, pf, None, Op.is_equal), ["nn", "cf"], ["mI"], 64)
+    for name, wgt in (("mN", -1.0), ("n16", -16.0), ("n2k", -2048.0), ("hI", BIG / 2)):
+        copy(ENG["k"], K(name), K("mI"), ["mI"], [name], 128 if ENG["k"] == "a" else 64, wgt)
+    copy("a", T.i32[:], K("mI"), ["mI"], ["i32"], 128)
     vec(ts(K("tmpa"), K("gn"), g16, -4.0, Op.is_equal, Op.mult), ["gn", "cf"], ["tmpa"], 64)
     sel(K("mV"), K("tmpa"), [[1, 128]], Op.is_ge, 1.0, -2, -1, ["tmpa"], ["mV"], 128)
     sel(K("mV"), K("mV"), [[1, 128]], Op.is_ge, 0.0, 0, -1, ["mV"], ["mV"], 128)
@@ -230,18 +251,20 @@ def build(g, core, T, topo, rank):
     vec(ts(K("to"), K("nn", 16, 160), pf, odd, Op.is_equal, Op.mult), ["nn", "cf"], ["to"], 72)
     vec(ts(K("zp", 0, 142), K("nn", 2, 144), gpar, None, Op.is_equal), ["nn", "cf"], ["zp"], 72)
     vec(ts(K("z1", 0, 143), K("nn", 1, 144), g16, None, Op.is_equal), ["nn", "cf"], ["z1"], 72)
-    for name, wgt in (("x1", 1.0), ("xh", 0.5), ("xn", -1.0)):
-        vec(ts(K(name), K("n2"), pf, wgt, Op.is_equal, Op.mult), ["n2", "cf"], [name], 128)
+    vec(ts(K("x1"), K("n2"), pf, None, Op.is_equal), ["n2", "cf"], ["x1"], 128)
+    copy("a", K("xn"), K("x1"), ["x1"], ["xn"], 256, -1.0)
+    copy("a", K("xh"), K("x1"), ["x1"], ["xh"], 256, 0.5)
     for name, wgt in (("s1", 1.0), ("sm", -2 * BIG), ("sa", -BIG)):
         vec(ts(K(name), K("nn", 16, 144, 16), g16, wgt, Op.is_equal, Op.mult), ["nn", "cf"], [name], 8)
     vec(ts(K("s15"), K("nn", 31, 159, 16), pf, None, Op.is_equal), ["nn", "cf"], ["s15"], 8)
     vec(ts(K("sp"), K("ip2"), gpar, None, Op.is_equal), ["ip2", "cf"], ["sp"], 16)
     vec(ts(T.db[:], T.gq[:], g16, BIG, Op.is_equal, Op.mult), ["gq", "cf"], ["db"], 4 * NQ)
-    vec(ts(T.dn[:], T.gq[:, :, 0:4], g16, -BIG, Op.is_equal, Op.mult), ["gq", "cf"], ["dn"], 16)
+    fill(K("cl16", 0, 8), 0.0, "cl16a", 8)
+    fill(K("cl16", 8, 16), 177.0, "cl16b", 8)
     fill(K("c132"), -132.0, "c132", 64)
     fill(K("o16"), 1.0 / 16, "o16", 64)
     fill(K("oB"), BIG / 128, "oB", 64)
-    fill(K("c96"), 96.0 / 256, "c96", 8)
+    fill(K("c96"), 32.0 / 256, "c96", 8)
     fill(T.keep[:], 1.0, "keep", 4 * NQ)
     fill(T.keep[:, 0:8 * NQ:NQ], 0.0, "keep", 8)
     iota(T.bf[:], [[NQ, 8]], NQ - 1, 0, "bf", 8)
@@ -249,30 +272,41 @@ def build(g, core, T, topo, rank):
     vec(ts(T.p1[:], T.px[:], 15, None, Op.bitwise_and), ["px"], ["p1"], 32)
     vec(ts(T.p2[:], T.px[:], 4, 16, Op.logical_shift_right, Op.bitwise_and), ["px"], ["p2"], 32)
     vec(tt(T.p3[:], T.p1[:], T.p2[:], Op.add), ["p1", "p2"], ["p3"], 64)
-    vec(ts(K("prs", 0, 32), T.p3[:], -1.0 / 256, None, Op.mult), ["p3"], ["prs0"], 32)
-    fill(K("prs", 32, 33), 1.0 / 256, "prs1", 1)
-    fill(K("prs", 33, 34), -32.0 / 256, "prs2", 1)
-    mm(sum([grp(T.R0[:, j, 0:NQ], [(K("alT"), K("prs", 0, NQ)), (K("mI"), K("c96", 0, NQ))], NQ) for j in range(8)], []),
-       ["alT", "prs0", "prs1", "prs2", "mI", "c96"], ["R0"])
-    vec(tt(T.pr[:], T.R0[:, :, 0:NQ], T.db[:], Op.mult), ["R0", "db"], ["pr"], 8 * NQ)
-    fill(T.zt[:], 0.0, "zt", 8 * 144)
+    vec(ts(K("prs", 0, NQ), T.p3[:], -1.0 / 256, None, Op.mult), ["p3"], ["prs"], 32)
+    fill(K("prs", 16, 17), 2.0 / 256, "prs", 1)
+    fill(K("prs", 33, 34), -32.0 / 256, "prs", 1)
+    mm(sum([grp(T.R0[:, NQ * j:NQ * j + NQ], [(K("alT"), K("prs", 0, NQ)), (K("mI"), K("c96", 0, NQ))], NQ) for j in range(8)], []),
+       ["alT", "prs", "mI", "c96"], ["R0"])
+    vec(tt(T.pr[:], T.R0[:, 0:8 * NQ], T.db[:], Op.mult), ["R0", "db"], ["pr"], 8 * NQ)
+    fill(T.zt[:, 0:4, :], 0.0, "z0", 2 * 144)
+    for a in range(4, 32, 4):
+        i = dma("s", (T.zt if a < 16 else T.zx)[:, a % 16:a % 16 + 4, :], T.zt[:, 0:4, :], "zcp", 112, ["z0"], ["z%d" % a], 2500.0)
+        for j in ops[i]["deps"]:
+            if ops[j]["e"] == "s":
+                ops[i]["deps"][j] = None
+    add("x", None, ["z%d" % a for a in range(4, 32, 4)], ["zt", "zx"], 0.0, ext=("zcp", 112))
     sel(K("tri"), K("o16"), [[1, 16], [16, 8]], Op.is_gt, EPS / 16, 0, -1, ["o16"], ["tri"], 128)
     sel(K("tri"), K("tri"), [[0, 16], [-16, 8]], Op.is_ge, 0.0, 0, 1, ["tri"], ["tri"], 128)
     sel(K("tri"), K("tri"), [[0, 16], [16, 8]], Op.is_ge, 0.0, 15, -1, ["tri"], ["tri"], 128)
     vec(ts(T.zt[:, :, 15:143:16], K("tri"), 16.0, None, Op.mult), ["tri", "zt"], ["zt"], 64)
+    act(K("sq"), K("tri"), Fn.Square, ["tri"], ["sq"], 128, scale=16.0)
+    act(T.zx[:, :, 15:143:16], K("sq"), Fn.Square, ["sq", "zx"], ["zx"], 128)
     vec(ts(T.m89[:], T.m88[:], EPS - 1.0, 0.0, Op.add, Op.max), ["m88"], ["m89"], 88)
-    vec(ts(T.d0[:], T.m89[:], 1.0, None, Op.min), ["m89"], ["d0"], 88)
-    fill(T.d0[:, 9:88:11], -KK, "d0", 8)
-    fill(T.d0[:, 10:88:11], -1.0, "d0", 8)
-    vec(ts(T.c88[:], T.m88[:], 0.0, None, Op.mult), ["m88"], ["c88"], 88)
-    vec(ts(T.c88[:, 8:88:11], T.i8[:], 0.0, -1.0, Op.mult, Op.add), ["i8", "c88"], ["c88"], 8)
-    vec(ts(T.c88[:, 9:88:11], T.i8[:], g16, -1.0, Op.subtract, Op.mult), ["i8", "cf", "c88"], ["c88"], 8)
+    vec(ts(T.d0[:, 88:176], T.m89[:], 1.0, None, Op.min), ["m89"], ["d0"], 88)
+    act(T.m89[:], T.d0[:, 88:176], Fn.Square, ["d0"], ["m89"], 88)
+    act(T.d0[:, 0:88], T.m89[:], Fn.Square, ["m89"], ["d0"], 88)
+    vec(ts(T.d0[:, 9:88:11], K("o16", 0, 8), 2.0 ** 59, -2.0 ** 59, Op.mult, Op.mult), ["d0", "o16"], ["d0"], 8)
+    fill(T.d0[:, 97:176:11], -2.0 ** 28, "d0", 8)
+    fill(T.d0[:, 10:176:11], -1.0, "d0", 8)
+    vec(ts(T.c88[:], T.keep[:, 0:176], 0.0, None, Op.mult), ["keep"], ["c88"], 88)
+    vec(ts(T.c88[:, 8:176:11], T.i8[:], 0.0, -16.5, Op.mult, Op.add), ["i8", "c88"], ["c88"], 8)
+    vec(ts(T.c88[:, 9:176:11], T.i8[:], g16, -1.0, Op.subtract, Op.mult), ["i8", "cf", "c88"], ["c88"], 8)
     for s in (0, 1):
         thf, thr = B("thf", s), B("thr", s)
         vec(cp(thf[:, 0:2], B("thb", s)[:, 0:2]), ["thb%d" % s], ["thf%d" % s], 1)
-        vec(ts(thr[:, :, 0:32], T.db[:, :, 0:32], thf[:, 1:2], None, Op.mult), ["db", "thf%d" % s], ["thra%d" % s], 128)
-        vec(ts(thr[:, :, 32], T.db[:, :, 32], thf[:, 0:1], None, Op.mult), ["db", "thf%d" % s], ["thrb%d" % s], 8)
-        vec(cp(thr[:, :, 33], T.db[:, :, 33]), ["db"], ["thrc%d" % s], 8)
+        vec(ts(thr[:], T.db[:], thf[:, 1:2], None, Op.mult), ["db", "thf%d" % s], ["thr%d" % s], 4 * NQ)
+        vec(ts(thr[:, 16:8 * NQ:NQ], T.db[:, 0:8 * NQ:NQ], thf[:, 0:1], None, Op.mult), ["db", "thf%d" % s], ["thr%d" % s], 8)
+        vec(cp(thr[:, 33:8 * NQ:NQ], T.db[:, 0:8 * NQ:NQ]), ["db"], ["thr%d" % s], 8)
         fill(B("ew", s)[:, :, 8:11, :], 0.0, "ewz%d" % s, 192)
 
     sends = {}
@@ -282,45 +316,55 @@ def build(g, core, T, topo, rank):
             return B("v16", h)[:], B("pzb", h)[:], B("vb0", h)[:], "v16%d" % h, "pzb%d" % h, "vb0%d" % h
         o = PK * (2 * (t - 1) + h)
         k = "pki%d%d" % (t, h)
-        return T.pki[:, o:o + 8], T.pki[:, o + 8:o + 136], T.pki[:, o + 136:o + 264], k, k, k
+        return T.pki[:, o:o + 8], T.pki[:, o + 16:o + 144], T.pki[:, o + 144:o + 272], k, k, k
 
-    def dedupe(t, h, off, rep):
+    def dedupe(t, h, kinds, kk):
         s = str(h)
         vl, z, vb, lk, zk, vk = src(t, h)
-        P, bank, ew, ds = T["M" + s], "M" + s, B("ew", h), B("ds", h)
+        P, bank, ew, ds, a = T["M" + s], "M" + s, B("ew", h), B("ds", h), 88 * (t == R - 1)
+        act(B("wl", h)[:], kinds, Fn.Sigmoid, [kk], ["wl" + s], 8, bias=17 * (17 + ETA) - ETA, scale=-17 - ETA)
+        mm([(P[:, a:176], K("mI"), T.c88[:, a:176], True, False, 176 - a)]
+           + [(P[:, b + 10:b + 88:11], K("mI"), vl, False, False, 8) for b in range(a, 176, 88)]
+           + [(P[:, 96:176:11], K("mI"), kinds, False, False, 8)], ["mI", "c88", lk, kk], [bank])
         for c in range(8):
-            vc = B("v32", h)[:, c:c + 1]
-            fn = ts(ew[:, :, 7 - c, :], vb, vc, B("sl", h)[:, c:c + 1], Op.is_equal, Op.is_gt) if rep else ts(ew[:, :, 7 - c, :], vb, vc, None, Op.is_equal)
-            vec(fn, [vk, "v32" + s] + ["sl" + s] * rep, ["ew%d%d" % (h, c)], 64)
-        lst = [(P[:, 0:88], K("mI"), T.c88[:], True, False, 88), (P[:, 10:88:11], K("mI"), vl, False, False, 8)]
-        if rep:
-            lst.append((P[:, 8:88:11], T.i32[:], B("sl", h)[:], False, False, 256))
-        lst += grp(P[:, 0:88], [(T.zt[:, r, 15 - r:143 - r], ew[:, :, :, r]) for r in range(16)], 88, False, True)
-        mm(lst, ["mI", "c88", lk, "zt", "ewz" + s] + ["sl" + s, "i32"] * rep + ["ew%d%d" % (h, c) for c in range(8)], [bank])
-        vec(lambda: V.tensor_tensor_scan(ds[:], T.d0[:], P[:, 0:88], 0.0, Op.mult, Op.max), [bank, "d0"], ["ds" + s], 88)
-        mm(sum([grp(P[:, 96 + 8 * j:104 + 8 * j], [(x, ds[:, 10:88:11])], 8) for j, x in enumerate(both("x1"))], []), ["x1", "ds" + s], [bank])
-        copy(ENG["off"], B(off, h)[:], P[:, 96:112], [bank], [off + s], 16)
+            vec(ts(ew[:, :, 7 - c, :], vb, B("v32", h)[:, c:c + 1], B("wl", h)[:, c:c + 1], Op.is_equal, Op.mult),
+                [vk, "v32" + s, "wl" + s], ["ew%d%d" % (h, c)], 64)
+        for b in range(a, 176, 88):
+            zz = T.zt if b else T.zx
+            mm(grp(P[:, b:b + 88], [(zz[:, r, 15 - r:143 - r], ew[:, :, :, r]) for r in range(16)], 88, False, b == 88),
+               ["zt", "zx", "ewz" + s] + ["ew%d%d" % (h, c) for c in range(8)], [bank])
+        vec(lambda: V.tensor_tensor_scan(ds[:, a:176], T.d0[:, a:176], P[:, a:176], 0.0, Op.mult, Op.max), [bank, "d0"], ["ds" + s], 176 - a)
+        m = 16 - a // 11
+        mm(sum([grp(P[:, 192 + m * j:192 + m * j + m], [(x, ds[:, a + 10:176:11])], m) for j, x in enumerate(both("x1"))], []), ["x1", "ds" + s], [bank])
+        copy(ENG["off"], B("off", h)[:, 0:2 * m], P[:, 192:192 + 2 * m], [bank], ["off" + s], 2 * m)
+        for j in (0, 1) * (not a):
+            vec(tt(B("xt", h)[:].indirect(B("off", h)[:, 16 * j:16 * j + 8]), blk(B("nx", h), j), K("c132"), Op.add),
+                ["off" + s, "nx" + s, "c132"], ["xt" + s], 128 * S, 35)
+        for j in (0, 1):
+            vec(cp(B("nbf", h)[:].indirect(B("off", h)[:, m * j + m - 8:m * j + m]), blk(B("nv", h), j)), ["off" + s, "nv" + s], ["nbf" + s], 128 * S, 35)
 
     def level(t, h):
-        s = str(h)
+        s, vu = str(h), B("vu", h)[:]
         vl, z, vb, lk, zk, vk = src(t, h)
         E, ek = T["E" + s], "E" + s
         if t > 0:
             add("x", None, [], [lk], 0.0, ext=("ar%d" % (2 * (t - 1) + h), acount), lat=COST["hop"])
             ops[-1]["deps"][sends[(t - 1, h)]] = False
-            copy(ENG["vu"], B("vu", h)[:], vl, [lk], ["vu" + s], 8)
+            copy(ENG["vu"], vu, vl, [lk], ["vu" + s], 8)
             copy(ENG["v32"], B("v32", h)[:], vl, [lk], ["v32" + s], 8)
         else:
-            vec(cp(B("vu", h)[:], B("pvb", h)[:]), ["pvb" + s], ["vu" + s], 8)
-            vec(cp(B("v32", h)[:], B("pvb", h)[:]), ["pvb" + s], ["v32" + s], 8)
-            vec(cp(vl, B("v32", h)[:]), ["v32" + s], [lk], 8)
-            copy("v", vb, T.iw[:].indirect(B("vu", h)[:]), ["iw", "vu" + s], [vk], 128 * G, fix=20.0)
-        vec(tt(B("dv", h)[:], B("xt", h)[:, 0:W].indirect(B("vu", h)[:]), z, Op.subtract), ["xt" + s, "vu" + s, zk], ["dv" + s], 128 * G, 20)
+            vec(cp(vu, B("pvb", h)[:]), ["pvb" + s], ["vu" + s], 8)
+            copy("p", B("v32", h)[:], B("pvb", h)[:], ["pvb" + s], ["v32" + s], 8)
+            copy("p", vl, B("pvb", h)[:], ["pvb" + s], [lk], 8)
+            copy("a", vb, T.iw[:].indirect(vu), ["iw", "vu" + s], [vk], 128 * G)
+        vec(tt(B("dv", h)[:], B("xt", h)[:, 0:W].indirect(vu), z, Op.subtract), ["xt" + s, "vu" + s, zk], ["dv" + s], 128 * G, 35)
         act(B("adv", h)[:], B("dv", h)[:], Fn.Abs, ["dv" + s], ["adv" + s], 128)
+        win, wk = (B("nbi", h)[:], "nbi" + s) if t == 0 else (B("nbf", h)[:, 0:W], "nbf" + s)
+        copy(ENG["c16"], B("c16", h)[:], win.indirect(vu), [wk, "vu" + s], ["c16" + s], 128 * G, fix=35.0)
         act(B("fs", h)[:], B("adv", h)[:], Fn.Sigmoid, ["adv" + s, "fbias"], ["fs" + s], 128, bias=fbias, scale=256.0)
         mm(sum([grp(pb(E, j), [(K("mV"), B("fs", h)[:])], 128) for j in range(4)], []), ["mV", "fs" + s], [ek])
         act(B("mk", h)[:], E[:], Fn.Sigmoid, [ek], ["mk" + s], 512, bias=-128.0, scale=256.0)
-        mm([(T["Z" + s][:, :, r:64:4], K("mI"), z, True, True, 128) for r in range(4)], ["mI", zk], ["Z" + s])
+        mm([(T["Z" + s][:, r:512:4], K("mI"), z, True, True, 128) for r in range(4)], ["mI", zk], ["Z" + s])
 
     def contacts(t, h):
         s = str(h)
@@ -328,7 +372,6 @@ def build(g, core, T, topo, rank):
         vl, z, vb, lk, zk, vk = src(t, h)
         xwin, mk, c16, cl, gm, xg = B("xt", h)[:, 0:W], B("mk", h), B("c16", h)[:], B("cl", h), B("gm", h), B("xg", h)
         win, wk = (B("nbi", h)[:], "nbi" + s) if t == 0 else (B("nbf", h)[:, 0:W], "nbf" + s)
-        copy(ENG["c16"], c16, win.indirect(B("vu", h)[:]), [wk, "vu" + s], ["c16" + s], 128 * G, fix=20.0)
         vec(lambda: V.transpose(B("tr", h)[:], c16), ["c16" + s], ["tr" + s], 64)
         lst = []
         for c2 in range(4):
@@ -339,64 +382,65 @@ def build(g, core, T, topo, rank):
         copy(ENG["tl"], B("tl", h)[:], blk(M, 0), [mk_], ["tl" + s], 128)
         mm(grp(pb(E, 0), [(K("alt"), mk[:, 0:128])], 128), ["alt", "mk" + s], [ek])
         vec(tt(B("q", h)[:], pb(E, 0), c16, Op.mult), [ek, "c16" + s], ["q" + s], 128)
-        mm(grp(E[:, 2, 0:8], [(wr_("z1", r), B("q", h)[:, r:128:16]) for r in range(16)], 8), ["z1", "q" + s], [ek])
-        copy(ENG["cll"], cl[:, 256:264], E[:, 2, 0:8], [ek], ["cll" + s], 8)
         for j in range(4):
-            vec(tt(gm[:, 512 * j:512 * j + 512], win.indirect(B("tl", h)[:, 32 * j:32 * j + 32]), mk[:], Op.mult),
-                [wk, "tl" + s, "mk" + s], ["gm%d%d" % (h, j)], 512 * G, 20)
-            mm(grp(M[:, 256 + 64 * j:320 + 64 * j], [(K("zp", 14 - 8 * ip - 2 * a, 142 - 8 * ip - 2 * a), gm[:, 512 * j + 128 * a + ip:512 * j + 128 * a + 128:2])
-                                    for a in range(4) for ip in (0, 1)], 64), ["zp", "gm%d%d" % (h, j)], [mk_])
-            copy(ENG["cl"], cl[:, 64 * j:64 * j + 64], M[:, 256 + 64 * j:320 + 64 * j], [mk_], ["cl%d%d" % (h, j)], 64)
             e = 8 * (j == 3)
-            act(xg[:, 1024 * j:1024 * j + 1024 + 16 * e], xwin.indirect(cl[:, 64 * j:64 * j + 64 + e]), Fn.Copy,
-                ["xt" + s, "cl%d%d" % (h, j)] + ["cll" + s] * (j == 3), ["xg%d%d" % (h, j)], (1024 + 16 * e) * G)
+            vec(tt(gm[:, 512 * j:512 * j + 512], win.indirect(B("tl", h)[:, 32 * j:32 * j + 32]), mk[:], Op.mult),
+                [wk, "tl" + s, "mk" + s], ["gm%d%d" % (h, j)], 512 * G, 35)
+            if e:
+                mm(grp(M[:, 384:392], [(wr_("z1", r), B("q", h)[:, r:128:16]) for r in range(16)], 8), ["z1", "q" + s], [mk_])
+            mm(grp(M[:, 128 + 64 * j:192 + 64 * j], [(K("zp", 14 - 8 * ip - 2 * a, 142 - 8 * ip - 2 * a), gm[:, 512 * j + 128 * a + ip:512 * j + 128 * a + 128:2])
+                                                     for a in range(4) for ip in (0, 1)], 64), ["zp", "gm%d%d" % (h, j)], [mk_])
+            copy(ENG["cl"], cl[:, 64 * j:64 * j + 64 + e], M[:, 128 + 64 * j:192 + 64 * j + e], [mk_], ["cl%d%d" % (h, j)], 64 + e)
+            cuts = [0, 32, 64 + e] if TUNE["split"] else [0, 64 + e]
+            for a, b in zip(cuts, cuts[1:]):
+                copy("v" if j in XV.get((t, h), ()) else "a", xg[:, 1024 * j + 16 * a:1024 * j + 16 * b], xwin.indirect(cl[:, 64 * j + a:64 * j + b]),
+                     ["xt" + s, "cl%d%d" % (h, j)], ["xg%d%d0" % (h, j)] * (a == 0) + ["xg%d%d1" % (h, j)] * (b > 32), 16 * (b - a) * G, fix=35.0)
         if t < R - 1:
             mm(sum([grp(pb(E, j), [(both("xh")[j], B("dv", h)[:]), (both("x1")[j], z)], 128) for j in (0, 1)], []), ["x1", "xh", "dv" + s, zk], [ek])
             act(B("nx", h)[:], pb(E, 0, 2), Fn.Identity, [ek], ["nx" + s], 256, bias=131.75)
-        lst = [(E[:, :, 0:NQ], mk[:, 0:128], T.pr[:], True, False, 8 * NQ)]
-        lst += [(E[:, :, 2 * k:2 * k + 2], blk(gm, k), K("sp"), False, False, 16) for k in range(16)]
-        lst += [(E[:, :, 32], B("q", h)[:], K("s1"), False, False, 8), (E[:, :, 33], c16, K("s15"), False, True, 8)]
-        mm(lst, ["mk" + s, "pr", "sp", "s1", "s15", "q" + s, "c16" + s] + ["gm%d%d" % (h, j) for j in range(4)], [ek])
-        copy(ENG["y"], B("ys", h)[:], E[:, :, 0:NQ], [ek], ["ys" + s], 8 * NQ)
+        lst = [(M[:, 0:8 * NQ], mk[:, 0:128], T.pr[:], True, False, 8 * NQ)]
+        lst += [(M[:, k:8 * NQ:17], blk(gm, k), K("sp"), False, False, 16) for k in range(16)]
+        lst += [(M[:, 16:8 * NQ:NQ], B("q", h)[:], K("s1"), False, False, 8), (M[:, 33:8 * NQ:NQ], c16, K("s15"), False, False, 8)]
+        mm(lst, ["mk" + s, "pr", "sp", "s1", "s15", "q" + s, "c16" + s] + ["gm%d%d" % (h, j) for j in range(4)], [mk_])
 
     def fold(t, h):
         s = str(h)
         vl, z, vb, lk, zk, vk = src(t, h)
         Rb, rk, Z, E, xg, ab = T["R" + s], "R" + s, T["Z" + s], T["E" + s], B("xg", h), B("ab", h)
-        lst = [(Rb[:, :, 0:NQ], K("o16"), B("thr", h)[:], True, False, 8 * NQ)]
-        lst.append((Rb[:, :, 0:33], z, T.db[:, :, 0:33], False, False, 8 * 33))
-        for u in AQ:
-            lst.append((Rb[:, :, 8 * (u // 2) + u % 2:8 * (u // 2) + 8:2], z, T.dn[:], False, False, 32))
-        mm(lst, ["o16", "thra" + s, "thrb" + s, "thrc" + s, "db", "dn", zk], [rk])
-        xs = T.db[:, :, 0]
+        aq = AQ.get((t, h), (1,))
+        lst = [(Rb[:, 0:8 * NQ], K("o16"), B("thr", h)[:], True, False, 8 * NQ), (Rb[:, 0:8 * NQ], z, T.db[:], False, False, 8 * NQ)]
+        lst += [(Rb[:, 17 * (u % 2) + 4 * (u // 2) + a:8 * NQ:NQ], z, K("sa"), False, False, 8) for u in aq for a in range(4)]
+        mm(lst, ["o16", "thr" + s, "db", "sa", zk], [rk])
+        xs, mem = T.db[:, 0:8 * NQ:NQ], [[0]]
         for u in range(8):
             j, par_ = u // 2, u % 2
-            xk, key, quad, res = "xg%d%d" % (h, j), "ab%d%d" % (h, u), xg[:, 1024 * j + par_:1024 * j + 1024:2], ab[:, 512 * u:512 * u + 512]
-            sets = [(Rb[:, :, 8 * j + 2 * a + par_], xg[:, 1024 * j + 2 * a + par_:1024 * j + 1024:8], ab[:, 512 * u + a:512 * u + 512:4]) for a in range(4)]
-            if u in AQ:
+            xk, key, quad, res = ["xg%d%d0" % (h, j), "xg%d%d1" % (h, j)], "ab%d%d" % (h, u), xg[:, 1024 * j + par_:1024 * j + 1024:2], ab[:, 512 * u:512 * u + 512]
+            sets = [(Rb[:, 17 * par_ + 4 * j + a:8 * NQ:NQ], xg[:, 1024 * j + 2 * a + par_:1024 * j + 1024:8], ab[:, 512 * u + a:512 * u + 512:4]) for a in range(4)]
+            if u in aq:
                 mm([(E[:], K("mI"), quad, True, False, 512)]
-                   + [(E[:, :, r:64:4], K("mN"), z, False, r == 3, 128) for r in range(4)], ["mI", "mN", xk, zk], ["E" + s])
+                   + [(E[:, r:512:4], K("mN"), z, False, r == 3, 128) for r in range(4)], ["mI", "mN", zk] + xk, ["E" + s])
                 act(res, E[:], Fn.Abs, ["E" + s], [key], 512)
-                mm([(o, m, K("sa"), False, False, 8) for o, x, m in sets], ["sa", key], [rk])
+                acc([(o, m, K("sa"), 8) for o, x, m in sets], ["sa", key], rk, mem)
             else:
-                vec(tt(res, quad, Z[:], Op.max), [xk, "Z" + s], [key], 512)
-                mm([(o, x, xs, False, False, 8) for o, x, m in sets], ["db", xk], [rk])
-                mm([(o, m, K("sm"), False, False, 8) for o, x, m in sets], ["sm", key], [rk])
-        vec(tt(ab[:, 4096:4224], xg[:, 4096:4224], Z[:, :, 0:64:4], Op.max), ["xg%d3" % h, "Z" + s], ["abl" + s], 128)
-        lst = [(Rb[:, :, 32], xg[:, 4096:4224], xs, False, False, 8)]
+                vec(tt(res, quad, Z[:], Op.max), xk + ["Z" + s], [key], 512)
+                acc([(o, x, xs, 8) for o, x, m in sets], ["db"] + xk, rk, mem)
+                acc([(o, m, K("sm"), 8) for o, x, m in sets], ["sm", key], rk, mem)
+        vec(tt(ab[:, 4096:4224], xg[:, 4096:4224], Z[:, 0:512:4], Op.max), ["xg%d31" % h, "Z" + s], ["abl" + s], 128)
         if t > 0:
-            lst.append((Rb[:, :, 32], K("oB"), K("am"), False, False, 8))
-        lst.append((Rb[:, :, 32], ab[:, 4096:4224], K("sm"), False, True, 8))
-        mm(lst, ["db", "sm", "oB", "xg%d3" % h, "abl" + s] + ["am"] * (t > 0), [rk])
+            acc([(Rb[:, 16:8 * NQ:NQ], K("oB"), K("am"), 8)], ["oB", "am"], rk, mem)
+        acc([(Rb[:, 16:8 * NQ:NQ], xg[:, 4096:4224], xs, 8), (Rb[:, 16:8 * NQ:NQ], ab[:, 4096:4224], K("sm"), 8)], ["db", "sm", "xg%d31" % h, "abl" + s], rk, mem)
+        return mem[1:]
 
-    def choose(t, h):
+    def choose(t, h, sums):
         s = str(h)
         vl, z, vb, lk, zk, vk = src(t, h)
         Rb, Z, E, rk, zb, ek = T["R" + s], T["Z" + s], T["E" + s], "R" + s, "Z" + s, "E" + s
-        sc, bst, pt, mk = B("sc", h), B("bst", h), B("pt", h)[:], B("mk", h)[:, 0:128]
+        M, bst, pt, mk = T["M" + s], B("bst", h), B("pt", h)[:], B("mk", h)[:, 0:128]
         last = t == R - 1
-        vec(tt(sc[:], Rb[:, :, 0:NQ], B("ys", h)[:], Op.min), [rk, "ys" + s], ["sc" + s], 8 * NQ)
-        vec(lambda: V.tensor_tensor_scan(bst[:], T.keep[:], sc[:], 0.0, Op.mult, Op.max), ["sc" + s, "keep"], ["bst" + s], 8 * NQ)
+        i = act(B("hit", h)[:], Rb[:, 0:8 * NQ], Fn.Sign, [rk], ["hit" + s], 8 * NQ, bias=-0.5, scale=1.0 / BIG)
+        ops[i]["deps"].update({j: True for j in sums})
+        mm([(M[:, 0:8 * NQ], K("hI"), B("hit", h)[:], False, True, 8 * NQ)], ["hI", "hit" + s], ["M" + s])
+        vec(lambda: V.tensor_tensor_scan(bst[:], T.keep[:], M[:, 0:8 * NQ], 0.0, Op.mult, Op.max), ["M" + s, "keep"], ["bst" + s], 8 * NQ)
         best = bst[:].indirect(T.bo[:])
         copy(ENG["pt"], pt, best, ["bst" + s, "bo"], ["pt" + s], 128 * G, 1.0 / 2048, -0.35, 20.0)
         copy(ENG["bc"], B("bc", h)[:], best, ["bst" + s, "bo"], ["bc" + s], 128 * G, fix=20.0)
@@ -404,39 +448,31 @@ def build(g, core, T, topo, rank):
         mm([(pb(Z, 0), pt, K("n2k"), False, True, 128), (pb(Z, 1), pt, K("mI"), True, True, 128)], ["pt" + s, "n2k", "mI"], [zb])
         o = SLOT * (2 * t + h)
         k = "po%d%d" % (t, h)
-        copy(ENG["vb"], T.pko[:, o + 136:o + 392], pb(Z, 0, 2), [zb], [k + "b"], 256)
+        copy(ENG["vb"], T.pko[:, o + 144:o + 400], pb(Z, 0, 2), [zb], [k + "b"], 256)
         mm(grp(pb(Rb, 0), [(K("mI"), B("dv", h)[:]), (K("mI"), z), (pt, K("n16"))], 128), ["mI", "dv" + s, zk, "pt" + s, "n16"], [rk])
         act(B("rr", h)[:], pb(Rb, 0), Fn.Relu, [rk], ["rr" + s], 128, bias=2560.0)
         mm(grp(pb(Rb, 1), [(K("mI"), z), (K("mN"), B("rr", h)[:])], 128), ["mI", "mN", zk, "rr" + s], [rk])
-        act(B("yzb", h)[:] if last else T.pko[:, o + 8:o + 136], pb(Rb, 1), Fn.Abs, [rk], [k + "z"], 128)
-        mm(grp(E[:, 0, 0:16], [(wr_("z1", r), T.pko[:, o + 136 + r:o + 392:16]) for r in range(16)], 16), ["z1", k + "b"], [ek])
-        copy(ENG["lst"], B("yvb", h)[:] if last else T.pko[:, o:o + 8], E[:, 0, 0:8], [ek], [k + "l"], 8, 1.0 / 16)
-        act(B("sl", h)[:], E[:, 0, 8:16], Fn.Abs, [ek], ["sl" + s], 8, bias=-176.5 / 16, scale=1.0 / 256)
+        act(B("yzb", h)[:] if last else T.pko[:, o + 16:o + 144], pb(Rb, 1), Fn.Abs, [rk], [k + "z"], 128)
+        mm(grp(E[:, 0:16], [(K("n16"), K("cl16"))] + [(wr_("z1", r), T.pko[:, o + 144 + r:o + 400:16]) for r in range(16)], 16),
+           ["z1", "n16", "cl16a", "cl16b", k + "b"], [ek])
+        act(T.pko[:, o:o + 16], E[:, 0:16], Fn.Abs, [ek], [k + "l"], 16, scale=1.0 / 16)
+        if last:
+            copy("a", B("yvb", h)[:], E[:, 0:8], [ek], [k + "v"], 8, 1.0 / 16)
         if not last:
             rid, pid = topo.addr(first, core)
             i = 2 * t + h
             sends[(t, h)] = add("p", lambda: [g.remote_dma(T.pki[:, PK * i:PK * i + PK], T.pko[:, o:o + PK], T.sem["ar%d" % i], T.sem.sent,
                                                            pid, rid, smask)], [k + "b", k + "z", k + "l"], [], 300.0, ext=("", 0))
-            act(B("hl", h)[:], B("pt", h)[:, 0:128:16], Fn.Relu, ["pt" + s], ["hl" + s], 8, bias=-192.0)
-        mm(grp(pb(Z, 2), [(K("mI"), T.pko[:, o + 136:o + 264]), (K("a2k"), mk)], 128), ["mI", "a2k", k + "b", "mk" + s], [zb])
+            act(B("hl", h)[:], B("pt", h)[:, 0:128:16], Fn.Relu, ["pt" + s], ["hl" + s], 8, bias=-193.0)
+        mm(grp(pb(Z, 2), [(K("mI"), T.pko[:, o + 144:o + 272]), (K("a2k"), mk)], 128), ["mI", "a2k", k + "b", "mk" + s], [zb])
         act(B("uu", h)[:], pb(Z, 2), Fn.Relu, [zb], ["uu" + s], 128, bias=-2048.0)
         mm(sum([grp(pb(Z, j), [(both("x1")[j], B("c16", h)[:]), (both("xn")[j], B("q", h)[:]), (both("x1")[j], B("uu", h)[:])], 128)
                 for j in (0, 1)], []), ["x1", "xn", "c16" + s, "q" + s, "uu" + s], [zb])
         copy(ENG["nv"], B("nv", h)[:], pb(Z, 0, 2), [zb], ["nv" + s], 256)
-        dedupe(t, h, "on", True)
-
-    def put_x(h):
-        for j in (0, 1):
-            vec(tt(B("xt", h)[:].indirect(B("ox", h)[:, 8 * j:8 * j + 8]), blk(B("nx", h), j), K("c132"), Op.add),
-                ["ox%d" % h, "nx%d" % h, "c132"], ["xt%d" % h], 128 * S, 20)
-
-    def put_nb(h):
-        for j in (0, 1):
-            vec(cp(B("nbf", h)[:].indirect(B("on", h)[:, 8 * j:8 * j + 8]), blk(B("nv", h), j)),
-                ["on%d" % h, "nv%d" % h], ["nbf%d" % h], 128 * S, 20)
+        dedupe(t, h, T.pko[:, o + 8:o + 16], k + "l")
 
     def tally():
-        P = T.E1[:, 1, 0:8]
+        P = T.E1[:, 64:72]
         mm(grp(P, [(K("o16"), B("hl", h)[:]) for h in (0, 1)], 8), ["o16", "hl0", "hl1"], ["E1"])
         act(T.hs[:], P, Fn.Identity, ["E1"], ["hc", "junk"], 8, 20.0, bias=256.0, scale=16.0, accum_out=T.hc[:])
         vec(ts(K("rq"), K("o16", 0, 8), T.hc[:], 0.47, Op.mult, Op.add), ["o16", "hc"], ["rq"], 8)
@@ -453,19 +489,13 @@ def build(g, core, T, topo, rank):
                 for a in range(0, W, 352):
                     copy(ENG["nbf"], B("nbf", h)[:, a:a + 352], B("nbi", h)[:, a:a + 352], ["nbi%d" % h], ["nbf%d_%d" % (h, a)], 352)
                 add("x", None, ["nbf%d_%d" % (h, a) for a in range(0, W, 352)], ["nbf%d" % h], 0.0)
-            if not last:
-                dedupe(t, h, "ox", False)
-            fold(t, h)
-            if not last:
-                put_x(h)
-            choose(t, h)
-            put_nb(h)
+            choose(t, h, fold(t, h))
             if last:
                 rows, k = slice(64 * h, 64 * h + 64), "po%d%d" % (t, h)
                 for j in (0, 1):
                     part = slice(64 * j, 64 * j + 64)
                     outs.append(dma("s", T.yz[rows, 128 * j:128 * j + 128], B("yzb", h)[part, :], "outd", 0, [k + "z"], [], 2500.0))
-                    outs.append(dma("s", T.yv[rows, 8 * j:8 * j + 8], B("yvb", h)[part, :], "outd", 0, [k + "l"], [], 2500.0))
+                    outs.append(dma("s", T.yv[rows, 8 * j:8 * j + 8], B("yvb", h)[part, :], "outd", 0, [k + "v"], [], 2500.0))
                 for j in (0, 1):
                     part = slice(64 * j, 64 * j + 64)
                     outs.append(dma("s", T.ynb[rows, 704 * j:704 * j + 704], B("nbf", h)[part, 704 * j:704 * j + 704], "outd", 0, ["nbf%d" % h], [], 3500.0))
@@ -478,101 +508,119 @@ def build(g, core, T, topo, rank):
     return ops, len(outs), count(smask)
 
 
-def place(ops, seq, pred):
-    start, busy = [0.0] * len(ops), {}
+def timed(seq, case, eng):
+    pred, cost, lat = case
+    at, why, free, last = [0.0] * len(eng), [-1] * len(eng), [0.0] * 6, [-1] * 6
+    end, top = 0.0, 0
     for i in seq:
-        o = ops[i]
-        t = 0.0
+        e = eng[i]
+        t, w = free[e], last[e]
         for j, gap in pred[i]:
-            if start[j] + gap > t:
-                t = start[j] + gap
-        if o["e"] != "x":
-            a, b = busy.setdefault(o["e"], ([], []))
-            k, hi = 0, len(b)
-            while k < hi:
-                m = (k + hi) // 2
-                if b[m] <= t:
-                    k = m + 1
-                else:
-                    hi = m
-            while k < len(a) and a[k] < t + o["cost"]:
-                t = max(t, b[k])
-                k += 1
-            a.insert(k, t)
-            b.insert(k, t + o["cost"])
-        start[i] = t
-    return start
+            x = at[j] + gap
+            if x > t:
+                t, w = x, -2 - j
+        at[i], why[i] = t, w
+        t += cost[i]
+        if e:
+            free[e], last[e] = t, i
+        if t + lat[i] > end:
+            end, top = t + lat[i], i
+    return end, why, top, at
+
+
+def search(cases, eng, kind, turn, phase, steps, heat, reach):
+    n = len(eng)
+    rng = np.random.default_rng(TUNE["seed"])
+    before = [[j for j, gap in p] for p in cases[0][0]]
+    after = [[] for _ in range(n)]
+    for i in range(n):
+        for j in before[i]:
+            after[j].append(i)
+
+    def score(ph):
+        key = [turn[i] + ph[kind[i]] for i in range(n)]
+        for i in range(n):
+            for j in before[i]:
+                if key[j] >= key[i]:
+                    key[i] = key[j] + 1e-9
+        seq = sorted(range(n), key=lambda i: key[i])
+        res = [timed(seq, c, eng) for c in cases]
+        return sum(r[0] for r in res) / len(res), res, key, seq
+
+    now = list(phase)
+    snow, res, key, seq = score(now)
+    best = (snow, key, seq, now)
+    for step in range(steps):
+        end, why, i, at = res[int(rng.integers(len(res)))]
+        pairs = []
+        while i >= 0:
+            w = why[i]
+            if w >= 0 and kind[w] != kind[i]:
+                pairs.append((w, i))
+            i = w if w >= 0 else -2 - w
+        w, u = pairs[int(rng.integers(len(pairs)))]
+        sign, a, b, links = (-1, u, w, before) if rng.random() < 0.5 else (1, w, u, after)
+        ph, todo, goal = list(now), [a], {a: key[b] + sign * (1e-4 + reach * float(rng.random()) ** 3)}
+        while todo:
+            x = todo.pop()
+            ph[kind[x]] = goal[x] - turn[x]
+            for y in links[x]:
+                if sign * (goal.get(y, key[y]) - goal[x]) <= 0:
+                    goal[y] = goal[x] + sign * 1e-6
+                    todo.append(y)
+        if b in goal:
+            continue
+        s, r, k, q = score(ph)
+        if s < snow - heat * 0.03 ** (step / steps) * math.log(1.0 - float(rng.random())):
+            now, snow, res, key, seq = ph, s, r, k, q
+            if s < best[0]:
+                best = (s, key, seq, now)
+    return best
 
 
 def plan(g, core, T, topo, rank):
-    base, others = dict(COST), []
+    known = {}
+    for visits, steps, heat in TUNE["stages"]:
+        cases, eng, key = pattern(g, core, T, topo, rank, visits, steps, heat, known)
+    n = len(eng)
+    return search(cases, eng, list(range(n)), [0] * n, key, TUNE["last"], TUNE["cool"], 0.04)[2]
+
+
+def pattern(g, core, T, topo, rank, R, steps, heat, known):
+    base, cases = dict(COST), []
     for case in CASES:
         COST.update(case)
-        others.append((dict(COST), build(g, core, T, topo, rank)[0]))
+        ops, sem = build(g, core, T, topo, rank, R)[0], COST["sem"]
         COST.update(base)
-    return schedule(build(g, core, T, topo, rank)[0], others)
-
-
-def schedule(ops, others=()):
-    n = len(ops)
-    fw, bw = [[] for _ in ops], [[] for _ in ops]
-    for i, o in enumerate(ops):
-        for j, hard in o["deps"].items():
-            extra = 0.0 if hard is None else ops[j]["lat"] + (COST["sem"] if hard and ops[j]["e"] != "x" else 0.0)
-            fw[i].append((j, ops[j]["cost"] + extra + 1e-3))
-            bw[j].append((i, o["cost"] + extra + 1e-3))
-    rng = np.random.default_rng(TUNE["seed"])
-
-    def span(st):
-        return max(st[i] + ops[i]["cost"] + ops[i]["lat"] for i in range(n))
-
-    def pack(key, pred):
-        k = list(key)
-        for i in (range(n) if pred is fw else range(n - 1, -1, -1)):
-            for j, gap in pred[i]:
-                k[i] = max(k[i], k[j] + 1e-3)
-        return place(ops, sorted(range(n), key=lambda i: k[i]), pred)
-
-    head = [0.0] * n
+        n, above, pred = len(ops), [], []
+        for o in ops:
+            far = 0
+            for j in o["deps"]:
+                far |= above[j]
+            pred.append([(j, ops[j]["cost"] + (0.0 if hard is None else ops[j]["lat"] + (sem if hard and ops[j]["e"] != "x" else 0.0)))
+                         for j, hard in o["deps"].items() if ops[j]["lat"] or not far >> j & 1])
+            above.append(far | sum(1 << j for j in o["deps"]))
+        cases.append((pred, [o["cost"] for o in ops], [o["lat"] for o in ops]))
+    eng = ["xvatps".index(o["e"]) for o in ops]
+    names = {}
+    kind = [names.setdefault(o["kind"] + (o["u"] < 0,), len(names)) for o in ops]
+    turn = [max(o["u"], 0) for o in ops]
+    free = timed(range(n), cases[0], [0] * n)[3]
+    late = [free[i] if turn[i] or ops[i]["u"] == 0 else 1e9 for i in range(n)]
     for i in range(n - 1, -1, -1):
-        head[i] = max([head[j] + gap for j, gap in bw[i]] + [ops[i]["lat"]])
-    best = now = pack([TUNE["lag"] * (ops[i]["u"] % 2) - head[i] - ops[i]["cost"] for i in range(n)], fw)
-    cases = []
-    for cost, alt in others:
-        cases.append(([[(j, alt[j]["cost"] + (0.0 if hard is None else alt[j]["lat"] + (cost["sem"] if hard and alt[j]["e"] != "x" else 0.0)))
-                        for j, hard in o["deps"].items()] for o in alt], [o["cost"] for o in alt], [o["lat"] for o in alt]))
-    eng = [o["e"] for o in ops]
-
-    def judge(st):
-        order, tot = sorted(range(n), key=lambda i: (st[i], i)), span(st)
-        for pred, cost, lat in cases:
-            at, free, end = [0.0] * n, {}, 0.0
-            for i in order:
-                t = free.get(eng[i], 0.0)
-                for j, gap in pred[i]:
-                    if at[j] + gap > t:
-                        t = at[j] + gap
-                at[i] = t
-                if eng[i] != "x":
-                    free[eng[i]] = t + cost[i]
-                end = max(end, t + cost[i] + lat[i])
-            tot += end
-        return tot / (1 + len(cases))
-
-    sbest = snow = judge(best)
-    for r in range(TUNE["rounds"]):
-        amp = TUNE["shake"] * float(rng.random())
-        lo = float(rng.random()) * now[-1]
-        st = pack([x + amp * float(y) * (lo < x < lo + TUNE["reach"]) for x, y in zip(now, rng.random(n))], fw)
-        if r % TUNE["back"] == 0:
-            back = pack([-(st[i] + ops[i]["cost"] + ops[i]["lat"]) for i in range(n)], bw)
-            st = pack([-(back[i] + ops[i]["cost"]) for i in range(n)], fw)
-        s = judge(st)
-        if s < snow + TUNE["heat"] * (1 - r / TUNE["rounds"]) * float(rng.random()):
-            now, snow = st, s
-        if s < sbest:
-            best, sbest = st, s
-    return sorted(range(n), key=lambda i: (best[i], i)), best, [best[i] + ops[i]["cost"] + ops[i]["lat"] for i in range(n)]
+        for j, gap in cases[0][0][i]:
+            if ops[j]["u"] < 0:
+                late[j] = min(late[j], late[i] - gap)
+    free = [late[i] + (free[i] - late[i]) * (ops[i]["u"] >= 0) for i in range(n)]
+    head = {u: min(free[i] for i in range(n) if ops[i]["u"] == u and ops[i]["e"] == "v") for u in range(2 * R)}
+    phase = [known.get(name) for name in names]
+    for u in [2, 3] + list(range(2 * R - 1, -2, -1)):
+        for i in range(n):
+            if ops[i]["u"] == u and phase[kind[i]] is None:
+                phase[kind[i]] = (free[i] - head[max(u, 0)]) / TUNE["half"]
+    best = search(cases, eng, kind, turn, phase, steps, heat, 0.08)
+    known.update(zip(names, best[3]))
+    return cases, eng, best[1]
 
 
 def rank_program(g, core, T, topo):
@@ -590,7 +638,7 @@ def rank_program(g, core, T, topo):
         return
     ops, nout, nsend = build(g, core, T, topo, rank)
     if "o" not in ORDER:
-        ORDER["o"] = plan(g, core, T, topo, rank)[0]
+        ORDER["o"] = plan(g, core, T, topo, rank)
     queue = {"v": g.vector, "a": g.scalar, "t": g.tensor, "p": g, "s": g.sync}
     sem = {"v": "sv", "a": "sa", "t": "st", "p": "sp"}
     total, mark, seen = {}, {}, {}

import math
import numpy as np
from concourse.mybir import AluOpType as Op, ActivationFunctionType as Fn

W, R = 1408, 5
WS = W + 128
PK, SLOT = 272, 400
NQ = 34
BIG, EPS, ETA = 2.0 ** 19, 2.0 ** -17, 24.26
AQ = {}
XV = {}
ENG = {"vu": "v", "v32": "p", "c16": "a", "tl": "a", "cl": "v", "vb": "a", "off": "v", "pt": "a", "nv": "a", "nbf": "p", "bc": "v", "k": "a"}

MATS = (("mI", 128), ("mN", 128), ("n16", 128), ("n2k", 128), ("hI", 128), ("sq", 128), ("cl16", 16), ("mV", 128), ("alt", 128), ("alT", 128), ("a2k", 128), ("c132", 128),
        ("z1", 144), ("zp", 144), ("te", 144), ("to", 144), ("x1", 256), ("xh", 256), ("xn", 256), ("o16", 128), ("oB", 128),
        ("tmpa", 128), ("tmpb", 128), ("sgn", 128), ("tri", 128), ("nn", 160), ("gn", 128), ("n2", 256), ("s1", 8), ("s15", 8),
        ("sm", 8), ("sa", 8), ("sp", 16), ("ip2", 16), ("rq", 8), ("prs", 40), ("c96", 40), ("am", 8))
MOFF = {}
_o = 0
for _n, _c in MATS:
    MOFF[_n] = (_o, _c)
    _o += _c

SCRATCH = {
    "km": ("sbuf", [128, _o], "bfloat16"),
    "pko": ("sbuf", [128, 10 * SLOT], "float16"), "pki": ("sbuf", [128, 8 * PK], "float16"),
    "iw": ("sbuf", [128, W], "int32"), "i32": ("sbuf", [128, 128], "float32"),
    "ip": ("sbuf", [128, 2], "int32"), "ci": ("sbuf", [128, 8], "int32"), "cf": ("sbuf", [128, 8], "float32"),
    "cs": ("sbuf", [128, 8], "float32"), "i8": ("sbuf", [128, 16], "float32"),
    "px": ("sbuf", [128, NQ], "int32"), "p1": ("sbuf", [128, NQ], "int32"), "p2": ("sbuf", [128, NQ], "int32"),
    "p3": ("sbuf", [128, NQ], "float32"), "hc": ("sbuf", [128, 1], "float32"), "hs": ("sbuf", [128, 8], "float32"),
    "zt": ("sbuf", [128, 16, 144], "bfloat16"), "zx": ("sbuf", [128, 16, 144], "bfloat16"),
    "gq": ("sbuf", [128, 8 * NQ], "bfloat16"), "db": ("sbuf", [128, 8 * NQ], "bfloat16"),
    "pr": ("sbuf", [128, 8 * NQ], "bfloat16"), "keep": ("sbuf", [128, 8 * NQ], "bfloat16"),
    "bo": ("sbuf", [128, 8], "uint16"), "bf": ("sbuf", [128, 8], "float32"),
    "m88": ("sbuf", [128, 88], "float32"), "m89": ("sbuf", [128, 88], "float32"), "d0": ("sbuf", [128, 176], "bfloat16"),
    "c88": ("sbuf", [128, 176], "float16"),
}
for _h in (0, 1):
    for _n, _c, _d in (("nbi", [W], "int32"), ("nbf", [WS], "float32"), ("xt", [WS], "bfloat16"), ("pvb", [8], "int32"),
                       ("pzb", [128], "bfloat16"), ("thb", [4], "int32"), ("yvb", [8], "float32"), ("yzb", [128], "bfloat16"),
                       ("vb0", [128], "float16"), ("v16", [8], "float16"), ("thf", [4], "float32"), ("v32", [8], "float32"),
                       ("vu", [8], "uint16"), ("dv", [128], "bfloat16"), ("adv", [128], "bfloat16"), ("fs", [128], "bfloat16"),
                       ("mk", [512], "bfloat16"), ("c16", [128], "float16"), ("tr", [128], "float16"), ("tl", [128], "uint16"),
                       ("q", [128], "float16"), ("cl", [264], "uint16"), ("gm", [2048], "float16"), ("xg", [4224], "bfloat16"),
                       ("ab", [4224], "bfloat16"), ("hit", [8 * NQ], "bfloat16"), ("bst", [8 * NQ], "float32"),
                       ("pt", [128], "bfloat16"), ("bc", [128], "float32"), ("rr", [128], "bfloat16"), ("wl", [8], "float32"),
                       ("hl", [8], "bfloat16"), ("uu", [128], "float16"), ("nv", [256], "float32"), ("nx", [256], "bfloat16"),
                       ("ew", [8, 11, 16], "bfloat16"), ("ds", [176], "float16"), ("off", [32], "uint16"),
                       ("thr", [8 * NQ], "bfloat16")):
        SCRATCH["%s%d" % (_n, _h)] = ("sbuf", [128] + _c, _d)
BANKS = ("Z0", "Z1", "R0", "R1", "M0", "M1", "E0", "E1")
for _n in BANKS:
    SCRATCH[_n] = ("psum", [128, 512], "float32")

OWN = [_n[:-1] for _n in SCRATCH if _n[:-1] + "1" in SCRATCH and _n[-1] == "0"] + ["abl", "po", "pk"]
SEMAPHORES = (["sv", "sa", "st", "sp", "sent", "outd", "zcp"] + ["ar%d" % i for i in range(8)]
              + ["l%s%d" % (x, s) for x in ("nb", "xd", "pv", "pz", "th") for s in (0, 1)])

COST = {"f": 0.97, "g": 1.56, "s": 3.8, "pe": 0.49, "fv": 15.0, "fa": 55.0, "fp": 4.0, "sem": 55.0, "hop": 4500.0, "dma": 0.8}
TUNE = {"stages": ((3, 42000, 1200.0), (R, 4000, 300.0)), "last": 4000, "cool": 100.0, "seed": 2, "half": 8000.0, "split": 0}
CASES = ({}, {"f": 0.9, "g": 1.3, "s": 4.5, "hop": 6000.0, "pe": 0.47, "sem": 80.0, "fv": 25.0})
ORDER = {}


def helper_of(T, topo, r):
    src, dst = T.cores[r], T.cores[(r + 1) % len(T.cores)]
    if topo.may_write(src, dst):
        return None
    c = [x for x in topo.cores_of(src) if x != src and T.rank_of(x) is None and topo.may_write(x, dst)]
    near = [x for x in c if topo.die(x) == topo.die(src)]
    return (near or c)[0]


def count(mask):
    return bin(mask).count("1")


def build(g, core, T, topo, rank, R=R):
    n = len(T.cores)
    hp = helper_of(T, topo, rank)
    first = hp if hp is not None else T.cores[(rank + 1) % n]
    smask = topo.mask(core, first)
    prev = (rank - 1) % n
    php = helper_of(T, topo, prev)
    acount = count(topo.mask(php if php is not None else T.cores[prev], core))
    V, A, PE = g.vector, g.scalar, g.tensor
    ops, state, cur, seen = [], {}, [-1], {}
    F, G, S = COST["f"], COST["g"], COST["s"]

    def add(e, fn, rd, wr, cost, ext=None, lat=0.0):
        i = len(ops)
        deps = {}
        for k in rd:
            s = state.setdefault(k, [None, []])
            if s[0] is not None:
                deps[s[0]] = True
            if k in BANKS:
                for j in s[1]:
                    if ops[j]["e"] != e:
                        deps[j] = True
        for k in wr:
            s = state.setdefault(k, [None, []])
            for j in ([s[0]] if s[0] is not None else []) + s[1]:
                deps[j] = deps.get(j, False) or ops[j]["e"] != e or e != "t"
        for k in rd:
            state[k][1].append(i)
        for k in wr:
            state[k] = [i, []]
        name = (wr + rd)[0].replace("po%d" % (cur[0] // 2), "po").replace("pki%d" % (cur[0] // 2), "pk")
        cut = max([len(b) for b in OWN if name.startswith(b + str(cur[0] % 2))] + [0]) if cur[0] >= 0 else 0
        name = e + (name[:cut] + name[cut + 1:] if cut else name)
        seen[(cur[0], name)] = seen.get((cur[0], name), 0) + 1
        ops.append({"e": e, "fn": fn, "deps": deps, "cost": cost, "ext": ext, "lat": lat, "n": (wr + rd)[0][:5], "u": cur[0],
                    "kind": (name, seen[(cur[0], name)])})
        return i

    def vec(fn, rd, wr, cyc, fix=0.0):
        return add("v", lambda: [fn()], rd, wr, COST["fv"] + fix + max(cyc, 64) * F)

    def act(out, in_, func, rd, wr, cyc, fix=0.0, **kw):
        return add("a", lambda: [A.activation(out, in_, func, **kw)], rd, wr, COST["fa"] + fix + cyc * F)

    def mm(lst, rd, wr):
        cost = sum(COST["fp"] + max(64, m[5]) * COST["pe"] for m in lst)
        return add("t", lambda: [PE.matmul(m[0], m[1], m[2], m[3], m[4]) for m in lst], rd, wr, cost)

    def acc(lst, rd, bank, members):
        left = members[0]

        def fn():
            left[0] -= 1
            return [PE.matmul(m[0], m[1], m[2], False, left[0] == 0 and m is lst[-1]) for m in lst]
        left[0] += 1
        i = add("t", fn, rd, [], sum(COST["fp"] + max(64, m[3]) * COST["pe"] for m in lst))
        ops[i]["deps"][state[bank][0]] = False
        ops[i]["n"] = bank
        members.append(i)

    def grp(out, pairs, nn_, start=True, stop=True):
        return [(out, a, b, start and i == 0, stop and i == len(pairs) - 1, nn_) for i, (a, b) in enumerate(pairs)]

    def pool(fn, rd, wr, cyc):
        return add("p", lambda: [fn()], rd, wr, 170 + 2 * cyc * F)

    def ts(out, in0, s1, s2, o0, o1=None):
        if o1 is None:
            return lambda: V.tensor_scalar(out, in0, s1, None, o0)
        return lambda: V.tensor_scalar(out, in0, s1, s2, o0, o1)

    def tt(out, a, b, o):
        return lambda: V.tensor_tensor(out, a, b, o)

    def cp(out, a):
        return lambda: V.tensor_copy(out, a)

    def fill(out, val, key, cyc, rd=()):
        return vec(lambda: V.memset(out, val), list(rd), [key], cyc)

    def sel(out, in_, pat, op, other, base, cm, rd, wr, cyc):
        return pool(lambda: g.affine_select(out, in_, pat, op, other, base, cm), rd, wr, cyc)

    def copy(e, out, in_, rd, wr, cols, scale=1.0, bias=0.0, fix=0.0):
        if e == "p":
            return sel(out, in_, [[0, cols]], Op.is_ge, 0.0, 0, 0, rd, wr, cols)
        if e == "a":
            if bias:
                return act(out, in_, Fn.Identity, rd, wr, cols, bias=bias, scale=scale)
            return act(out, in_, Fn.Copy, rd, wr, cols, scale=scale)
        if scale == 1.0 and not bias:
            return vec(cp(out, in_), rd, wr, cols, fix)
        return vec(ts(out, in_, scale, bias, Op.mult, Op.add), rd, wr, cols, fix)

    def dma(q, out, in_, sem, val, rd, wr, lat):
        eng = g.sync if q == "s" else A
        return add(q, lambda: [eng.dma_start(out, in_).then_inc(T.sem[sem], 16)], rd + ["q" + q], wr + ["q" + q], 60.0, ext=(sem, val), lat=lat * COST["dma"])

    def K(name, a=0, b=None, step=1):
        o, c = MOFF[name]
        return T.km[:, o + a:o + (c if b is None else b):step]

    def wr_(z, r):
        return K(z, 15 - r, 143 - r)

    def B(name, s):
        return T["%s%d" % (name, s)]

    def blk(b, j):
        return b[:, 128 * j:128 * j + 128]

    def pb(bank, j, m=1):
        return bank[:, 128 * j:128 * (j + m)]

    def both(name):
        return [K(name, 0, 128), K(name, 128, 256)]

    for s in (0, 1):
        rows = slice(64 * s, 64 * s + 64)
        for name, buf, wd, lat in (("pv", "pvb", 8, 2500.0), ("xd", "xt", W, 3200.0), ("pz", "pzb", 128, 3000.0), ("nb", "nbi", W, 4500.0), ("th", "thb", 2, 4000.0)):
            for h in (0, 1):
                own = name in ("pv", "pz")
                i = dma("sa"[h], B(buf, s)[64 * h:64 * h + 64, 0:wd], T[name][rows, wd * h * own:wd * h * own + wd],
                        "l%s%d" % (name, s), 32, [], ["%s%d%d" % (buf, s, h)], lat + 3000.0 * s)
                for j in ops[i]["deps"]:
                    ops[i]["deps"][j] = None
            add("x", None, ["%s%d0" % (buf, s), "%s%d1" % (buf, s)], ["%s%d" % (buf, s)], 0.0, ext=("l%s%d" % (name, s), 32))

    def iota(out, pat, base, cm, key, cyc, small=True):
        if small:
            pool(lambda: g.iota(out, pat, base, cm, allow_small_or_imprecise_dtypes=True), [], [key], cyc)
        else:
            pool(lambda: g.iota(out, pat, base, cm), [], [key], cyc)

    iota(T.ip[:], [[16, 2]], 0, 1, "ip", 2, False)
    iota(K("nn"), [[1, 160]], -16, 0, "nn", 160)
    iota(K("gn"), [[16, 8], [0, 16]], 0, 0, "gn", 128)
    iota(T.i8[:], [[0, 2], [16, 8]], W, 1, "i8", 16)
    iota(K("n2"), [[-64, 2], [0, 2], [1, 64]], 64, 0, "n2", 256)
    iota(K("sgn"), [[0, 64], [-2, 2]], 1, 0, "sgn", 128)
    iota(K("ip2"), [[16, 8], [1, 2]], 0, 0, "ip2", 16)
    iota(T.gq[:], [[16, 8], [0, NQ]], 0, 0, "gq", 8 * NQ)
    iota(T.px[:], [[256, 2], [1, 17]], 128 + 32768, -257, "px", NQ, False)
    iota(T.m88[:], [[1, 8], [1, 11]], -7, 0, "m88", 88)
    iota(T.iw[:], [[1, W]], 0, 0, "iw", W, False)
    for j, m in enumerate((127, 112, 113, 15)):
        vec(ts(T.ci[:, j:j + 1], T.ip[:, 0:1], m, None, Op.bitwise_and), ["ip"], ["ci%d" % j], 1)
    vec(ts(T.ci[:, 4:6], T.ip[:], 4, 1, Op.logical_shift_right, Op.bitwise_and), ["ip"], ["ci4"], 1)
    vec(cp(T.cf[:, 0:6], T.ci[:, 0:6]), ["ci%d" % j for j in range(5)], ["cf"], 1)
    pf, g16, gpar, kf, odd, even = [T.cf[:, j:j + 1] for j in range(6)]
    k14, fb0, fbias, par, psign = [T.cs[:, j:j + 1] for j in range(5)]
    act(k14, kf, Fn.Sigmoid, ["cf"], ["k14"], 1, 1300.0, bias=256.0 * 14.5, scale=-256.0)
    vec(ts(fb0, kf, 14.0, 2.0, Op.is_equal, Op.mult), ["cf"], ["fb0"], 1)
    vec(ts(par, fb0, k14, 8192.0, Op.add, Op.mult), ["fb0", "k14"], ["fb1"], 1)
    vec(ts(fbias, par, -8192.0 - 384.0, None, Op.add), ["fb1"], ["fbias"], 1)
    n0 = K("nn", 16, 144)
    vec(ts(K("mI"), n0, pf, None, Op.is_equal), ["nn", "cf"], ["mI"], 64)
    for name, wgt in (("mN", -1.0), ("n16", -16.0), ("n2k", -2048.0), ("hI", BIG / 2)):
        copy(ENG["k"], K(name), K("mI"), ["mI"], [name], 128 if ENG["k"] == "a" else 64, wgt)
    copy("a", T.i32[:], K("mI"), ["mI"], ["i32"], 128)
    vec(ts(K("tmpa"), K("gn"), g16, -4.0, Op.is_equal, Op.mult), ["gn", "cf"], ["tmpa"], 64)
    sel(K("mV"), K("tmpa"), [[1, 128]], Op.is_ge, 1.0, -2, -1, ["tmpa"], ["mV"], 128)
    sel(K("mV"), K("mV"), [[1, 128]], Op.is_ge, 0.0, 0, -1, ["mV"], ["mV"], 128)
    vec(ts(psign, gpar, g16, -2.0, Op.subtract, Op.mult), ["cf"], ["ps0"], 1)
    vec(ts(psign, psign, 1.0, None, Op.add), ["ps0"], ["psign"], 1)
    vec(ts(K("tmpb"), K("gn"), g16, psign, Op.is_equal, Op.mult), ["gn", "cf", "psign"], ["tmpb"], 64)
    vec(tt(K("tmpb"), K("tmpb"), K("sgn"), Op.mult), ["tmpb", "sgn"], ["tmpb"], 256)
    sel(K("alt"), K("tmpb"), [[1, 128]], Op.is_ge, 0.0, 0, -1, ["tmpb"], ["alt"], 128)
    vec(lambda: V.transpose(K("alT"), K("alt")), ["alt"], ["alT"], 64)
    vec(ts(K("a2k"), K("alt"), 2048.0, None, Op.mult), ["alt"], ["a2k"], 64)
    vec(ts(K("te"), K("nn", 0, 144), pf, even, Op.is_equal, Op.mult), ["nn", "cf"], ["te"], 72)
    vec(ts(K("to"), K("nn", 16, 160), pf, odd, Op.is_equal, Op.mult), ["nn", "cf"], ["to"], 72)
    vec(ts(K("zp", 0, 142), K("nn", 2, 144), gpar, None, Op.is_equal), ["nn", "cf"], ["zp"], 72)
    vec(ts(K("z1", 0, 143), K("nn", 1, 144), g16, None, Op.is_equal), ["nn", "cf"], ["z1"], 72)
    vec(ts(K("x1"), K("n2"), pf, None, Op.is_equal), ["n2", "cf"], ["x1"], 128)
    copy("a", K("xn"), K("x1"), ["x1"], ["xn"], 256, -1.0)
    copy("a", K("xh"), K("x1"), ["x1"], ["xh"], 256, 0.5)
    for name, wgt in (("s1", 1.0), ("sm", -2 * BIG), ("sa", -BIG)):
        vec(ts(K(name), K("nn", 16, 144, 16), g16, wgt, Op.is_equal, Op.mult), ["nn", "cf"], [name], 8)
    vec(ts(K("s15"), K("nn", 31, 159, 16), pf, None, Op.is_equal), ["nn", "cf"], ["s15"], 8)
    vec(ts(K("sp"), K("ip2"), gpar, None, Op.is_equal), ["ip2", "cf"], ["sp"], 16)
    vec(ts(T.db[:], T.gq[:], g16, BIG, Op.is_equal, Op.mult), ["gq", "cf"], ["db"], 4 * NQ)
    fill(K("cl16", 0, 8), 0.0, "cl16a", 8)
    fill(K("cl16", 8, 16), 177.0, "cl16b", 8)
    fill(K("c132"), -132.0, "c132", 64)
    fill(K("o16"), 1.0 / 16, "o16", 64)
    fill(K("oB"), BIG / 128, "oB", 64)
    fill(K("c96"), 32.0 / 256, "c96", 8)
    fill(T.keep[:], 1.0, "keep", 4 * NQ)
    fill(T.keep[:, 0:8 * NQ:NQ], 0.0, "keep", 8)
    iota(T.bf[:], [[NQ, 8]], NQ - 1, 0, "bf", 8)
    vec(cp(T.bo[:], T.bf[:]), ["bf"], ["bo"], 8)
    vec(ts(T.p1[:], T.px[:], 15, None, Op.bitwise_and), ["px"], ["p1"], 32)
    vec(ts(T.p2[:], T.px[:], 4, 16, Op.logical_shift_right, Op.bitwise_and), ["px"], ["p2"], 32)
    vec(tt(T.p3[:], T.p1[:], T.p2[:], Op.add), ["p1", "p2"], ["p3"], 64)
    vec(ts(K("prs", 0, NQ), T.p3[:], -1.0 / 256, None, Op.mult), ["p3"], ["prs"], 32)
    fill(K("prs", 16, 17), 2.0 / 256, "prs", 1)
    fill(K("prs", 33, 34), -32.0 / 256, "prs", 1)
    mm(sum([grp(T.R0[:, NQ * j:NQ * j + NQ], [(K("alT"), K("prs", 0, NQ)), (K("mI"), K("c96", 0, NQ))], NQ) for j in range(8)], []),
       ["alT", "prs", "mI", "c96"], ["R0"])
    vec(tt(T.pr[:], T.R0[:, 0:8 * NQ], T.db[:], Op.mult), ["R0", "db"], ["pr"], 8 * NQ)
    fill(T.zt[:, 0:4, :], 0.0, "z0", 2 * 144)
    for a in range(4, 32, 4):
        i = dma("s", (T.zt if a < 16 else T.zx)[:, a % 16:a % 16 + 4, :], T.zt[:, 0:4, :], "zcp", 112, ["z0"], ["z%d" % a], 2500.0)
        for j in ops[i]["deps"]:
            if ops[j]["e"] == "s":
                ops[i]["deps"][j] = None
    add("x", None, ["z%d" % a for a in range(4, 32, 4)], ["zt", "zx"], 0.0, ext=("zcp", 112))
    sel(K("tri"), K("o16"), [[1, 16], [16, 8]], Op.is_gt, EPS / 16, 0, -1, ["o16"], ["tri"], 128)
    sel(K("tri"), K("tri"), [[0, 16], [-16, 8]], Op.is_ge, 0.0, 0, 1, ["tri"], ["tri"], 128)
    sel(K("tri"), K("tri"), [[0, 16], [16, 8]], Op.is_ge, 0.0, 15, -1, ["tri"], ["tri"], 128)
    vec(ts(T.zt[:, :, 15:143:16], K("tri"), 16.0, None, Op.mult), ["tri", "zt"], ["zt"], 64)
    act(K("sq"), K("tri"), Fn.Square, ["tri"], ["sq"], 128, scale=16.0)
    act(T.zx[:, :, 15:143:16], K("sq"), Fn.Square, ["sq", "zx"], ["zx"], 128)
    vec(ts(T.m89[:], T.m88[:], EPS - 1.0, 0.0, Op.add, Op.max), ["m88"], ["m89"], 88)
    vec(ts(T.d0[:, 88:176], T.m89[:], 1.0, None, Op.min), ["m89"], ["d0"], 88)
    act(T.m89[:], T.d0[:, 88:176], Fn.Square, ["d0"], ["m89"], 88)
    act(T.d0[:, 0:88], T.m89[:], Fn.Square, ["m89"], ["d0"], 88)
    vec(ts(T.d0[:, 9:88:11], K("o16", 0, 8), 2.0 ** 59, -2.0 ** 59, Op.mult, Op.mult), ["d0", "o16"], ["d0"], 8)
    fill(T.d0[:, 97:176:11], -2.0 ** 28, "d0", 8)
    fill(T.d0[:, 10:176:11], -1.0, "d0", 8)
    vec(ts(T.c88[:], T.keep[:, 0:176], 0.0, None, Op.mult), ["keep"], ["c88"], 88)
    vec(ts(T.c88[:, 8:176:11], T.i8[:], 0.0, -16.5, Op.mult, Op.add), ["i8", "c88"], ["c88"], 8)
    vec(ts(T.c88[:, 9:176:11], T.i8[:], g16, -1.0, Op.subtract, Op.mult), ["i8", "cf", "c88"], ["c88"], 8)
    for s in (0, 1):
        thf, thr = B("thf", s), B("thr", s)
        vec(cp(thf[:, 0:2], B("thb", s)[:, 0:2]), ["thb%d" % s], ["thf%d" % s], 1)
        vec(ts(thr[:], T.db[:], thf[:, 1:2], None, Op.mult), ["db", "thf%d" % s], ["thr%d" % s], 4 * NQ)
        vec(ts(thr[:, 16:8 * NQ:NQ], T.db[:, 0:8 * NQ:NQ], thf[:, 0:1], None, Op.mult), ["db", "thf%d" % s], ["thr%d" % s], 8)
        vec(cp(thr[:, 33:8 * NQ:NQ], T.db[:, 0:8 * NQ:NQ]), ["db"], ["thr%d" % s], 8)
        fill(B("ew", s)[:, :, 8:11, :], 0.0, "ewz%d" % s, 192)

    sends = {}

    def src(t, h):
        if t == 0:
            return B("v16", h)[:], B("pzb", h)[:], B("vb0", h)[:], "v16%d" % h, "pzb%d" % h, "vb0%d" % h
        o = PK * (2 * (t - 1) + h)
        k = "pki%d%d" % (t, h)
        return T.pki[:, o:o + 8], T.pki[:, o + 16:o + 144], T.pki[:, o + 144:o + 272], k, k, k

    def dedupe(t, h, kinds, kk):
        s = str(h)
        vl, z, vb, lk, zk, vk = src(t, h)
        P, bank, ew, ds, a = T["M" + s], "M" + s, B("ew", h), B("ds", h), 88 * (t == R - 1)
        act(B("wl", h)[:], kinds, Fn.Sigmoid, [kk], ["wl" + s], 8, bias=17 * (17 + ETA) - ETA, scale=-17 - ETA)
        mm([(P[:, a:176], K("mI"), T.c88[:, a:176], True, False, 176 - a)]
           + [(P[:, b + 10:b + 88:11], K("mI"), vl, False, False, 8) for b in range(a, 176, 88)]
           + [(P[:, 96:176:11], K("mI"), kinds, False, False, 8)], ["mI", "c88", lk, kk], [bank])
        for c in range(8):
            vec(ts(ew[:, :, 7 - c, :], vb, B("v32", h)[:, c:c + 1], B("wl", h)[:, c:c + 1], Op.is_equal, Op.mult),
                [vk, "v32" + s, "wl" + s], ["ew%d%d" % (h, c)], 64)
        for b in range(a, 176, 88):
            zz = T.zt if b else T.zx
            mm(grp(P[:, b:b + 88], [(zz[:, r, 15 - r:143 - r], ew[:, :, :, r]) for r in range(16)], 88, False, b == 88),
               ["zt", "zx", "ewz" + s] + ["ew%d%d" % (h, c) for c in range(8)], [bank])
        vec(lambda: V.tensor_tensor_scan(ds[:, a:176], T.d0[:, a:176], P[:, a:176], 0.0, Op.mult, Op.max), [bank, "d0"], ["ds" + s], 176 - a)
        m = 16 - a // 11
        mm(sum([grp(P[:, 192 + m * j:192 + m * j + m], [(x, ds[:, a + 10:176:11])], m) for j, x in enumerate(both("x1"))], []), ["x1", "ds" + s], [bank])
        copy(ENG["off"], B("off", h)[:, 0:2 * m], P[:, 192:192 + 2 * m], [bank], ["off" + s], 2 * m)
        for j in (0, 1) * (not a):
            vec(tt(B("xt", h)[:].indirect(B("off", h)[:, 16 * j:16 * j + 8]), blk(B("nx", h), j), K("c132"), Op.add),
                ["off" + s, "nx" + s, "c132"], ["xt" + s], 128 * S, 35)
        for j in (0, 1):
            vec(cp(B("nbf", h)[:].indirect(B("off", h)[:, m * j + m - 8:m * j + m]), blk(B("nv", h), j)), ["off" + s, "nv" + s], ["nbf" + s], 128 * S, 35)

    def level(t, h):
        s, vu = str(h), B("vu", h)[:]
        vl, z, vb, lk, zk, vk = src(t, h)
        E, ek = T["E" + s], "E" + s
        if t > 0:
            add("x", None, [], [lk], 0.0, ext=("ar%d" % (2 * (t - 1) + h), acount), lat=COST["hop"])
            ops[-1]["deps"][sends[(t - 1, h)]] = False
            copy(ENG["vu"], vu, vl, [lk], ["vu" + s], 8)
            copy(ENG["v32"], B("v32", h)[:], vl, [lk], ["v32" + s], 8)
        else:
            vec(cp(vu, B("pvb", h)[:]), ["pvb" + s], ["vu" + s], 8)
            copy("p", B("v32", h)[:], B("pvb", h)[:], ["pvb" + s], ["v32" + s], 8)
            copy("p", vl, B("pvb", h)[:], ["pvb" + s], [lk], 8)
            copy("a", vb, T.iw[:].indirect(vu), ["iw", "vu" + s], [vk], 128 * G)
        vec(tt(B("dv", h)[:], B("xt", h)[:, 0:W].indirect(vu), z, Op.subtract), ["xt" + s, "vu" + s, zk], ["dv" + s], 128 * G, 35)
        act(B("adv", h)[:], B("dv", h)[:], Fn.Abs, ["dv" + s], ["adv" + s], 128)
        win, wk = (B("nbi", h)[:], "nbi" + s) if t == 0 else (B("nbf", h)[:, 0:W], "nbf" + s)
        copy(ENG["c16"], B("c16", h)[:], win.indirect(vu), [wk, "vu" + s], ["c16" + s], 128 * G, fix=35.0)
        act(B("fs", h)[:], B("adv", h)[:], Fn.Sigmoid, ["adv" + s, "fbias"], ["fs" + s], 128, bias=fbias, scale=256.0)
        mm(sum([grp(pb(E, j), [(K("mV"), B("fs", h)[:])], 128) for j in range(4)], []), ["mV", "fs" + s], [ek])
        act(B("mk", h)[:], E[:], Fn.Sigmoid, [ek], ["mk" + s], 512, bias=-128.0, scale=256.0)
        mm([(T["Z" + s][:, r:512:4], K("mI"), z, True, True, 128) for r in range(4)], ["mI", zk], ["Z" + s])

    def contacts(t, h):
        s = str(h)
        E, M, ek, mk_ = T["E" + s], T["M" + s], "E" + s, "M" + s
        vl, z, vb, lk, zk, vk = src(t, h)
        xwin, mk, c16, cl, gm, xg = B("xt", h)[:, 0:W], B("mk", h), B("c16", h)[:], B("cl", h), B("gm", h), B("xg", h)
        win, wk = (B("nbi", h)[:], "nbi" + s) if t == 0 else (B("nbf", h)[:, 0:W], "nbf" + s)
        vec(lambda: V.transpose(B("tr", h)[:], c16), ["c16" + s], ["tr" + s], 64)
        lst = []
        for c2 in range(4):
            for hh in (0, 1):
                mats = (K("te", 16, 144), K("te", 0, 128)) if hh == 0 else (K("to", 16, 144), K("to", 0, 128))
                lst += grp(M[:, 2 * c2 + hh:128:8], [(mats[gl], B("tr", h)[:, 32 * c2 + 16 * gl:32 * c2 + 16 * gl + 16]) for gl in (0, 1)], 16)
        mm(lst, ["te", "to", "tr" + s], [mk_])
        copy(ENG["tl"], B("tl", h)[:], blk(M, 0), [mk_], ["tl" + s], 128)
        mm(grp(pb(E, 0), [(K("alt"), mk[:, 0:128])], 128), ["alt", "mk" + s], [ek])
        vec(tt(B("q", h)[:], pb(E, 0), c16, Op.mult), [ek, "c16" + s], ["q" + s], 128)
        for j in range(4):
            e = 8 * (j == 3)
            vec(tt(gm[:, 512 * j:512 * j + 512], win.indirect(B("tl", h)[:, 32 * j:32 * j + 32]), mk[:], Op.mult),
                [wk, "tl" + s, "mk" + s], ["gm%d%d" % (h, j)], 512 * G, 35)
            if e:
                mm(grp(M[:, 384:392], [(wr_("z1", r), B("q", h)[:, r:128:16]) for r in range(16)], 8), ["z1", "q" + s], [mk_])
            mm(grp(M[:, 128 + 64 * j:192 + 64 * j], [(K("zp", 14 - 8 * ip - 2 * a, 142 - 8 * ip - 2 * a), gm[:, 512 * j + 128 * a + ip:512 * j + 128 * a + 128:2])
                                                     for a in range(4) for ip in (0, 1)], 64), ["zp", "gm%d%d" % (h, j)], [mk_])
            copy(ENG["cl"], cl[:, 64 * j:64 * j + 64 + e], M[:, 128 + 64 * j:192 + 64 * j + e], [mk_], ["cl%d%d" % (h, j)], 64 + e)
            cuts = [0, 32, 64 + e] if TUNE["split"] else [0, 64 + e]
            for a, b in zip(cuts, cuts[1:]):
                copy("v" if j in XV.get((t, h), ()) else "a", xg[:, 1024 * j + 16 * a:1024 * j + 16 * b], xwin.indirect(cl[:, 64 * j + a:64 * j + b]),
                     ["xt" + s, "cl%d%d" % (h, j)], ["xg%d%d0" % (h, j)] * (a == 0) + ["xg%d%d1" % (h, j)] * (b > 32), 16 * (b - a) * G, fix=35.0)
        if t < R - 1:
            mm(sum([grp(pb(E, j), [(both("xh")[j], B("dv", h)[:]), (both("x1")[j], z)], 128) for j in (0, 1)], []), ["x1", "xh", "dv" + s, zk], [ek])
            act(B("nx", h)[:], pb(E, 0, 2), Fn.Identity, [ek], ["nx" + s], 256, bias=131.75)
        lst = [(M[:, 0:8 * NQ], mk[:, 0:128], T.pr[:], True, False, 8 * NQ)]
        lst += [(M[:, k:8 * NQ:17], blk(gm, k), K("sp"), False, False, 16) for k in range(16)]
        lst += [(M[:, 16:8 * NQ:NQ], B("q", h)[:], K("s1"), False, False, 8), (M[:, 33:8 * NQ:NQ], c16, K("s15"), False, False, 8)]
        mm(lst, ["mk" + s, "pr", "sp", "s1", "s15", "q" + s, "c16" + s] + ["gm%d%d" % (h, j) for j in range(4)], [mk_])

    def fold(t, h):
        s = str(h)
        vl, z, vb, lk, zk, vk = src(t, h)
        Rb, rk, Z, E, xg, ab = T["R" + s], "R" + s, T["Z" + s], T["E" + s], B("xg", h), B("ab", h)
        aq = AQ.get((t, h), (1,))
        lst = [(Rb[:, 0:8 * NQ], K("o16"), B("thr", h)[:], True, False, 8 * NQ), (Rb[:, 0:8 * NQ], z, T.db[:], False, False, 8 * NQ)]
        lst += [(Rb[:, 17 * (u % 2) + 4 * (u // 2) + a:8 * NQ:NQ], z, K("sa"), False, False, 8) for u in aq for a in range(4)]
        mm(lst, ["o16", "thr" + s, "db", "sa", zk], [rk])
        xs, mem = T.db[:, 0:8 * NQ:NQ], [[0]]
        for u in range(8):
            j, par_ = u // 2, u % 2
            xk, key, quad, res = ["xg%d%d0" % (h, j), "xg%d%d1" % (h, j)], "ab%d%d" % (h, u), xg[:, 1024 * j + par_:1024 * j + 1024:2], ab[:, 512 * u:512 * u + 512]
            sets = [(Rb[:, 17 * par_ + 4 * j + a:8 * NQ:NQ], xg[:, 1024 * j + 2 * a + par_:1024 * j + 1024:8], ab[:, 512 * u + a:512 * u + 512:4]) for a in range(4)]
            if u in aq:
                mm([(E[:], K("mI"), quad, True, False, 512)]
                   + [(E[:, r:512:4], K("mN"), z, False, r == 3, 128) for r in range(4)], ["mI", "mN", zk] + xk, ["E" + s])
                act(res, E[:], Fn.Abs, ["E" + s], [key], 512)
                acc([(o, m, K("sa"), 8) for o, x, m in sets], ["sa", key], rk, mem)
            else:
                vec(tt(res, quad, Z[:], Op.max), xk + ["Z" + s], [key], 512)
                acc([(o, x, xs, 8) for o, x, m in sets], ["db"] + xk, rk, mem)
                acc([(o, m, K("sm"), 8) for o, x, m in sets], ["sm", key], rk, mem)
        vec(tt(ab[:, 4096:4224], xg[:, 4096:4224], Z[:, 0:512:4], Op.max), ["xg%d31" % h, "Z" + s], ["abl" + s], 128)
        if t > 0:
            acc([(Rb[:, 16:8 * NQ:NQ], K("oB"), K("am"), 8)], ["oB", "am"], rk, mem)
        acc([(Rb[:, 16:8 * NQ:NQ], xg[:, 4096:4224], xs, 8), (Rb[:, 16:8 * NQ:NQ], ab[:, 4096:4224], K("sm"), 8)], ["db", "sm", "xg%d31" % h, "abl" + s], rk, mem)
        return mem[1:]

    def choose(t, h, sums):
        s = str(h)
        vl, z, vb, lk, zk, vk = src(t, h)
        Rb, Z, E, rk, zb, ek = T["R" + s], T["Z" + s], T["E" + s], "R" + s, "Z" + s, "E" + s
        M, bst, pt, mk = T["M" + s], B("bst", h), B("pt", h)[:], B("mk", h)[:, 0:128]
        last = t == R - 1
        i = act(B("hit", h)[:], Rb[:, 0:8 * NQ], Fn.Sign, [rk], ["hit" + s], 8 * NQ, bias=-0.5, scale=1.0 / BIG)
        ops[i]["deps"].update({j: True for j in sums})
        mm([(M[:, 0:8 * NQ], K("hI"), B("hit", h)[:], False, True, 8 * NQ)], ["hI", "hit" + s], ["M" + s])
        vec(lambda: V.tensor_tensor_scan(bst[:], T.keep[:], M[:, 0:8 * NQ], 0.0, Op.mult, Op.max), ["M" + s, "keep"], ["bst" + s], 8 * NQ)
        best = bst[:].indirect(T.bo[:])
        copy(ENG["pt"], pt, best, ["bst" + s, "bo"], ["pt" + s], 128 * G, 1.0 / 2048, -0.35, 20.0)
        copy(ENG["bc"], B("bc", h)[:], best, ["bst" + s, "bo"], ["bc" + s], 128 * G, fix=20.0)
        mm([(pb(Z, 0), B("bc", h)[:], T.i32[:], True, False, 512)], ["bc" + s, "i32"], [zb])
        mm([(pb(Z, 0), pt, K("n2k"), False, True, 128), (pb(Z, 1), pt, K("mI"), True, True, 128)], ["pt" + s, "n2k", "mI"], [zb])
        o = SLOT * (2 * t + h)
        k = "po%d%d" % (t, h)
        copy(ENG["vb"], T.pko[:, o + 144:o + 400], pb(Z, 0, 2), [zb], [k + "b"], 256)
        mm(grp(pb(Rb, 0), [(K("mI"), B("dv", h)[:]), (K("mI"), z), (pt, K("n16"))], 128), ["mI", "dv" + s, zk, "pt" + s, "n16"], [rk])
        act(B("rr", h)[:], pb(Rb, 0), Fn.Relu, [rk], ["rr" + s], 128, bias=2560.0)
        mm(grp(pb(Rb, 1), [(K("mI"), z), (K("mN"), B("rr", h)[:])], 128), ["mI", "mN", zk, "rr" + s], [rk])
        act(B("yzb", h)[:] if last else T.pko[:, o + 16:o + 144], pb(Rb, 1), Fn.Abs, [rk], [k + "z"], 128)
        mm(grp(E[:, 0:16], [(K("n16"), K("cl16"))] + [(wr_("z1", r), T.pko[:, o + 144 + r:o + 400:16]) for r in range(16)], 16),
           ["z1", "n16", "cl16a", "cl16b", k + "b"], [ek])
        act(T.pko[:, o:o + 16], E[:, 0:16], Fn.Abs, [ek], [k + "l"], 16, scale=1.0 / 16)
        if last:
            copy("a", B("yvb", h)[:], E[:, 0:8], [ek], [k + "v"], 8, 1.0 / 16)
        if not last:
            rid, pid = topo.addr(first, core)
            i = 2 * t + h
            sends[(t, h)] = add("p", lambda: [g.remote_dma(T.pki[:, PK * i:PK * i + PK], T.pko[:, o:o + PK], T.sem["ar%d" % i], T.sem.sent,
                                                           pid, rid, smask)], [k + "b", k + "z", k + "l"], [], 300.0, ext=("", 0))
            act(B("hl", h)[:], B("pt", h)[:, 0:128:16], Fn.Relu, ["pt" + s], ["hl" + s], 8, bias=-193.0)
        mm(grp(pb(Z, 2), [(K("mI"), T.pko[:, o + 144:o + 272]), (K("a2k"), mk)], 128), ["mI", "a2k", k + "b", "mk" + s], [zb])
        act(B("uu", h)[:], pb(Z, 2), Fn.Relu, [zb], ["uu" + s], 128, bias=-2048.0)
        mm(sum([grp(pb(Z, j), [(both("x1")[j], B("c16", h)[:]), (both("xn")[j], B("q", h)[:]), (both("x1")[j], B("uu", h)[:])], 128)
                for j in (0, 1)], []), ["x1", "xn", "c16" + s, "q" + s, "uu" + s], [zb])
        copy(ENG["nv"], B("nv", h)[:], pb(Z, 0, 2), [zb], ["nv" + s], 256)
        dedupe(t, h, T.pko[:, o + 8:o + 16], k + "l")

    def tally():
        P = T.E1[:, 64:72]
        mm(grp(P, [(K("o16"), B("hl", h)[:]) for h in (0, 1)], 8), ["o16", "hl0", "hl1"], ["E1"])
        act(T.hs[:], P, Fn.Identity, ["E1"], ["hc", "junk"], 8, 20.0, bias=256.0, scale=16.0, accum_out=T.hc[:])
        vec(ts(K("rq"), K("o16", 0, 8), T.hc[:], 0.47, Op.mult, Op.add), ["o16", "hc"], ["rq"], 8)
        vec(ts(K("am"), K("rq"), 16.0, T.hc[:], Op.mult, Op.subtract), ["rq", "hc"], ["am"], 8)

    outs = []
    for t in range(R):
        last = t == R - 1
        for h in (0, 1):
            cur[0] = 2 * t + h
            level(t, h)
            contacts(t, h)
            if t == 0:
                for a in range(0, W, 352):
                    copy(ENG["nbf"], B("nbf", h)[:, a:a + 352], B("nbi", h)[:, a:a + 352], ["nbi%d" % h], ["nbf%d_%d" % (h, a)], 352)
                add("x", None, ["nbf%d_%d" % (h, a) for a in range(0, W, 352)], ["nbf%d" % h], 0.0)
            choose(t, h, fold(t, h))
            if last:
                rows, k = slice(64 * h, 64 * h + 64), "po%d%d" % (t, h)
                for j in (0, 1):
                    part = slice(64 * j, 64 * j + 64)
                    outs.append(dma("s", T.yz[rows, 128 * j:128 * j + 128], B("yzb", h)[part, :], "outd", 0, [k + "z"], [], 2500.0))
                    outs.append(dma("s", T.yv[rows, 8 * j:8 * j + 8], B("yvb", h)[part, :], "outd", 0, [k + "v"], [], 2500.0))
                for j in (0, 1):
                    part = slice(64 * j, 64 * j + 64)
                    outs.append(dma("s", T.ynb[rows, 704 * j:704 * j + 704], B("nbf", h)[part, 704 * j:704 * j + 704], "outd", 0, ["nbf%d" % h], [], 3500.0))
        if not last:
            tally()
    for i in outs:
        for j in ops[i]["deps"]:
            if ops[j]["e"] == "s":
                ops[i]["deps"][j] = None
    return ops, len(outs), count(smask)


def timed(seq, case, eng):
    pred, cost, lat = case
    at, why, free, last = [0.0] * len(eng), [-1] * len(eng), [0.0] * 6, [-1] * 6
    end, top = 0.0, 0
    for i in seq:
        e = eng[i]
        t, w = free[e], last[e]
        for j, gap in pred[i]:
            x = at[j] + gap
            if x > t:
                t, w = x, -2 - j
        at[i], why[i] = t, w
        t += cost[i]
        if e:
            free[e], last[e] = t, i
        if t + lat[i] > end:
            end, top = t + lat[i], i
    return end, why, top, at


def search(cases, eng, kind, turn, phase, steps, heat, reach):
    n = len(eng)
    rng = np.random.default_rng(TUNE["seed"])
    before = [[j for j, gap in p] for p in cases[0][0]]
    after = [[] for _ in range(n)]
    for i in range(n):
        for j in before[i]:
            after[j].append(i)

    def score(ph):
        key = [turn[i] + ph[kind[i]] for i in range(n)]
        for i in range(n):
            for j in before[i]:
                if key[j] >= key[i]:
                    key[i] = key[j] + 1e-9
        seq = sorted(range(n), key=lambda i: key[i])
        res = [timed(seq, c, eng) for c in cases]
        return sum(r[0] for r in res) / len(res), res, key, seq

    now = list(phase)
    snow, res, key, seq = score(now)
    best = (snow, key, seq, now)
    for step in range(steps):
        end, why, i, at = res[int(rng.integers(len(res)))]
        pairs = []
        while i >= 0:
            w = why[i]
            if w >= 0 and kind[w] != kind[i]:
                pairs.append((w, i))
            i = w if w >= 0 else -2 - w
        w, u = pairs[int(rng.integers(len(pairs)))]
        sign, a, b, links = (-1, u, w, before) if rng.random() < 0.5 else (1, w, u, after)
        ph, todo, goal = list(now), [a], {a: key[b] + sign * (1e-4 + reach * float(rng.random()) ** 3)}
        while todo:
            x = todo.pop()
            ph[kind[x]] = goal[x] - turn[x]
            for y in links[x]:
                if sign * (goal.get(y, key[y]) - goal[x]) <= 0:
                    goal[y] = goal[x] + sign * 1e-6
                    todo.append(y)
        if b in goal:
            continue
        s, r, k, q = score(ph)
        if s < snow - heat * 0.03 ** (step / steps) * math.log(1.0 - float(rng.random())):
            now, snow, res, key, seq = ph, s, r, k, q
            if s < best[0]:
                best = (s, key, seq, now)
    return best


def plan(g, core, T, topo, rank):
    known = {}
    for visits, steps, heat in TUNE["stages"]:
        cases, eng, key = pattern(g, core, T, topo, rank, visits, steps, heat, known)
    n = len(eng)
    return search(cases, eng, list(range(n)), [0] * n, key, TUNE["last"], TUNE["cool"], 0.04)[2]


def pattern(g, core, T, topo, rank, R, steps, heat, known):
    base, cases = dict(COST), []
    for case in CASES:
        COST.update(case)
        ops, sem = build(g, core, T, topo, rank, R)[0], COST["sem"]
        COST.update(base)
        n, above, pred = len(ops), [], []
        for o in ops:
            far = 0
            for j in o["deps"]:
                far |= above[j]
            pred.append([(j, ops[j]["cost"] + (0.0 if hard is None else ops[j]["lat"] + (sem if hard and ops[j]["e"] != "x" else 0.0)))
                         for j, hard in o["deps"].items() if ops[j]["lat"] or not far >> j & 1])
            above.append(far | sum(1 << j for j in o["deps"]))
        cases.append((pred, [o["cost"] for o in ops], [o["lat"] for o in ops]))
    eng = ["xvatps".index(o["e"]) for o in ops]
    names = {}
    kind = [names.setdefault(o["kind"] + (o["u"] < 0,), len(names)) for o in ops]
    turn = [max(o["u"], 0) for o in ops]
    free = timed(range(n), cases[0], [0] * n)[3]
    late = [free[i] if turn[i] or ops[i]["u"] == 0 else 1e9 for i in range(n)]
    for i in range(n - 1, -1, -1):
        for j, gap in cases[0][0][i]:
            if ops[j]["u"] < 0:
                late[j] = min(late[j], late[i] - gap)
    free = [late[i] + (free[i] - late[i]) * (ops[i]["u"] >= 0) for i in range(n)]
    head = {u: min(free[i] for i in range(n) if ops[i]["u"] == u and ops[i]["e"] == "v") for u in range(2 * R)}
    phase = [known.get(name) for name in names]
    for u in [2, 3] + list(range(2 * R - 1, -2, -1)):
        for i in range(n):
            if ops[i]["u"] == u and phase[kind[i]] is None:
                phase[kind[i]] = (free[i] - head[max(u, 0)]) / TUNE["half"]
    best = search(cases, eng, kind, turn, phase, steps, heat, 0.08)
    known.update(zip(names, best[3]))
    return cases, eng, best[1]


def rank_program(g, core, T, topo):
    rank = T.rank_of(core)
    if rank is None:
        for r in range(len(T.cores)):
            if helper_of(T, topo, r) == core:
                dst = T.cores[(r + 1) % len(T.cores)]
                rid, pid = topo.addr(dst, core)
                m, got = topo.mask(core, dst), count(topo.mask(T.cores[r], core))
                for i in range(2 * (R - 1)):
                    g.wait_ge(T.sem["ar%d" % i], got)
                    g.remote_dma(T.pki[:, PK * i:PK * i + PK], T.pki[:, PK * i:PK * i + PK], T.sem["ar%d" % i], T.sem.sent, pid, rid, m)
                g.wait_ge(T.sem.sent, 2 * (R - 1) * count(m))
        return
    ops, nout, nsend = build(g, core, T, topo, rank)
    if "o" not in ORDER:
        ORDER["o"] = plan(g, core, T, topo, rank)
    queue = {"v": g.vector, "a": g.scalar, "t": g.tensor, "p": g, "s": g.sync}
    sem = {"v": "sv", "a": "sa", "t": "st", "p": "sp"}
    total, mark, seen = {}, {}, {}
    for i in ORDER["o"]:
        o = ops[i]
        need = {}
        for j, hard in o["deps"].items():
            if hard:
                for s, val in mark[j].items():
                    need[s] = max(need.get(s, 0), val)
        if o["e"] == "x":
            mark[i] = dict([o["ext"]]) if o["ext"] else need
            continue
        for s, val in need.items():
            if seen.get((o["e"], s), 0) < val:
                queue[o["e"]].wait_ge(T.sem[s], val)
                seen[(o["e"], s)] = val
        ins = o["fn"]()
        if o["ext"] is not None:
            mark[i] = dict([o["ext"]])
        else:
            s = sem[o["e"]]
            for x in ins:
                x.then_inc(T.sem[s], 1)
            total[s] = total.get(s, 0) + len(ins)
            mark[i] = {s: total[s]}
    for s, val in total.items():
        g.wait_ge(T.sem[s], val)
    g.wait_ge(T.sem.sent, 2 * (R - 1) * nsend)
    g.sync.wait_ge(T.sem.outd, 16 * nout)
